import numpy as np, ml_dtypes
CORES = [6,15,38,47]
N = 4
BF = ml_dtypes.bfloat16
def gentries(a):
    return np.ascontiguousarray(a.reshape(8, 16, -1).transpose(0, 2, 1)).reshape(8, -1)
def gtable(e):
    e = np.asarray(e); return np.ascontiguousarray(e.reshape(8, -1, 16).transpose(0, 2, 1)).reshape(128, -1).astype(np.int32)
W, M, L, D, S = 4096, 4096, 128, 32, 4
K = L * D
def cols(rng, n):
    base = rng.integers(0, 256, (N, 8, 1, n)); amp = rng.integers(0, 129, (N, 8, 1, n))
    return np.clip(np.rint(base + amp * (2.0 * rng.random((N, 8, 16, n)) - 1.0)), 0, 255).astype(np.int64)
def parts(rng):
    X, Z = cols(rng, W), cols(rng, L)
    P = rng.integers(0, W, (N, 8, M)); V = rng.integers(0, W, (N, 8, K)); pool = rng.integers(0, M, (N, 8, 256))
    O = np.where(rng.random((N, 8, K)) < 0.5, rng.integers(0, M, (N, 8, K)), np.take_along_axis(pool, rng.integers(0, 256, (N, 8, K)), 2))
    c = rng.random((N, 8, K)); T = np.where(c < 0.45, rng.integers(0, S + 2, (N, 8, K)), np.where(c < 0.85, 99, rng.integers(0, 99, (N, 8, K))))
    return X, Z, P, O, V, T, rng.integers(200, 3400, (N, 8, S))
def pack(X, Z, P, O, V, T, th):
    return {"x": np.ascontiguousarray(X).reshape(N, 128, W).astype(np.float32).astype(BF), "z": np.ascontiguousarray(Z).reshape(N, 128, L).astype(np.float32).astype(BF), "px": P.astype(np.int32),
            "ol": np.stack([gtable(a) for a in O]), "nl": np.stack([gtable(a) for a in V]), "tl": np.stack([gtable(a) for a in T]), "th": th.astype(np.int32)}
def setup_inputs(rng):
    return pack(*parts(rng))
def setup_inputs_spread(rng):
    X = (np.exp2(8 * rng.random((N, 8, 1, W))) * rng.random((N, 8, 16, W))).astype(np.int64); Z = (np.exp2(8 * rng.random((N, 8, 1, L))) * rng.random((N, 8, 16, L))).astype(np.int64)
    e = rng.integers(1, 5, (3, N, 8, 1))
    P = (W * rng.random((N, 8, M)) ** e[0]).astype(np.int64); O = (M * rng.random((N, 8, K)) ** e[1]).astype(np.int64); V = (W * rng.random((N, 8, K)) ** e[2]).astype(np.int64)
    T = np.where(rng.random((N, 8, K)) < 0.3, 99, (100 * rng.random((N, 8, K)) ** 4).astype(np.int64)); th = (4081 * rng.random((N, 8, S)) ** 2).astype(np.int64)
    return pack(X, Z, P, O, V, T, th)
def setup_inputs_ends(rng):
    def ends(n):
        m = rng.integers(0, 3, (N, 8, 1, n)); return np.where(m == 2, 255 * rng.integers(0, 2, (N, 8, 16, n)), 255 * np.minimum(m, 1)) + np.zeros((N, 8, 16, n), np.int64)
    X, Z = ends(W), ends(L); X[..., 0] = 0; X[..., W - 1] = 255
    P = (W - 1) * rng.integers(0, 2, (N, 8, M)); O = (M - 1) * rng.integers(0, 2, (N, 8, K)); V = (W - 1) * rng.integers(0, 2, (N, 8, K)); T = 99 * rng.integers(0, 2, (N, 8, K))
    th = 4080 * rng.integers(0, 2, (N, 8, S)); th[:, 0, 0] = 0; th[:, 1, 0] = 4080; th[0, 7, 0] = 0; th[N - 1, 7, 0] = 4080
    star = int(np.argmax(((37 * np.arange(M)) & (W - 1)) == W - 1))
    for pair, v, n, o, ks in (((0, L - 1), 0, 0, star, (0, 1, D - 1)), ((1, L - 2), 255, W - 1, star, (0, 1, D - 1)), ((2, L - 3), 0, W - 1, M - 1, (0, 3, D - 1))):
        for l in pair:
            Z[..., l] = v
            for k in ks: V[..., k * L + l] = n; T[..., k * L + l] = 0; O[..., k * L + l] = o
    return pack(X, Z, P, O, V, T, th)
def setup_inputs_corners(rng):
    X, Z, P, O, V, T, th = parts(rng)
    th = np.where(rng.random((N, 8, S)) < 0.5, 4080 * rng.integers(0, 2, (N, 8, S)), th)
    for a in range(N):
        ct, cp, co, cv, cz = [rng.permutation(8) for i in range(5)]
        for g in range(8):
            T[a, g] = rng.choice(np.array(((0,), (99,), (98,), (S,), (S - 1,), (0, 98), (1, 2, 99), (0, 1, 2, S - 1, S, S + 1, 98, 99))[ct[g]]), K)
            if cp[g] < 5: P[a, g] = (np.arange(M) & (W - 1), np.zeros(M, np.int64), np.full(M, W - 1), W - 1 - (np.arange(M) & (W - 1)), rng.choice(np.array([0, W - 1]), M))[cp[g]]
            if co[g] < 4: O[a, g] = (np.zeros(K, np.int64), np.full(K, M - 1), rng.choice(np.array([0, M - 1]), K), np.arange(K))[co[g]]
            if cv[g] < 4: V[a, g] = (np.zeros(K, np.int64), np.full(K, W - 1), rng.choice(np.array([0, W - 1]), K), np.arange(K) & (W - 1))[cv[g]]
            if cz[g] < 2: Z[a, g] = 255 * cz[g]
    e = int(rng.integers(0, 8)); X[:, e] = 255; Z[:, e] = 0; Z[:, e, 0, 1::2] = 1; th[:, e, 0] = 4079
    O[:, e, 1::2] = 32 * (M // 32 - 1 - rng.integers(0, 8, (N, K // 2))) + 17
    return pack(X, Z, P, O, V, T, th)
def setup_inputs_crowd(rng):
    X, Z, P, O, V, T, th = parts(rng); pm = rng.permutation(8)
    for g in range(8):
        c = int(pm[g])
        if c < 2: th[:, g] = 4080; T[:, g] = 99
        if c == 2 or c == 3: th[:, g] = 0
        if c == 4 or c == 5: X[:, g, :, 0] = 0; th[:, g] = rng.integers(100, 1500, (N, S))
        for a in range(N):
            one = int(rng.integers(1, L)); p = int(rng.integers(0, M))
            if c == 1: T[a, g, int(rng.integers(0, K))] = 98
            if 2 <= c < 6: O[a, g] = p
            if c == 4 or c == 5:
                V[a, g] = 0; T[a, g] = 0; v = rng.integers(0, 256, 16); v[0] = 255; v[1] = 0
                Z[a, g] = v[np.argsort(rng.random((16, L)), axis=0)]
            if c == 3 or c == 5: O[a, g, one::L] = (p + 1 + int(rng.integers(0, M - 1))) % M
            if c == 5: Z[a, g, :, one] = rng.integers(0, 256, 16)
            if c == 6:
                l = np.arange(K) % L; w = rng.integers(0, M, L); n = int(rng.integers(0, W)); O[a, g] = w[np.minimum(l, L - 1 - l)]; V[a, g] = n; T[a, g] = 0; X[a, g, :, n] = 0
                Z[a, g, 0] = 255; Z[a, g, 15] = 0; v = Z[a, g][:, np.minimum(np.arange(L), L - 1 - np.arange(L))]
                Z[a, g] = np.where(np.arange(L) < L // 2, v, v[::-1])
            if c == 7: O[a, g] = rng.choice(rng.integers(0, M, 4), K)
    return pack(X, Z, P, O, V, T, th)
def setup_inputs_ties(rng):
    X, Z, P, O, V, T, th = parts(rng)
    pat = 64 * rng.integers(0, 4, (N, 8, 16, 8)); X = np.take_along_axis(pat, rng.integers(0, 8, (N, 8, 1, W)), 3)
    Z = np.where(rng.random((N, 8, 1, L)) < 0.5, np.take_along_axis(np.roll(pat, -1, axis=0), rng.integers(0, 8, (N, 8, 1, L)), 3), 64 * rng.integers(0, 4, (N, 8, 16, L)))
    T = np.where(rng.random((N, 8, K)) < 0.7, rng.integers(0, S + 1, (N, 8, K)), 99); th = 64 * rng.integers(0, 40, (N, 8, S)); th[:, ::3, 1] = 0; th[:, 1::3, 0] = 0
    return pack(X, Z, P, O, V, T, th)
def check_inputs(d):
    bad = []
    for k, lo, hi in (("x", 0, 255), ("z", 0, 255), ("px", 0, W - 1), ("ol", 0, M - 1), ("nl", 0, W - 1), ("tl", 0, 99), ("th", 0, 4080)):
        v = np.asarray(d[k]).astype(np.float64)
        if not (np.min(v) >= lo and np.max(v) <= hi): bad.append("range of " + k)
        elif np.any(v != np.floor(v)): bad.append("whole numbers in " + k)
    return bad
def reference(x, z, px, ol, nl, tl, th):
    X = x.astype(np.float32).astype(np.int64).reshape(N, 8, 16, W); Z = z.astype(np.float32).astype(np.int64).reshape(N, 8, 16, L); P = px.astype(np.int64)
    O, V, T = [np.stack([gentries(a) for a in b]).astype(np.int64) for b in (ol, nl, tl)]
    lower = np.tri(L, L, -1, dtype=bool); lane = np.arange(L); A = np.zeros((N, 8, 1), np.int64)
    for s in range(S):
        R = np.where(T <= s, V, np.take_along_axis(P, O, 2))
        y = np.take_along_axis(X, R[:, :, None, :], 3); u = np.add.reduce(np.abs(y - np.tile(Z, (1, 1, 1, D))), axis=2)
        h = (((u * O) >> 5) + u + 37 * O + A) & (W - 1)
        h, O, V, T, Z = [np.roll(a, 1, axis=0) for a in (h, O, V, T, Z)]
        G = np.take_along_axis(X, h[:, :, None, :], 3); d = np.add.reduce(np.abs(G - np.tile(Z, (1, 1, 1, D))), axis=2)
        lim = th[:, :, s:s + 1].astype(np.int64)
        red = (d <= lim) & ~((T > s) & (T < 99))
        V = np.where(red, h, V); T = np.where(red, s + 2, T); A = np.sum(red.astype(np.int64), axis=2, keepdims=True)
        by = d.reshape(N, 8, D, L); j = np.argmax(by, axis=2) * L + lane; b = np.argmin(by, axis=2) * L + lane
        go = np.take_along_axis(d, j, 2) > lim
        np.put_along_axis(T, j, np.where(go, 99, np.take_along_axis(T, j, 2)), 2)
        oj = np.take_along_axis(O, j, 2); hj = np.take_along_axis(h, j, 2); hb = np.take_along_axis(h, b, 2)
        win = go & ~np.any((oj[..., :, None] == oj[..., None, :]) & lower & go[..., None, :], axis=3)
        q, g, l = np.nonzero(win); P[q, g, oj[q, g, l]] = hj[q, g, l]
        Z = (Z + np.take_along_axis(G, b[:, :, None, :], 3)) >> 1
        win = ~np.any((hb[..., :, None] == hb[..., None, :]) & lower, axis=3)
        q, g, l = np.nonzero(win); X[q, g, :, hb[q, g, l]] = Z[q, g, :, l]
    return {"yx": X.reshape(N, 128, W).astype(np.float32).astype(BF), "yp": P.astype(np.float32), "yz": Z.reshape(N, 128, L).astype(np.float32).astype(BF),
            "yn": np.stack([gtable(a) for a in V]).astype(np.float32), "yt": np.stack([gtable(a) for a in T]).astype(np.float32)}

@@ -1,0 +1,621 @@
+from concourse.bass import DstId, RemoteDMATransfer
+from concourse.mybir import AluOpType as A, ActivationFunctionType as F
+
+S = 4
+PO = 32
+XW, PWW = 4112, 4144
+BIG = float(1 << 23)
+ZT, NS, OW = 384, 320, 520
+bf, f32, i32, u16 = "bfloat16", "float32", "int32", "uint16"
+
+
+def _sb(w, d):
+    return ("sbuf", [128, w], d)
+
+
+SCRATCH = {
+    "X": _sb(XW, bf), "PW": _sb(PWW, bf), "y1": _sb(4096, bf), "m1": _sb(4096, bf), "y3": _sb(4096, bf), "m3": _sb(4096, bf), "gp": _sb(4096, bf),
+    "ZTo": _sb(5 * ZT, bf), "NSo": _sb(5 * NS, f32), "ZTi": _sb(4 * ZT, bf), "NSi": _sb(4 * NS, f32),
+    "OO": _sb(4 * OW, f32), "O16": _sb(4 * 256, u16), "Ho": _sb(4 * 256, u16), "Hi": _sb(4 * 256, u16),
+    "pxi": _sb(256, i32), "oli": _sb(256, i32), "nli": _sb(256, i32), "tli": _sb(256, i32), "thi": _sb(4, i32),
+    "phi": _sb(256, bf), "plo": _sb(256, bf),
+    "ip": _sb(8, i32), "ib": _sb(8, i32), "col": _sb(16, f32), "io1": _sb(144, f32), "io2": _sb(128, f32), "io3": _sb(128, f32), "io4": _sb(64, f32),
+    "E2": _sb(144, bf), "Ey": _sb(144, bf), "Ep": _sb(144, bf), "E1f": _sb(144, f32), "A01": _sb(128, bf),
+    "If": _sb(128, f32), "nIf": _sb(128, f32), "Ib": _sb(128, bf), "nI8": _sb(128, bf), "I99": _sb(128, bf), "sI": _sb(512, bf),
+    "BD": _sb(128, f32), "DM": _sb(128, f32), "LM": _sb(128, bf), "colc": _sb(256, bf), "c62": _sb(8, f32),
+    "sg1": _sb(128, f32), "sg2": _sb(128, f32), "d0x": _sb(256, f32), "d0n": _sb(256, f32),
+    "lst": _sb(64, u16), "thf": _sb(4, f32), "thS": _sb(4, f32), "thA": _sb(4, f32), "thB": _sb(4, f32),
+    "hf": _sb(264, f32), "scM": _sb(256, f32), "scN": _sb(256, f32), "Ksb": _sb(256, f32), "thE": _sb(256, f32), "ta": _sb(256, f32), "tb": _sb(256, f32),
+    "pi1": _sb(8, i32), "pi2": _sb(8, i32), "cj": _sb(8, u16), "xi1": _sb(8, i32), "xi2": _sb(8, i32), "cb": _sb(8, u16),
+    "MkO": _sb(128, f32), "Mkh": _sb(128, f32), "Mkhb": _sb(128, bf), "Mkb": _sb(128, f32), "kO": _sb(128, f32), "kb": _sb(128, f32),
+    "eqO": _sb(128, f32), "eqb": _sb(128, f32), "duO": _sb(128, f32), "dub": _sb(128, f32),
+    "pt8": _sb(8, f32), "xt8": _sb(8, f32), "offP": _sb(16, u16), "offX": _sb(16, u16), "val": _sb(128, bf), "hb": _sb(8, u16),
+    "zs": _sb(128, f32), "zi": _sb(128, i32), "sz8": _sb(8, f32),
+    "red": _sb(256, bf), "ref": _sb(256, bf), "tgt": _sb(256, bf), "sel": _sb(256, bf), "Qs": _sb(256, f32), "dN": _sb(256, f32), "Tr": _sb(256, f32),
+    "junk": _sb(256, bf), "acol": _sb(8, f32), "Rf": _sb(256, f32), "R16": _sb(256, u16), "tf": _sb(256, f32), "vi": _sb(256, i32), "hi": _sb(256, i32),
+    "oP": _sb(256, f32), "oN": _sb(256, f32), "oT": _sb(256, f32),
+    "b0": ("psum", [128, 512], f32), "b1": ("psum", [128, 512], f32), "b2": ("psum", [128, 512], f32), "b3": ("psum", [128, 512], f32),
+    "pt": ("psum", [128, 8, 8, 16], f32), "b6": ("psum", [128, 512], f32), "b7": ("psum", [128, 512], f32),
+}
+SEMAPHORES = (["v", "a", "t", "g", "sent"] + ["d%d" % i for i in range(20)] + ["h%d" % i for i in range(16)]
+              + ["z%d" % i for i in range(4)] + ["t%d" % i for i in range(4)] + ["n%d" % i for i in range(4)] + ["o%d" % i for i in range(3)])
+TAG = [""]
+NODES = []
+
+
+def _turns(names):
+    return {x.replace("send_", "send "): 0.5 * i for i, x in enumerate(names.split())}
+
+
+CFG = {
+    "gp0": [("a", 0, 8), ("v", 8, 16), ("a", 16, 24), ("v", 24, 32)],
+    "gp": [("a", 0, 8), ("a", 8, 16), ("a", 16, 24), ("a", 24, 32)],
+    "y10": [("v", 0, 4), ("a", 4, 8), ("a", 8, 16), ("a", 16, 24), ("a", 24, 30), ("a", 30, 32)],
+    "y1": [("a", 0, 3), ("v", 3, 8), ("v", 8, 16), ("a", 16, 24), ("a", 24, 30), ("a", 30, 32)],
+    "m1": [(0, 8), (8, 16), (16, 17), (17, 18), (18, 19), (19, 24), (24, 29), (29, 30), (30, 32)],
+    "y3": [("a", 0, 8), ("a", 8, 16), ("a", 16, 21), ("v", 21, 24), ("a", 24, 29), ("a", 29, 32)],
+    "m3": [(0, 8), (8, 16), (16, 24), (24, 27), (27, 29), (29, 32)],
+    "eng": {"Qs": "a", "Tr": "a", "Nn": "a", "A": "a"},
+    "xs": 1024,
+    "slack": 0.0,
+    "share": 0.2,
+    "turn": _turns("Qs R1 us MkO keyP uy1 zs Mkhb val h1 kc rowP km0 hb T scM po0 q GP0 send_h rowX km1 Mkh keyX h0 Ksb scN lmP GP1 eqP ref R0 sz hn h3 "
+                   "duP lmX zn p um0 red po po3 um2 um3 uy2 scatP cm send_z send_t y1_0 h2 zi uy0 R3 R2 m1_0 offP A y1_1 po2 GP2 uy3 send_n GP3 x "
+                   "tile3 Mkb eqX offX scatX OC duX m1_1 m1_2 um1 y1_2 y1_3 sel m1_3 y3_0 km3 ks Nn ky2 y3_1 Tr po1 m3_0 m3_1 y3_2 ky0 dN y3_3 ky3 "
+                   "m3_2 N km2 send_o tile tgt m3_3 hf ky1 Tn thE"),
+    "turn0": _turns("R1 dma px send_z us fill iota c uy1 in h0 send_t po0 Qs sel tgt kc send_n um2 R3 sz send_o GP0 GP1 R0 h1 send_h po OC h3 R2 GP2 "
+                    "po3 cm h2 GP3 q y1_0 y1_1 uy0 uy2 uy3 um3 po1 m1_0 y1_2 um0 ky2 m1_1 m1_2 m1_3 km0 m3_0 ky3 y1_3 po2 ks tile y3_0 y3_1 um1 "
+                    "y3_2 m3_1 m3_2 tile3 ky0 y3_3 km1 km3 ky1 m3_3 hf km2 c2 thE"),
+    "turn4": _turns("Mkb x offX zs val scatX scN duX Mkhb rowX zn dma duP eqX T eqP dN lmP hb oP keyX MkO zi oN Mkh keyP scM Ksb ref p offP scatP Tn "
+                    "rowP oT N red Nn lmX hn Tr"),
+}
+EST = dict(cyc=1.04, g=1.56, sc=3.8, ind=55.0, pe=0.52, wake=60.0, dlat=2000.0, dbw=250.0, issue=1000.0, rlat=2600.0, rbw=60.0)
+
+
+def run_plan(nodes, P, order=None, cfg=None):
+    n = len(nodes)
+    busy, lat = [0.0] * n, [0.0] * n
+    for i, x in enumerate(nodes):
+        k, c = x["c"]
+        if k == "n":
+            busy[i] = max(64, c) * P["cyc"]
+        elif k == "g":
+            busy[i] = P["ind"] + c * P["g"] * P["cyc"]
+        elif k == "s":
+            busy[i] = P["ind"] + c * P["sc"] * P["cyc"]
+        elif k == "pe":
+            busy[i] = c * P["pe"]
+        elif k == "dma":
+            busy[i], lat[i] = 60.0, P["dlat"] + c / P["dbw"]
+        else:
+            busy[i], lat[i] = P["issue"], P["rlat"] + c / P["rbw"]
+    free, pipe, done, start, bfree = {}, {"dma": 0.0, "send": 0.0}, [None] * n, [0.0] * n, {}
+
+    def est(i):
+        x = nodes[i]
+        t0 = free.get(x["e"], 0.0)
+        for p in x["pre"]:
+            t0 = max(t0, done[p] + (0.0 if x["e"] == "t" and nodes[p]["e"] == "t" else P["wake"]))
+        for b in x["B"]:
+            for e2, t2 in bfree.get(b, {}).items():
+                if e2 != x["e"]:
+                    t0 = max(t0, t2 + P["wake"])
+        return t0
+
+    def place(i, t0):
+        x = nodes[i]
+        start[i] = t0
+        free[x["e"]] = t0 + busy[i]
+        k, c = x["c"]
+        if k in pipe:
+            d = c / P["dbw" if k == "dma" else "rbw"]
+            pipe[k] = max(pipe[k] + d + (150.0 if k == "dma" else 500.0), t0 + busy[i] + lat[i])
+            done[i] = pipe[k]
+        else:
+            done[i] = t0 + busy[i]
+        for b in x["B"]:
+            bfree.setdefault(b, {})[x["e"]] = done[i]
+
+    if order is not None:
+        for i in order:
+            place(i, est(i))
+        return order, max(done), start, done
+    suc = [[] for i in range(n)]
+    prio = [-100.0 * x["ph"] - cfg["turn" if 0 < x["ph"] < S else "turn%d" % x["ph"]].get(x["tag"], cfg["turn"].get(x["tag"], 0.0)) for x in nodes]
+    left, lastw, before = [0] * n, {}, {}
+    for p, i in sorted([(-prio[i], i) for i, x in enumerate(nodes) if x["tag"][:2] in ("GP", "y1", "y3", "m1", "m3")]):
+        if nodes[i]["e"] in lastw:
+            before[i] = lastw[nodes[i]["e"]]
+        lastw[nodes[i]["e"]] = i
+    for i, x in enumerate(nodes):
+        pre = set(x["pre"] + ([before[i]] if i in before else []))
+        left[i] = len(pre)
+        for p in pre:
+            suc[p].append(i)
+    ready, order = [i for i in range(n) if left[i] == 0], []
+    while ready:
+        es = [(est(i), i) for i in ready]
+        t0, i0 = min(es)
+        mine = [(prio[i], -i, t, i) for t, i in es if nodes[i]["e"] == nodes[i0]["e"]]
+        t1, i1 = max([m for m in mine if m[2] <= t0 + cfg["slack"]])[2:]
+        t1, i1 = max([m for m in mine if m[2] <= t1 + cfg["share"] * busy[i1]])[2:]
+        place(i1, t1)
+        order.append(i1)
+        ready.remove(i1)
+        for j in suc[i1]:
+            left[j] -= 1
+            if left[j] == 0:
+                ready.append(j)
+    assert len(order) == n
+    return order, max(done), start, done
+
+
+def rank_program(g, core, T, topo):
+    rank = T.rank_of(core)
+    if rank is None:
+        return
+    nxt = T.cores[(rank + 1) % len(T.cores)]
+    prv = T.cores[(rank - 1) % len(T.cores)]
+    assert topo.may_write(core, nxt)
+    rid, pid = topo.addr(nxt)[0], topo.addr(nxt)[1]
+    mask = topo.mask(core, nxt)
+    n_in = len(topo.engines(prv, core))
+    n_out = len(topo.engines(core, nxt))
+    v, a, t = g.vector, g.scalar, g.tensor
+    Q = {"v": v, "a": a, "t": t, "g": g, "s": g.sync}
+    cnt = {"v": 0, "a": 0, "t": 0, "g": 0, "d": 0, "sent": 0, "ph": 0}
+    clock = {e: {} for e in Q}
+    wr, rd, bank = {}, {}, {}
+    nodes, lw, lr, lb = [], {}, {}, {}
+
+    def node(e, tag, c, fn, R, W, B):
+        i = len(nodes)
+        pre = set(lw[r] for r in R if r in lw)
+        for w in W:
+            pre |= set(lr.get(w, []))
+            if w in lw:
+                pre.add(lw[w])
+        if e == "t":
+            for b in B:
+                if b in lb:
+                    pre.add(lb[b])
+                lb[b] = i
+        for r in R:
+            lr.setdefault(r, []).append(i)
+        for w in W:
+            lw[w] = i
+            lr[w] = []
+        nodes.append(dict(e=e, tag=tag, ph=cnt["ph"], c=c, fn=fn, R=list(R), W=list(W), B=list(B), pre=sorted(pre)))
+
+    def op(e, tag, fn, R=(), W=(), B=(), c=64, k="n"):
+        node(e, tag, (k, c), fn, R, W, B)
+
+    def dma(e, out, in_, nb, R=(), W=()):
+        node(e, "dma", ("dma", nb), lambda: Q[e].dma_start(out, in_), R, W, ())
+
+    def send(out, in_, sem, nb, R, lands):
+        wr[lands] = (sem, sem, n_in, {})
+        node("g", "send " + sem[:1], ("send", nb), lambda: g.remote_dma(out, in_, T.sem[sem], T.sem.sent, pid, rid, mask), R, [lands], ())
+
+    def send2(pairs, sem, nb, R, lands):
+        es = topo.engines(core, nxt)
+        half = [es[:len(es) // 2], es[len(es) // 2:]]
+        for x in lands:
+            wr[x] = (sem, sem, n_in, {})
+        trs = [RemoteDMATransfer(dst_ids=[DstId(rid=rid, pnc=pid)], dma_engine_mask=sum(1 << e for e in h), remote_sem=T.sem[sem], src=p[1], dst=p[0])
+               for p, h in zip(pairs, half)]
+        node("g", "send " + sem[:1], ("send", nb), lambda: g.remote_dma_fused(trs, local_sem=T.sem.sent), R, lands, ())
+
+    def need(e, ev):
+        sem, val, ck = ev[1], ev[2], ev[3]
+        if clock[e].get(sem, 0) >= val:
+            return
+        Q[e].wait_ge(T.sem[sem], val)
+        clock[e][sem] = val
+        for k in ck:
+            if clock[e].get(k, 0) < ck[k]:
+                clock[e][k] = ck[k]
+
+    def waits(e, me, R, W, B):
+        evs = [wr[r] for r in R if r in wr]
+        for w in W:
+            evs += rd.get(w, []) + ([wr[w]] if w in wr else [])
+        for b in B:
+            evs += [x for k, x in bank.get(b, {}).items() if k != me]
+        evs.sort(key=lambda x: -x[2])
+        for ev in evs:
+            if not (me == "t" and ev[0] == "t"):
+                need(e, ev)
+
+    def note(ev, R, W, B):
+        for r in R:
+            rd.setdefault(r, []).append(ev)
+        for w in W:
+            wr[w] = ev
+            rd[w] = []
+        for b in B:
+            bank.setdefault(b, {})[ev[0]] = ev
+
+    def emit(x):
+        e, k = x["e"], x["c"][0]
+        TAG[0] = x["tag"]
+        if k == "send":
+            waits("g", "rem", x["R"], (), ())
+            x["fn"]()
+            cnt["sent"] += n_out
+        elif k == "dma":
+            sem = "d%d" % cnt["d"]
+            cnt["d"] += 1
+            waits(e, sem, x["R"], x["W"], ())
+            x["fn"]().then_inc(T.sem[sem], 16)
+            note((sem, sem, 16, dict(clock[e])), x["R"], x["W"], ())
+        else:
+            waits(e, e, x["R"], x["W"], x["B"])
+            cnt[e] += 1
+            x["fn"]().then_inc(T.sem[e], 1)
+            note((e, e, cnt[e], dict(clock[e])), x["R"], x["W"], x["B"])
+
+    def copy(tag, out, in_, R, W, B=(), c=64, k="n", e="v"):
+        if e == "v":
+            op("v", tag, lambda: v.tensor_copy(out, in_), R, W, B, c, k)
+        else:
+            op("a", tag, lambda: a.activation(out, in_, F.Copy), R, W, B, c, k)
+
+    def ts(tag, out, in0, s1, s2, o0, o1, R, W, B=(), c=64, k="n"):
+        if o1 is None:
+            op("v", tag, lambda: v.tensor_scalar(out, in0, s1, None, o0), R, W, B, c, k)
+        else:
+            op("v", tag, lambda: v.tensor_scalar(out, in0, s1, s2, o0, o1), R, W, B, c, k)
+
+    def tt(tag, out, in0, in1, o, R, W, B=(), c=64, k="n"):
+        op("v", tag, lambda: v.tensor_tensor(out, in0, in1, o), R, W, B, c, k)
+
+    def scan(tag, out, d0, d1, init, o0, o1, R, W, B=(), c=128):
+        op("v", tag, lambda: v.tensor_tensor_scan(out, d0, d1, init, o0, o1), R, W, B, c)
+
+    def act(tag, out, in_, f, R, W, B=(), c=256, **kw):
+        op("a", tag, lambda: a.activation(out, in_, f, **kw), R, W, B, c)
+
+    def fill(out, val, W, c=64):
+        op("v", "fill", lambda: v.memset(out, val), (), W, (), c)
+
+    def iota(out, pat, base, W, c, cm=0, **kw):
+        op("g", "iota", lambda: g.iota(out, pat, base, cm, **kw), (), W, (), 156 + 2 * c)
+
+    def mm(tag, out, res, bk, l, r, R, start, stop, c):
+        op("t", tag, lambda: t.matmul(out, l, r, start, stop), R, [res], [bk], c, "pe")
+
+    def mm16(tag, out, res, bk, E, rhs, R, start, stop, c=1024):
+        def fn():
+            for r in range(16):
+                last = t.matmul(out, E[:, 15 - r:143 - r], rhs(r), start and r == 0, stop and r == 15)
+            return last
+        op("t", tag, fn, R, [res], [bk], c, "pe")
+
+    def blocks(name, b0, b1):
+        return [(name, b) for b in range(b0, b1)]
+
+    def col(i):
+        return T.col[:, i:i + 1]
+
+    Xw, Pw, K = T.X[:, 0:XW], T.PW[:, 0:PWW], T.b0[:, 0:256]
+    C_P, C_R, C_G, C_LT2, C_DX, C_DP, C_PI, C_E, C_R7 = range(9)
+    L_IN, L_OUT, L_B32, L_B8 = T.lst[:, 0:16], T.lst[:, 16:32], T.lst[:, 32:48], T.lst[:, 56:60]
+    XR, PR = ["Xa", "Xb", "Xc"], ["PW", "PWa", "PWb"]
+    HF = [("hf", k) for k in range(4)] + ["hf1"]
+    CM0 = -37888.0 - 80.0 * 131072
+
+    def OF(k, w=264):
+        return T.OO[:, k * OW:k * OW + w]
+
+    def OC(k, a0=0, a1=256):
+        return T.OO[:, k * OW + 264 + a0:k * OW + 264 + a1]
+
+    def Nof(buf, k):
+        return buf[:, k * NS:k * NS + 256]
+
+    def Tof(buf, k):
+        return buf[:, k * ZT + 128:k * ZT + 384]
+
+    def OOR(k):
+        return [("OO", k)]
+
+    def O16R(k):
+        return [("O16p", j) for j in range(4)] if k == 0 else [("O16", k)]
+
+    dma("s", T.pxi[:], T.px[:], 131072, W=["pxi"])
+    dma("a", T.oli[:], T.ol[:], 131072, W=["oli"])
+    dma("s", T.tli[:], T.tl[:], 131072, W=["tli"])
+    dma("a", T.nli[:], T.nl[:], 131072, W=["nli"])
+    dma("s", T.ZTo[:, 0:128], T.z[:], 32768, W=[("z", 0)])
+    xs = CFG["xs"]
+    dma("s", T.X[:, 0:xs], T.x[:, 0:xs], 256 * xs, W=["Xa"])
+    fl = dict(allow_small_or_imprecise_dtypes=True)
+    iota(T.ip[:], [[0, 8]], 0, ["ip"], 8, 1)
+    iota(T.io4[:, 0:16], [[1, 8], [-128, 2]], 248, ["io4a"], 16, **fl)
+    iota(T.io1[:], [[1, 144]], -15, ["io1"], 144, **fl)
+    iota(T.io4[:, 56:60], [[2, 4]], 0, ["io4e"], 4, **fl)
+    iota(T.io2[:], [[16, 8], [0, 16]], 0, ["io2"], 128, **fl)
+    iota(T.io3[:], [[0, 8], [1, 16]], 0, ["io3"], 128, **fl)
+    iota(T.colc[:], [[1, 256]], 0, ["colc"], 256, **fl)
+    iota(T.io4[:, 16:32], [[-2, 16]], 31, ["io4b"], 16, **fl)
+    iota(T.io4[:, 32:48], [[32, 8], [0, 2]], 31, ["io4c"], 16, **fl)
+    iota(T.c62[:], [[64, 8]], 62, ["c62"], 8, **fl)
+
+    fill(T.PW[:], 0.0, ["PW"], 2072)
+    fill(T.thi[:], 0, ["thi"])
+    dma("a", T.thi[0:128:16, :], T.th[:], 128, W=["thi"])
+    copy("px", T.phi[:], T.pxi[:], ["pxi"], ["phi"], c=256)
+    tt("px", T.plo[:], T.pxi[:], T.phi[:], A.subtract, ["pxi", "phi"], ["plo"], c=512)
+    dma("s", T.PW[0:128:16, PO:PO + 4096], T.phi[:], 65536, ["phi", "PW"], ["PWa"])
+    dma("a", T.PW[1:128:16, PO:PO + 4096], T.plo[:], 65536, ["plo", "PW"], ["PWb"])
+    dma("s", T.X[:, xs:4096], T.x[:, xs:4096], 256 * (4096 - xs), ["plo"], ["Xb"])
+    p0 = T.ip[:, 0:1]
+    ts("c", T.ib[:, 0:1], p0, 15, None, A.bitwise_and, None, ["ip"], ["ib0"])
+    ts("c", T.ib[:, 1:2], p0, 7, None, A.bitwise_and, None, ["ip"], ["ib1"])
+    ts("c", T.ib[:, 2:3], p0, 3, 1, A.arith_shift_right, A.bitwise_and, ["ip"], ["ib2"])
+    copy("c", col(C_P), p0, ["ip"], ["cP"])
+    copy("c", col(C_R), T.ib[:, 0:1], ["ib0"], ["cR"])
+    copy("c", col(C_E), T.ib[:, 2:3], ["ib2"], ["cE"])
+    ts("c", col(C_PI), T.ib[:, 0:1], -8.0, None, A.mult, None, ["ib0"], ["cPI"])
+    ts("c", L_IN, T.io4[:, 0:16], col(C_PI), None, A.add, None, ["io4a", "cPI"], ["L_IN"])
+    tt("c", col(C_G), p0, T.ib[:, 0:1], A.subtract, ["ip", "ib0"], ["cG"])
+    ts("in", T.OO[:, 0:256], T.oli[:, 0:256].indirect(L_IN), float(PO), None, A.add, None, ["oli", "L_IN"], [("OO", 0)], c=256, k="g")
+    for k in range(4):
+        copy("in", T.O16[:, 64 * k:64 * k + 64], T.OO[:, k:256:4], [("OO", 0)], [("O16p", k)])
+        iota(T.OO[:, k * OW + 256:k * OW + 264], [[0, 8]], 6000, [("OF1", k)], 8, **fl)
+    copy("in", Tof(T.ZTo, 0), T.tli[:, 0:256].indirect(L_IN), ["tli", "L_IN"], [("T", 0)], c=256, k="g")
+    copy("in", Nof(T.NSo, 0), T.nli[:, 0:256].indirect(L_IN), ["nli", "L_IN"], [("N", 0)], c=256, k="g")
+    iota(T.X[:, 4096:XW], [[0, 16]], 0, ["Xc"], 16, **fl)
+    m128 = T.io1[:, 15:143]
+    ts("c", col(C_LT2), T.ib[:, 0:1], 2.0, None, A.is_lt, None, ["ib0"], ["cLT2"])
+    ts("c", T.Ey[:], T.io1[:], col(C_G), -512.0, A.is_equal, A.mult, ["io1", "cG"], ["Ey"], c=144)
+    ts("c", T.Ep[:], T.io1[:], col(C_G), col(C_LT2), A.is_equal, A.mult, ["io1", "cG", "cLT2"], ["Ep"], c=144)
+    ts("c", T.Ib[:], m128, col(C_P), None, A.is_equal, None, ["io1", "cP"], ["Ib"], c=128)
+    ts("c", L_B8, T.io4[:, 56:60], col(C_E), None, A.add, None, ["io4e", "cE"], ["L_B8"])
+    ts("c", T.BD[:], T.io2[:], col(C_G), None, A.is_equal, None, ["io2", "cG"], ["BD"], c=128)
+    copy("c", T.thf[:], T.thi[:], ["thi"], ["thf"])
+    mm("c", T.b7[:, 0:4], "pth", "b7", T.BD[:], T.thf[:], ["BD", "thf"], True, True, 256)
+    act("c", T.If[:], T.Ib[:], F.Copy, ["Ib"], ["If"], c=128)
+    act("c", T.nI8[:], T.Ib[:], F.Identity, ["Ib"], ["nI8"], c=128, scale=-8192.0)
+    act("c", T.E2[:], T.Ey[:], F.Identity, ["Ey"], ["E2"], c=144, scale=-2.0)
+    act("c2", T.nIf[:], T.Ib[:], F.Identity, ["Ib"], ["nIf"], c=128, scale=-1.0)
+    act("c2", T.I99[:], T.Ib[:], F.Identity, ["Ib"], ["I99"], c=128, scale=99.0)
+    act("c2", T.E1f[:], T.Ey[:], F.Identity, ["Ey"], ["E1f"], c=144, scale=-1.0 / 512)
+    for s in range(S):
+        act("c2", T.sI[:, 128 * s:128 * s + 128], T.Ib[:], F.Identity, ["Ib"], [("sI", s)], c=128, scale=float(s + 2))
+    act("c2", T.thS[:], T.b7[:, 0:4], F.Identity, ["pth"], ["thS"], ["b7"], c=64, scale=512.0, bias=256.0 - 2048 * 512)
+    act("c2", T.thA[:], T.b7[:, 0:4], F.Identity, ["pth"], ["thA"], ["b7"], c=64, scale=256.0, bias=256.0 * (1 - 2048) + (1 << 20))
+    act("c2", T.thB[:], T.b7[:, 0:4], F.Identity, ["pth"], ["thB"], ["b7"], c=64, scale=256.0, bias=256.0 * (1 - 2048) - (1 << 20))
+    act("c2", col(C_DX), col(C_R), F.Identity, ["cR"], ["cDX"], c=64, bias=4096.0)
+    act("c2", col(C_DP), col(C_R), F.Identity, ["cR"], ["cDP"], c=64, bias=4096.0 + PO)
+    act("c2", T.sg1[:], T.io3[:], F.Sign, ["io3"], ["sg1"], c=128, scale=-1.0, bias=15.0)
+    act("c2", T.sg2[:], T.io3[:], F.Sign, ["io3"], ["sg2"], c=128)
+    act("c2", T.sg2[:, 15:128:16], T.c62[:], F.Identity, ["c62"], ["sg2"], c=64, scale=0.0, bias=8192.0)
+    iota(T.d0x[:], [[0, 256]], 1 << 23, ["d0x"], 256, **fl)
+    iota(T.d0n[:], [[0, 256]], 2, ["d0n"], 256, **fl)
+    act("c2", T.d0n[:, 0:256:32], T.c62[:], F.Identity, ["c62"], ["d0n"], c=64, scale=0.0, bias=BIG)
+    iota(T.hf[:, 256:264], [[0, 8]], 0, ["hf1"], 8, **fl)
+    ts("c2", T.DM[:], T.io3[:], col(C_R), None, A.is_equal, None, ["io3", "cR"], ["DM"], c=128)
+    ts("c2", T.LM[:], T.io3[:], col(C_R), 8192.0, A.is_ge, A.mult, ["io3", "cR"], ["LM"], c=128)
+    tt("c2", T.A01[:], T.E1f[:, 15:143], T.E1f[:, 14:142], A.subtract, ["E1f"], ["A01"], c=256)
+    ts("c2", col(C_R7), T.ib[:, 1:2], 32.0, col(C_E), A.mult, A.subtract, ["ib1", "cE"], ["cR7"])
+    copy("c2", L_B32, T.io4[:, 32:48], ["io4c"], ["L_B"])
+    ts("c2", L_OUT, T.io4[:, 16:32], col(C_R7), None, A.add, None, ["io4b", "cR7"], ["L_OUT"])
+
+    def gather(e, tag, dst, name, win, R, lists, b0, b1):
+        copy("%s%d" % (tag, b0 // 8), dst[:, 128 * b0:128 * b1], win.indirect(lists(8 * b0, 8 * b1)), R, blocks(name, b0, b1), c=128 * (b1 - b0), k="g", e=e)
+
+    def vmax(tag, m, mn, y, yn, b0, b1):
+        c0 = b0 % 8
+        bk = sorted(set(["pt%d" % (c // 4) for c in range(c0, c0 + b1 - b0)]))
+        tt("%s%d" % (tag, b0 // 8), m[:, 128 * b0:128 * b1], y[:, 128 * b0:128 * b1], T.pt[:, c0:c0 + b1 - b0], A.max,
+           blocks(yn, b0, b1) + bk, blocks(mn, b0, b1), bk, c=128 * (b1 - b0))
+
+    def tile(buf, z0, zR):
+        def half(h):
+            def fn():
+                for k in range(8):
+                    last = t.matmul(T.pt[:, 4 * h:4 * h + 4, k, :], T.Ib[:], buf[:, z0 + 64 * h:z0 + 64 * h + 64], True, True)
+                return last
+            op("t", "tile" if buf is T.ZTo else "tile3", fn, ["Ib"] + zR, ["pt%d" % h], ["pt%d" % h], 512, "pe")
+        half(0), half(1)
+
+    def fold(tag, out, res, bk, En, name, k, start, stop):
+        mm16("%s%d" % (tag, k), out, res, bk, T[En], lambda r: T[name][:, 1024 * k + r:1024 * (k + 1):16], [En] + blocks(name, 8 * k, 8 * k + 8), start, stop)
+
+    def lane_sums(o):
+        mm16("sz", T.b7[:, 8:16], "psz", "b7", T.Ey, lambda r: T.ZTo[:, o * ZT + r:o * ZT + 128:16], ["Ey", ("z", o)], True, True)
+        ts("sz", T.sz8[:], T.b7[:, 8:16], -float(1 << 20), None, A.add, None, ["psz"], ["sz8"], ["b7"])
+        copy("sz", T.NSo[:, o * NS + 256:o * NS + 320], T.sz8[:, 0:8].indirect(L_B8), ["sz8", "L_B8"], [("Sz", o)], c=64, k="g")
+
+    def chooser(Nap, NR, names):
+        pq = T.b6[:, 256:512]
+        mm("q", pq, "pQ", "b6", T.If[:], Nap, ["If"] + NR, True, False, 1024)
+        for i, nm in enumerate(names):
+            mm("q", pq, "pQ", "b6", T.nI8[:], T[nm][:], ["nI8", nm], False, i == len(names) - 1, 256)
+        ts("sel", T.sel[:], pq, 0.0, None, A.is_ge, None, ["pQ"], ["sel"], ["b6"], c=256)
+        copy("Qs", T.Qs[:], pq, ["pQ"], ["Qs"], ["b6"], c=256, e=CFG["eng"]["Qs"])
+
+    def part1(o):
+        for k in range(4):
+            act("OC", OC(o, 64 * k, 64 * k + 64), T.OO[:, o * OW + k:o * OW + 256:4], F.Identity, OOR(o), [("OC", o, k)], c=64, scale=1.0 / 512)
+        act("cm", T.b6[:, 256:512], OC(o), F.Identity, [("OC", o, k) for k in range(4)] + ["ac1"], ["pQ"], ["b6"], bias=T.acol[:, 4:5], scale=3232.0 * 512)
+        for e, b0, b1 in CFG["gp0" if o == 0 else "gp"]:
+            gather(e, "GP", T.gp, "gp", Pw, PR + O16R(o), lambda x0, x1: T.O16[:, 256 * o + x0:256 * o + x1], b0, b1)
+        for k in range(4):
+            bk, c0, c1 = "b2" if k % 2 == 0 else "b3", 64 * k, 64 * k + 64
+            mm("po", T[bk][:, 0:64], ("po", k % 2), bk, T.nI8[:], T.sel[:, k:256:4], ["nI8", "sel"], True, False, 64)
+            fold("po", T[bk][:, 0:64], ("po", k % 2), bk, "Ep", "gp", k, False, True)
+            tt("R%d" % k, T.Rf[:, c0:c1], T[bk][:, 0:64], T.Qs[:, k:256:4], A.max, [("po", k % 2), "Qs"], [("Rf", k)], [bk])
+            copy("R%d" % k, T.R16[:, c0:c1], T.Rf[:, c0:c1], [("Rf", k)], [("R16", k)])
+        for e, b0, b1 in CFG["y10" if o == 0 else "y1"]:
+            gather(e, "y1_", T.y1, "y1", Xw, XR + [("R16", b0 // 8)], lambda x0, x1: T.R16[:, x0:x1], b0, b1)
+        for b0, b1 in CFG["m1"]:
+            vmax("m1_", T.m1, "m1", T.y1, "y1", b0, b1)
+        for k in range(4):
+            bk, c0, c1 = "b0" if k % 2 == 0 else "b1", 64 * k, 64 * k + 64
+            pu, res = T[bk][:, 256:320], ("u", k % 2)
+            fold("uy", pu, res, bk, "Ey", "y1", k, True, False)
+            mm("us", pu, res, bk, T.If[:], T.NSo[:, o * NS + 256:o * NS + 320], ["If", ("Sz", o)], False, False, 256)
+            fold("um", pu, res, bk, "E2", "m1", k, False, True)
+            tt("h%d" % k, T.tf[:, c0:c1], pu, OC(o, c0, c1), A.mult, [res, ("OC", o, k)], [("tf", k)], [bk])
+            tt("h%d" % k, T.vi[:, c0:c1], T.tf[:, c0:c1], T.b6[:, 256 + c0:256 + c1], A.add, [("tf", k), "pQ"], [("vi", k)], ["b6"])
+            ts("h%d" % k, T.hi[:, c0:c1], T.vi[:, c0:c1], 5, 4095, A.arith_shift_right, A.bitwise_and, [("vi", k)], [("hi", k)])
+            copy("h%d" % k, T.Ho[:, 256 * o + c0:256 * o + c1], T.hi[:, c0:c1], [("hi", k)], [("Ho", o, k)])
+            send(T.Hi[:, 256 * o + c0:256 * o + c1], T.Ho[:, 256 * o + c0:256 * o + c1], "h%d" % (4 * o + k), 16384, [("Ho", o, k)], ("Hi", o, k))
+
+    def send_state(o):
+        z0, s0 = o * ZT, o * NS + 256
+        send2([(T.ZTi[:, z0:z0 + 128], T.ZTo[:, z0:z0 + 128]), (T.NSi[:, s0:s0 + 64], T.NSo[:, s0:s0 + 64])], "z%d" % o, 65536,
+              [("z", o), ("Sz", o)], [("Zi", o), ("Si", o)])
+        if o < S - 1:
+            send(OF(o + 1, 256), OF(o, 256), "o%d" % o, 131072, OOR(o) + [("Hi", o - 1, 3)], ("OO", o + 1))
+
+    def send_rest(o):
+        after = [("Ho", o, 3)] if o else []
+        if o < S - 1:
+            send2([(Tof(T.ZTi, o), Tof(T.ZTo, o)), (T.O16[:, (o + 1) * 256:(o + 2) * 256], T.O16[:, o * 256:(o + 1) * 256])], "t%d" % o, 131072,
+                  [("T", o)] + O16R(o) + after, [("Ti", o), ("O16", o + 1)])
+        else:
+            send(Tof(T.ZTi, o), Tof(T.ZTo, o), "t%d" % o, 65536, [("T", o)] + after, ("Ti", o))
+        send(Nof(T.NSi, o), Nof(T.NSo, o), "n%d" % o, 131072, [("N", o)] + after, ("Ni", o))
+
+    def part3(s):
+        tile(T.ZTi, s * ZT, [("Zi", s)])
+        for e, b0, b1 in CFG["y3"]:
+            gather(e, "y3_", T.y3, "y3", Xw, XR + [("Hi", s, b0 // 8)], lambda x0, x1: T.Hi[:, 256 * s + x0:256 * s + x1], b0, b1)
+        for b0, b1 in CFG["m3"]:
+            vmax("m3_", T.m3, "m3", T.y3, "y3", b0, b1)
+        for k in range(4):
+            out = T.b0[:, k:256:4]
+            mm("kc", out, "K", "b0", T.Ib[:], T.colc[:, k:256:4], ["Ib", "colc"], True, False, 64)
+            mm("ks", out, "K", "b0", T.If[:], T.NSi[:, s * NS + 256:s * NS + 320], ["If", ("Si", s)], False, False, 256)
+            fold("ky", out, "K", "b0", "Ey", "y3", k, False, False)
+            fold("km", out, "K", "b0", "E2", "m3", k, False, True)
+            copy("hf", T.hf[:, k:256:4], T.Hi[:, 256 * s + 64 * k:256 * s + 64 * k + 64], [("Hi", s, k)], [("hf", k)])
+        Tin = Tof(T.ZTi, s)
+        act("thE", T.d0x[:, 0:256:32], T.c62[:], F.Identity, ["c62", "thS"], ["d0x"], c=64, bias=T.thS[:, s:s + 1], scale=0.0)
+        act("thE", T.ta[:], Tin, F.Abs, [("Ti", s)], ["ta"], bias=-(s + 99) / 2.0)
+        act("thE", T.tb[:], T.ta[:], F.Sign, ["ta"], ["tb"], bias=-(98 - s) / 2.0)
+        act("thE", T.thE[:], T.tb[:], F.Identity, ["tb", "thA", "thB"], ["thE"], bias=T.thB[:, s:s + 1], scale=T.thA[:, s:s + 1])
+        if s < S - 1:
+            act("tgt", T.tgt[:], Tin, F.Relu, [("Ti", s)], ["tgt"], bias=-float(s + 1))
+
+    def first_of_block(x, ps, res, Mk, key, eq, du, t8, off, dummy, dR):
+        mm("lm" + x, ps, res, "b1", T.Ib[:], T.LM[:], ["Ib", "LM"], True, False, 128)
+        mm("row" + x, ps, res, "b1", T.BD[:], T[Mk][:], ["BD", Mk], False, True, 512)
+        scan("key" + x, T[key][:, ::-1], T.sg1[:, ::-1], T[Mk][:, ::-1], 0.0, A.mult, A.add, ["sg1", Mk], [key])
+        tt("eq" + x, T[eq][:], ps, T[key][:], A.is_equal, [res, key], [eq], ["b1"], c=128)
+        scan("du" + x, T[du][:], T.sg2[:], T[eq][:], 0.0, A.mult, A.add, ["sg2", eq], [du])
+        tt("off" + x, T[t8][:], T[du][:, 15:128:16], T[key][:, 0:128:16], A.add, [du, key], [t8])
+        ts("off" + x, T[off][:, 0:16:2], T[t8][:], dummy, None, A.min, None, [t8, dR], [off])
+
+    def refuse(s):
+        o = (s + 1) % S
+        scan("scM", T.scM[:], T.d0x[:], K, T.thS[:, s:s + 1], A.min, A.max, ["d0x", "K", "thS"], ["scM"], ["b0"], c=256)
+        act("Ksb", T.Ksb[:], K, F.Copy, ["K"], ["Ksb"], ["b0"])
+        copy("p", T.pi1[:], T.scM[:, 31:256:32], ["scM"], ["pi1"])
+        ts("p", T.pi2[:], T.pi1[:], 511, None, A.bitwise_and, None, ["pi1"], ["pi2"])
+        copy("p", T.cj[:], T.pi2[:], ["pi2"], ["cj"])
+        tt("MkO", T.MkO[:], OF(o).indirect(T.cj[:, 0:8]), T.DM[:], A.mult, OOR(o) + [("OF1", o), "cj", "DM"], ["MkO"], c=128, k="g")
+        tt("Mkh", T.Mkh[:], T.hf[:, 0:264].indirect(T.cj[:, 0:8]), T.DM[:], A.mult, HF + ["cj", "DM"], ["Mkh"], c=128, k="g")
+        act("Mkhb", T.Mkhb[:], T.Mkh[:], F.Copy, ["Mkh"], ["Mkhb"], c=128)
+        mm("val", T.b2[:, 64:192], "pv", "b2", T.E1f[:, 14:142], T.Mkh[:], ["E1f", "Mkh"], True, False, 512)
+        mm("val", T.b2[:, 64:192], "pv", "b2", T.A01[:], T.Mkhb[:], ["A01", "Mkhb"], False, True, 128)
+        act("val", T.val[:], T.b2[:, 64:192], F.Copy, ["pv"], ["val"], ["b2"], c=128)
+        first_of_block("P", T.b1[:, 0:128], "rowO", "MkO", "kO", "eqO", "duO", "pt8", "offP", col(C_DP), "cDP")
+        for c in range(7, -1, -1):
+            copy("scatP", Pw.indirect(T.offP[:, 2 * c:2 * c + 1]), T.val[:, 16 * c:16 * c + 16], ["offP", "val"], PR, c=16, k="s")
+
+    def learn(s):
+        z1 = (s + 1) * ZT
+        scan("scN", T.scN[:], T.d0n[:], K, 0.0, A.add, A.min, ["d0n", "K"], ["scN"], ["b0"], c=256)
+        tt("x", T.xi1[:], T.c62[:], T.scN[:, 31:256:32], A.subtract, ["c62", "scN"], ["xi1"])
+        ts("x", T.xi2[:], T.xi1[:], 511, None, A.bitwise_and, None, ["xi1"], ["xi2"])
+        copy("x", T.cb[:], T.xi2[:], ["xi2"], ["cb"])
+        tt("Mkb", T.Mkb[:], T.hf[:, 0:264].indirect(T.cb[:, 0:8]), T.DM[:], A.mult, HF + ["cb", "DM"], ["Mkb"], c=128, k="g")
+        first_of_block("X", T.b1[:, 128:256], "rowX", "Mkb", "kb", "eqb", "dub", "xt8", "offX", col(C_DX), "cDX")
+        copy("hb", T.hb[:], T.kb[:, 0:128:16], ["kb"], ["hb"])
+        tt("zs", T.zs[:], Xw.indirect(T.hb[:, 0:8]), T.ZTi[:, s * ZT:s * ZT + 128], A.add, XR + ["hb", ("Zi", s)], ["zs"], c=128, k="g")
+        ts("zi", T.zi[:], T.zs[:], 0.5, -0.25, A.mult, A.add, ["zs"], ["zi"], c=128)
+        copy("zn", T.ZTo[:, z1:z1 + 128], T.zi[:], ["zi"], [("z", s + 1)], c=128)
+        for c in range(7, -1, -1):
+            copy("scatX", Xw.indirect(T.offX[:, 2 * c:2 * c + 1]), T.ZTo[:, z1 + 16 * c:z1 + 16 * c + 16], ["offX", ("z", s + 1)], XR, c=16, k="s")
+
+    def marks(s):
+        mm("hn", T.b6[:, 0:256], "pHN", "b6", T.nIf[:], Nof(T.NSi, s), ["nIf", ("Ni", s)], True, False, 1024)
+        mm("hn", T.b6[:, 0:256], "pHN", "b6", T.If[:], T.hf[:, 0:256], ["If"] + HF, False, True, 1024)
+        tt("red", T.red[:], K, T.thE[:], A.is_lt, ["K", "thE"], ["red"], ["b0"], c=256)
+        tt("ref", T.ref[:], T.scM[:, 0:256].indirect(L_B32), T.Ksb[:], A.is_equal, ["scM", "L_B", "Ksb"], ["ref"], c=256, k="g")
+
+    def count():
+        if CFG["eng"]["A"] == "a":
+            act("A", T.junk[:], T.red[:], F.Copy, ["red"], ["junk", "ac0"], accum_out=T.acol[:, 0:1])
+        mm("A", T.b7[:, 0:1], "pA", "b7", T.BD[:], T.acol[:, 0:1], ["BD", "ac0"], True, True, 256)
+        ts("A", T.acol[:, 4:5], T.b7[:, 0:1], 32.0, CM0, A.mult, A.add, ["pA"], ["ac1"], ["b7"])
+
+    def new_state(s):
+        p7, p3 = T.b7[:, 256:512], T.b3[:, 256:512]
+        mm("T", p7, "pT", "b7", T.Ib[:], Tof(T.ZTi, s), ["Ib", ("Ti", s)], True, False, 256)
+        mm("T", p7, "pT", "b7", T.nI8[:], T.red[:], ["nI8", "red"], False, False, 256)
+        mm("T", p7, "pT", "b7", T.nI8[:], T.ref[:], ["nI8", "ref"], False, True, 256)
+        mm("T", p3, "pM", "b3", T.sI[:, 128 * s:128 * s + 128], T.red[:], [("sI", s), "red"], True, False, 256)
+        mm("T", p3, "pM", "b3", T.I99[:], T.ref[:], ["I99", "ref"], False, True, 256)
+        if CFG["eng"]["Tr"] == "a":
+            act("Tr", T.Tr[:], p7, F.Relu, ["pT"], ["Tr"], ["b7"])
+        else:
+            ts("Tr", T.Tr[:], p7, 0.0, None, A.max, None, ["pT"], ["Tr"], ["b7"], c=256)
+        tt("Tn", Tof(T.ZTo, s + 1), p3, T.Tr[:], A.add, ["pM", "Tr"], [("T", s + 1)], ["b3"], c=256)
+        tt("dN", T.dN[:], T.b6[:, 0:256], T.red[:], A.mult, ["pHN", "red"], ["dN"], ["b6"], c=256)
+        mm("N", p7, "pT", "b7", T.If[:], Nof(T.NSi, s), ["If", ("Ni", s)], True, False, 1024)
+        mm("N", p7, "pT", "b7", T.If[:], T.dN[:], ["If", "dN"], False, True, 1024)
+        copy("Nn", Nof(T.NSo, s + 1), p7, ["pT"], [("N", s + 1)], ["b7"], c=256, e=CFG["eng"]["Nn"])
+
+    act("tgt", T.tgt[:], Tof(T.ZTo, 0), F.Relu, [("T", 0)], ["tgt"])
+    tile(T.ZTo, 0, [("z", 0)])
+    lane_sums(0)
+    chooser(Nof(T.NSo, 0), [("N", 0)], ["tgt"])
+    iota(T.acol[:, 4:5], [[0, 1]], int(CM0), ["ac1"], 1, **fl)
+    send_state(0)
+    part1(0)
+    send_rest(0)
+    for s in range(S):
+        part3(s)
+        cnt["ph"] += 1
+        if s < S - 1:
+            refuse(s)
+            marks(s)
+            learn(s)
+            chooser(Nof(T.NSi, s), [("Ni", s)], ["tgt", "red", "ref"])
+            count()
+            tile(T.ZTo, (s + 1) * ZT, [("z", s + 1)])
+            lane_sums(s + 1)
+            new_state(s)
+            send_state(s + 1)
+            part1(s + 1)
+            send_rest(s + 1)
+        else:
+            learn(s)
+            dma("s", T.yx[:], T.X[:, 0:4096], 1048576, XR, ["yx"])
+            dma("s", T.yz[:], T.ZTo[:, S * ZT:S * ZT + 128], 32768, [("z", S)], ["yz"])
+            refuse(s)
+            marks(s)
+            new_state(s)
+            mm16("oP", T.b2[:, 256:512], "poP", "b2", T.Ep, lambda r: T.PW[:, PO + 256 * r:PO + 256 * r + 256], ["Ep"] + PR, True, True, 4096)
+            act("oP", T.oP[:], T.b2[:, 256:512], F.Copy, ["poP"], ["oP"], ["b2"])
+            dma("a", T.yp[:], T.oP[:], 131072, ["oP"], ["yp"])
+            copy("oT", T.oT[:], Tof(T.ZTo, S).indirect(L_OUT), [("T", S), "L_OUT"], ["oT"], c=256, k="g")
+            dma("s", T.yt[:], T.oT[:], 131072, ["oT"], ["yt"])
+            copy("oN", T.oN[:], Nof(T.NSo, S).indirect(L_OUT), [("N", S), "L_OUT"], ["oN"], c=256, k="g", e="a")
+            dma("a", T.yn[:], T.oN[:], 131072, ["oN"], ["yn"])
+
+    NODES[:] = nodes
+    for i in run_plan(nodes, EST, None, CFG)[0]:
+        emit(nodes[i])
+    TAG[0] = "end"
+    for e in "vatg":
+        g.sync.wait_ge(T.sem[e], cnt[e])
+    for k in range(cnt["d"]):
+        g.sync.wait_ge(T.sem["d%d" % k], 16)
+    g.wait_ge(T.sem.sent, cnt["sent"])

@@ -5,8 +5,9 @@ S = 4
 PO = 32
 XW, PWW = 4112, 4144
 BIG = float(1 << 23)
-ZT, NS, OW = 384, 320, 520
-bf, f32, i32, u16 = "bfloat16", "float32", "int32", "uint16"
+ZT, OW = 384, 264
+H = 2048.0
+bf, f16, f32, i32, u16 = "bfloat16", "float16", "float32", "int32", "uint16"
 
 
 def _sb(w, d):
@@ -15,64 +16,53 @@ def _sb(w, d):
 
 SCRATCH = {
     "X": _sb(XW, bf), "PW": _sb(PWW, bf), "y1": _sb(4096, bf), "m1": _sb(4096, bf), "y3": _sb(4096, bf), "m3": _sb(4096, bf), "gp": _sb(4096, bf),
-    "ZTo": _sb(5 * ZT, bf), "NSo": _sb(5 * NS, f32), "ZTi": _sb(4 * ZT, bf), "NSi": _sb(4 * NS, f32),
+    "ZTo": _sb(5 * ZT, bf), "No": _sb(4 * 256, f16), "ZTi": _sb(4 * ZT, bf), "Ni": _sb(4 * 256, f16),
     "OO": _sb(4 * OW, f32), "O16": _sb(4 * 256, u16), "Ho": _sb(4 * 256, u16), "Hi": _sb(4 * 256, u16),
     "pxi": _sb(256, i32), "oli": _sb(256, i32), "nli": _sb(256, i32), "tli": _sb(256, i32), "thi": _sb(4, i32),
-    "phi": _sb(256, bf), "plo": _sb(256, bf),
-    "ip": _sb(8, i32), "ib": _sb(8, i32), "col": _sb(16, f32), "io1": _sb(144, f32), "io2": _sb(128, f32), "io3": _sb(128, f32), "io4": _sb(64, f32),
-    "E2": _sb(144, bf), "Ey": _sb(144, bf), "Ep": _sb(144, bf), "E1f": _sb(144, f32), "A01": _sb(128, bf),
-    "If": _sb(128, f32), "nIf": _sb(128, f32), "Ib": _sb(128, bf), "nI8": _sb(128, bf), "I99": _sb(128, bf), "sI": _sb(512, bf),
-    "BD": _sb(128, f32), "DM": _sb(128, f32), "LM": _sb(128, bf), "colc": _sb(256, bf), "c62": _sb(8, f32),
+    "pxf": _sb(256, f32), "phi": _sb(256, bf), "plo": _sb(256, bf),
+    "ip": _sb(8, i32), "ib": _sb(8, i32), "col": _sb(16, f32), "io1": _sb(144, f32), "io2": _sb(128, f32), "io3": _sb(128, f32),
+    "Es": _sb(4 * 144, bf), "E1f": _sb(144, f32), "A01": _sb(128, bf), "Eg": _sb(32, bf), "If": _sb(128, f32), "Is": _sb(13 * 128, bf),
+    "I16": _sb(256, f16), "Pm": _sb(4 * 256, f16), "Rep": _sb(128, f16), "KL": _sb(512, f16), "KR": _sb(256, f16), "colc": _sb(256, bf),
+    "BD": _sb(128, f32), "DM": _sb(128, f32), "LM": _sb(128, bf), "ones": _sb(256, bf), "c62": _sb(8, f32),
     "sg1": _sb(128, f32), "sg2": _sb(128, f32), "d0x": _sb(256, f32), "d0n": _sb(256, f32),
-    "lst": _sb(64, u16), "thf": _sb(4, f32), "thS": _sb(4, f32), "thA": _sb(4, f32), "thB": _sb(4, f32),
-    "hf": _sb(264, f32), "scM": _sb(256, f32), "scN": _sb(256, f32), "Ksb": _sb(256, f32), "thE": _sb(256, f32), "ta": _sb(256, f32), "tb": _sb(256, f32),
-    "pi1": _sb(8, i32), "pi2": _sb(8, i32), "cj": _sb(8, u16), "xi1": _sb(8, i32), "xi2": _sb(8, i32), "cb": _sb(8, u16),
-    "MkO": _sb(128, f32), "Mkh": _sb(128, f32), "Mkhb": _sb(128, bf), "Mkb": _sb(128, f32), "kO": _sb(128, f32), "kb": _sb(128, f32),
-    "eqO": _sb(128, f32), "eqb": _sb(128, f32), "duO": _sb(128, f32), "dub": _sb(128, f32),
-    "pt8": _sb(8, f32), "xt8": _sb(8, f32), "offP": _sb(16, u16), "offX": _sb(16, u16), "val": _sb(128, bf), "hb": _sb(8, u16),
-    "zs": _sb(128, f32), "zi": _sb(128, i32), "sz8": _sb(8, f32),
-    "red": _sb(256, bf), "ref": _sb(256, bf), "tgt": _sb(256, bf), "sel": _sb(256, bf), "Qs": _sb(256, f32), "dN": _sb(256, f32), "Tr": _sb(256, f32),
-    "junk": _sb(256, bf), "acol": _sb(8, f32), "Rf": _sb(256, f32), "R16": _sb(256, u16), "tf": _sb(256, f32), "vi": _sb(256, i32), "hi": _sb(256, i32),
+    "LB": _sb(16, u16), "thf": _sb(4, f32), "Sz": _sb(256, f16),
+    "hf": _sb(264, f32), "scM": _sb(256, f32), "scN": _sb(256, f32), "e1": _sb(256, f32), "e2": _sb(256, bf),
+    "pi1": _sb(8, i32), "pi2": _sb(8, i32), "xi1": _sb(8, i32), "xi2": _sb(8, i32), "cj": _sb(16, u16),
+    "MkP": _sb(128, f32), "MkX": _sb(128, f32), "Mkh": _sb(128, f32), "Mkhb": _sb(128, bf), "gb": _sb(128, bf),
+    "keyP": _sb(128, f32), "keyX": _sb(128, f32), "eqP": _sb(128, f32), "eqX": _sb(128, f32), "duP": _sb(128, f32), "duX": _sb(128, f32),
+    "t8P": _sb(8, f32), "t8X": _sb(8, f32), "offP": _sb(16, u16), "offX": _sb(16, u16), "val": _sb(128, bf), "hb": _sb(8, u16),
+    "zs": _sb(128, f32), "zi": _sb(128, i32),
+    "sg": _sb(256, bf), "ref": _sb(256, bf), "s3": _sb(256, bf), "Tr": _sb(256, bf), "Qs": _sb(384, f32), "t1": _sb(256, f32),
+    "Rf": _sb(512, f16), "uf": _sb(512, f16), "Kf": _sb(512, f16),
+    "acol": _sb(8, f32), "R16": _sb(256, u16), "tf": _sb(256, f32), "vi": _sb(256, i32), "hi": _sb(256, i32),
     "oP": _sb(256, f32), "oN": _sb(256, f32), "oT": _sb(256, f32),
-    "b0": ("psum", [128, 512], f32), "b1": ("psum", [128, 512], f32), "b2": ("psum", [128, 512], f32), "b3": ("psum", [128, 512], f32),
-    "pt": ("psum", [128, 8, 8, 16], f32), "b6": ("psum", [128, 512], f32), "b7": ("psum", [128, 512], f32),
 }
+for _b in ("b0", "b1", "b2", "b3", "pt", "pu", "b6", "b7"):
+    SCRATCH[_b] = ("psum", [128, 512], f32)
 SEMAPHORES = (["v", "a", "t", "g", "sent"] + ["d%d" % i for i in range(20)] + ["h%d" % i for i in range(16)]
-              + ["z%d" % i for i in range(4)] + ["t%d" % i for i in range(4)] + ["n%d" % i for i in range(4)] + ["o%d" % i for i in range(3)])
+              + ["z%d" % i for i in range(4)] + ["t%d" % i for i in range(4)] + ["n%d" % i for i in range(4)] + ["o%d" % i for i in range(3)] + ["l%d" % i for i in range(3)])
 TAG = [""]
-NODES = []
-
-
-def _turns(names):
-    return {x.replace("send_", "send "): 0.5 * i for i, x in enumerate(names.split())}
-
+PLAN = []
 
 CFG = {
-    "gp0": [("a", 0, 8), ("v", 8, 16), ("a", 16, 24), ("v", 24, 32)],
-    "gp": [("a", 0, 8), ("a", 8, 16), ("a", 16, 24), ("a", 24, 32)],
-    "y10": [("v", 0, 4), ("a", 4, 8), ("a", 8, 16), ("a", 16, 24), ("a", 24, 30), ("a", 30, 32)],
-    "y1": [("a", 0, 3), ("v", 3, 8), ("v", 8, 16), ("a", 16, 24), ("a", 24, 30), ("a", 30, 32)],
-    "m1": [(0, 8), (8, 16), (16, 17), (17, 18), (18, 19), (19, 24), (24, 29), (29, 30), (30, 32)],
-    "y3": [("a", 0, 8), ("a", 8, 16), ("a", 16, 21), ("v", 21, 24), ("a", 24, 29), ("a", 29, 32)],
-    "m3": [(0, 8), (8, 16), (16, 24), (24, 27), (27, 29), (29, 32)],
-    "eng": {"Qs": "a", "Tr": "a", "Nn": "a", "A": "a"},
-    "xs": 1024,
-    "slack": 0.0,
-    "share": 0.2,
-    "turn": _turns("Qs R1 us MkO keyP uy1 zs Mkhb val h1 kc rowP km0 hb T scM po0 q GP0 send_h rowX km1 Mkh keyX h0 Ksb scN lmP GP1 eqP ref R0 sz hn h3 "
-                   "duP lmX zn p um0 red po po3 um2 um3 uy2 scatP cm send_z send_t y1_0 h2 zi uy0 R3 R2 m1_0 offP A y1_1 po2 GP2 uy3 send_n GP3 x "
-                   "tile3 Mkb eqX offX scatX OC duX m1_1 m1_2 um1 y1_2 y1_3 sel m1_3 y3_0 km3 ks Nn ky2 y3_1 Tr po1 m3_0 m3_1 y3_2 ky0 dN y3_3 ky3 "
-                   "m3_2 N km2 send_o tile tgt m3_3 hf ky1 Tn thE"),
-    "turn0": _turns("R1 dma px send_z us fill iota c uy1 in h0 send_t po0 Qs sel tgt kc send_n um2 R3 sz send_o GP0 GP1 R0 h1 send_h po OC h3 R2 GP2 "
-                    "po3 cm h2 GP3 q y1_0 y1_1 uy0 uy2 uy3 um3 po1 m1_0 y1_2 um0 ky2 m1_1 m1_2 m1_3 km0 m3_0 ky3 y1_3 po2 ks tile y3_0 y3_1 um1 "
-                    "y3_2 m3_1 m3_2 tile3 ky0 y3_3 km1 km3 ky1 m3_3 hf km2 c2 thE"),
-    "turn4": _turns("Mkb x offX zs val scatX scN duX Mkhb rowX zn dma duP eqX T eqP dN lmP hb oP keyX MkO zi oN Mkh keyP scM Ksb ref p offP scatP Tn "
-                    "rowP oT N red Nn lmX hn Tr"),
+    "gp": [0, 128, 256], "y1": [0, 128, 224, 256], "y3": [0, 128, 224, 256],
+    "run": {"a": 4, "v": 2, "m": 4},
+    "eng": {"Qs": "a", "Tn": "a", "z0": "a", "z1": "v"},
+    "xs": 256, "share": 0.1, "ahead": 50.0, "hold": {},
+    "after": {"t": -1, "n": 9},
+    "turn": "scM scN p MkP x lmP rowP Mkh keyP eqP k2 sg val duP offP scatP MkX lmX rowX keyX hb zs zp A cm ref eqX q duX s3 zi zn offX send_z Tr qn q2 Qs "
+            "zt szu scatX T Tn send_t send_h gp_0 po0 R0 gp_1 po1 R1 gp_2 po2 R2 us y1_0 uy0 m1_0 um0 h0 zt3 szk y1_1 uy1 m1_1 um1 h1 y1_2 uy2 m1_2 um2 h2 "
+            "y1_3 uy3 m1_3 um3 h3 N t1 Nn send_n ks hf y3_0 ky0 m3_0 km0 K0 y3_1 ky1 m3_1 km1 K1 y3_2 ky2 m3_2 km2 K2 y3_3 ky3 m3_3 km3 K3 e send_o send_l",
+    "first": "PW dma_pxi dma_oli dma_thi dma_tli dma_ZTo dma_nli px dma_PW dma_X send_z",
+    "last": "scN x scM p MkX lmX rowX keyX hb eqX zs duX zi offX zn scatX dma_yx",
 }
-EST = dict(cyc=1.04, g=1.56, sc=3.8, ind=55.0, pe=0.52, wake=60.0, dlat=2000.0, dbw=250.0, issue=1000.0, rlat=2600.0, rbw=60.0)
+CFG.update(gp=[0, 96, 224, 256], y1=[0, 96, 192, 256], y3=[0, 128, 224, 256], seq="p0 p1 p2 u0 u1 u2", flat=(64,))
+CFG.update({'turn': 'hb p keyP scM scN MkP x lmP rowP Mkh eqP k2 po2 offP sg val duP scatP MkX lmX rowX keyX zs zp R1 A ref eqX q duX s3 zi zn offX R2 send_z Tr qn q2 Qs scatX send_h R0 po po0 po1 h0 h2 K0 K1 K2 gp_0 zt gp_1 cm T N send_t us uy0 Tn szu ks um0 m1_0 y1_0 uy1 h1 um1 m1_1 y1_1 zt3 uy2 um2 m1_2 y1_2 gp_2 ky0 km0 m3_0 m3_1 szk t1 Nn hf e ke ky1 km1 y3_0 y3_1 ky2 km2 m3_2 y3_2 send_l send_o send_n', 'first': 'PW R2 dma_pxi dma_oli dma_thi um0 dma_tli dma_ZTo dma_nli zt3 px dma_PW dma_X send_z', 'last': 'scN x lmP scM p MkX lmX rowX Mkh keyX eqX zs duX zi offX zn scatX dma_yx', 'hold': {'R0': 70, 'R1': 70, 'R2': 70, 'h0': 70, 'h1': 70, 'h2': 70, 'K0': 70, 'K1': 70, 'K2': 70, 'Qs': 300, 'p': 70, 'MkP': 70, 'zi': 150, 's3': 300}, 'run': {'a': 3, 'v': 2, 'm': 2, 'y3_2v': 6, 'y1_2v': 0, 'gp_0a': 5, 'y3_0a': 8, 'y1_2a': 1, 'y3_1a': 8, 'gp_1v': 3, 'y1_0v': 6, 'gp_1a': 8, 'y3_0v': 8, 'm3_0m': 3, 'y3_1v': 3, 'gp_2a': 6, 'y3_2a': 5}, 'ahead': 50.0, 'share': 0})
+CFG.update(dict(gp=[0,64,192,256],y1=[0,64,128,192,256],y3=[0,128,224,256],after={"t":-1,"n":-1},seq="p0 u0 p1 p2 u1 u2 u3", **{'turn': 'rowX Mkh keyP scM scN p MkP x lmP rowP eqP zi k2 sg N t1 val duX duP offP scatP MkX lmX keyX hb zs zp eqX q po1 s3 Qs zn A offX send_z Nn Tr qn q2 ref scatX send_h po po0 cm R0 R1 po2 R2 h0 h1 h2 h3 szu K0 K1 K2 K3 zt uy0 um0 m1_0 gp_0 y1_0 gp_1 gp_2 T y1_1 Tn send_t uy1 um1 us m1_1 zt3 szk uy2 um2 m1_2 y1_2 uy3 um3 m1_3 y1_3 ks ky0 km0 send_o m3_0 y3_0 m3_1 send_n hf e ke ky1 km1 y3_1 ky2 km2 m3_2 y3_2 ky3 km3 m3_3 y3_3 send_l', 'first': 'PW dma_pxi dma_oli dma_thi po dma_tli dma_nli px dma_PW dma_X send_z', 'last': 'scN x scM p MkX lmX rowX hb eqX zs zi offX zn scatX dma_yx', 'hold': {'p': 150, 'MkP': 60, 'rowP': 60, 'eqP': 60, 'duP': 60, 'scatP': 60, 'R0': 60, 'R1': 150, 'R2': 1, 'h0': 80, 'h1': 60, 'h2': 60, 'h3': 60, 'K0': 1, 'K1': 60, 'K2': 60, 'po0': 60, 'um0': 60, 'um1': 60, 'um2': 60, 'um3': 1, 'km2': 60, 'scM': 60, 'val': 60, 'po1': 1, 'scatX': 250, 'y1_2': 40, 'uy0': 1, 'po': 40, 'km0': 40}, 'run': {'a': 4, 'v': 2, 'm': 8, 'y3_1v': 1, 'm3_1m': 6, 'y1_2v': 2, 'm1_2m': 8, 'm3_2m': 5, 'y1_3v': 6, 'm3_0m': 4, 'm1_0m': 5, 'y3_0a': 3, 'gp_2a': 8, 'gp_1a': 8, 'gp_0a': 5}, 'ahead': 0, 'share': 0}))
+EST = dict(cyc=0.87, g=1.56, sc=3.8, ind=55.0, pe=0.6, wake=185.0, dlat=800.0, drow=160.0, dbw=380.0, issue=400.0, rlat=700.0, rrow=320.0, rbw=128.0)
 
 
-def run_plan(nodes, P, order=None, cfg=None):
+def run_plan(nodes, P, cfg):
     n = len(nodes)
     busy, lat = [0.0] * n, [0.0] * n
     for i, x in enumerate(nodes):
@@ -80,74 +70,93 @@ def run_plan(nodes, P, order=None, cfg=None):
         if k == "n":
             busy[i] = max(64, c) * P["cyc"]
         elif k == "g":
-            busy[i] = P["ind"] + c * P["g"] * P["cyc"]
+            busy[i] = (0.0 if x["e"] == "x" else P["ind"]) + c * P["g"] * P["cyc"]
         elif k == "s":
             busy[i] = P["ind"] + c * P["sc"] * P["cyc"]
         elif k == "pe":
             busy[i] = c * P["pe"]
         elif k == "dma":
-            busy[i], lat[i] = 60.0, P["dlat"] + c / P["dbw"]
+            busy[i], lat[i] = 60.0, P["dlat"] + P["drow"] + c / P["dbw"]
         else:
-            busy[i], lat[i] = P["issue"], P["rlat"] + c / P["rbw"]
-    free, pipe, done, start, bfree = {}, {"dma": 0.0, "send": 0.0}, [None] * n, [0.0] * n, {}
-
-    def est(i):
-        x = nodes[i]
-        t0 = free.get(x["e"], 0.0)
+            busy[i], lat[i] = P["issue"], P["rlat"] + P["rrow"] + c / P["rbw"]
+    free, pipe, done, bfree = {}, [0.0], [None] * n, {}
+    suc = [[] for i in range(n)]
+    for i, x in enumerate(nodes):
         for p in x["pre"]:
-            t0 = max(t0, done[p] + (0.0 if x["e"] == "t" and nodes[p]["e"] == "t" else P["wake"]))
+            suc[p].append(i)
+    prio, since = [0.0] * n, {}
+    turn = [({0: cfg["first"], S: cfg["last"]}.get(ph, "") + " " + cfg["turn"]).split()[::-1] for ph in range(S + 1)]
+    turn = [{x.replace("send_", "send "): j for j, x in enumerate(names)} for names in turn]
+    for i in range(n - 1, -1, -1):
+        x = nodes[i]
+        if x["tag"] in turn[x["ph"]]:
+            prio[i] = 1e4 * (turn[x["ph"]][x["tag"]] - 1000 * x["ph"])
+        else:
+            prio[i] = busy[i] + lat[i] + max([prio[j] for j in suc[i]] + [-1e7 * S])
+
+    def est(i, e):
+        x = nodes[i]
+        if i not in since:
+            since[i] = max([done[p] + (0.0 if e == "t" and nodes[p]["e"] == "t" else P["wake"]) for p in x["pre"]] + [0.0])
+        t0 = max(since[i], free.get(e, 0.0))
         for b in x["B"]:
             for e2, t2 in bfree.get(b, {}).items():
-                if e2 != x["e"]:
+                if e2 != e:
                     t0 = max(t0, t2 + P["wake"])
         return t0
 
-    def place(i, t0):
+    def place(i, e, t0):
         x = nodes[i]
-        start[i] = t0
-        free[x["e"]] = t0 + busy[i]
-        k, c = x["c"]
-        if k in pipe:
-            d = c / P["dbw" if k == "dma" else "rbw"]
-            pipe[k] = max(pipe[k] + d + (150.0 if k == "dma" else 500.0), t0 + busy[i] + lat[i])
-            done[i] = pipe[k]
+        x["e"] = e
+        free[e] = t0 + busy[i]
+        k = x["c"][0]
+        if k == "dma":
+            pipe[0] = done[i] = max(pipe[0], t0 + busy[i] + P["dlat"]) + lat[i] - P["dlat"]
+        elif k == "send":
+            pipe[0] = max(pipe[0], t0 + busy[i]) + lat[i] - P["rlat"]
+            done[i] = pipe[0] + P["rlat"]
         else:
             done[i] = t0 + busy[i]
         for b in x["B"]:
-            bfree.setdefault(b, {})[x["e"]] = done[i]
+            bfree.setdefault(b, {})[e] = done[i]
 
-    if order is not None:
-        for i in order:
-            place(i, est(i))
-        return order, max(done), start, done
-    suc = [[] for i in range(n)]
-    prio = [-100.0 * x["ph"] - cfg["turn" if 0 < x["ph"] < S else "turn%d" % x["ph"]].get(x["tag"], cfg["turn"].get(x["tag"], 0.0)) for x in nodes]
-    left, lastw, before = [0] * n, {}, {}
-    for p, i in sorted([(-prio[i], i) for i, x in enumerate(nodes) if x["tag"][:2] in ("GP", "y1", "y3", "m1", "m3")]):
-        if nodes[i]["e"] in lastw:
-            before[i] = lastw[nodes[i]["e"]]
-        lastw[nodes[i]["e"]] = i
-    for i, x in enumerate(nodes):
-        pre = set(x["pre"] + ([before[i]] if i in before else []))
-        left[i] = len(pre)
-        for p in pre:
-            suc[p].append(i)
+    left = [len(x["pre"]) for x in nodes]
     ready, order = [i for i in range(n) if left[i] == 0], []
     while ready:
-        es = [(est(i), i) for i in ready]
-        t0, i0 = min(es)
-        mine = [(prio[i], -i, t, i) for t, i in es if nodes[i]["e"] == nodes[i0]["e"]]
-        t1, i1 = max([m for m in mine if m[2] <= t0 + cfg["slack"]])[2:]
-        t1, i1 = max([m for m in mine if m[2] <= t1 + cfg["share"] * busy[i1]])[2:]
-        place(i1, t1)
+        es = [(est(i, e), e, i) for i in ready for e in (nodes[i]["e"] if nodes[i]["e"] != "x" else "av" if cfg["run"].get(nodes[i]["tag"] + "v", 1) else "a")]
+        t0, e0 = min(es)[:2]
+        mine = [(prio[i] - (1e9 if e == "v" and nodes[i]["e"] == "x" else 0.0), -i, t, i) for t, e, i in es if e == e0]
+        now = sorted([m for m in mine if m[2] <= t0], reverse=True)
+        soon = [(m[2] + cfg["hold"][nodes[m[3]]["tag"]], m) for m in mine if m > now[0] and nodes[m[3]]["tag"] in cfg["hold"]]
+        room, first = min(soon) if soon else (1e18, None)
+        t1, i1 = ([m for m in now if t0 + busy[m[3]] + (P["ind"] if nodes[m[3]]["e"] == "x" else 0.0) <= room] + [first])[0][2:]
+        x, run = nodes[i1], [i1]
+        if x["span"]:
+            near = sorted(i for t, e, i in es if e == e0 and t <= t1 and nodes[i]["tag"] == x["tag"] and nodes[i]["ph"] == x["ph"])
+            kind = "m" if x["e"] == "v" else e0
+            most = max(1, min(cfg["run"].get(x["tag"] + kind, cfg["run"][kind]), int((room - t1 - (P["ind"] if kind != "m" else 0.0)) / busy[i1])))
+            if kind == "v":
+                near = near[::-1]
+            run = near[:1]
+            for i in near[1:min(most, 4) if kind == "m" else most]:
+                if abs(i - run[-1]) != 1:
+                    break
+                run.append(i)
+            run.sort()
+            i1, x = run[0], nodes[run[0]]
+            busy[i1] = sum(busy[i] for i in run) + (P["ind"] if kind != "m" else 0.0)
+            x["span"] = (x["span"][0], nodes[run[-1]]["span"][1])
+            x["R"], x["W"] = sum([nodes[i]["R"] for i in run], []), sum([nodes[i]["W"] for i in run], [])
+        place(i1, e0, t1)
         order.append(i1)
-        ready.remove(i1)
-        for j in suc[i1]:
-            left[j] -= 1
-            if left[j] == 0:
-                ready.append(j)
-    assert len(order) == n
-    return order, max(done), start, done
+        for i in run:
+            done[i] = done[i1]
+            ready.remove(i)
+            for j in suc[i]:
+                left[j] -= 1
+                if left[j] == 0:
+                    ready.append(j)
+    return [(i, {k: nodes[i][k] for k in ("e", "span", "R", "W")}) for i in order]
 
 
 def rank_program(g, core, T, topo):
@@ -163,12 +172,12 @@ def rank_program(g, core, T, topo):
     n_out = len(topo.engines(core, nxt))
     v, a, t = g.vector, g.scalar, g.tensor
     Q = {"v": v, "a": a, "t": t, "g": g, "s": g.sync}
-    cnt = {"v": 0, "a": 0, "t": 0, "g": 0, "d": 0, "sent": 0, "ph": 0}
+    cnt = {"v": 0, "a": 0, "t": 0, "g": 0, "d": 0, "sent": 0, "ph": 0, "F": 0}
     clock = {e: {} for e in Q}
     wr, rd, bank = {}, {}, {}
     nodes, lw, lr, lb = [], {}, {}, {}
 
-    def node(e, tag, c, fn, R, W, B):
+    def node(e, tag, c, fn, R, W, B, span=None):
         i = len(nodes)
         pre = set(lw[r] for r in R if r in lw)
         for w in W:
@@ -185,26 +194,17 @@ def rank_program(g, core, T, topo):
         for w in W:
             lw[w] = i
             lr[w] = []
-        nodes.append(dict(e=e, tag=tag, ph=cnt["ph"], c=c, fn=fn, R=list(R), W=list(W), B=list(B), pre=sorted(pre)))
+        nodes.append(dict(e=e, tag=tag, c=c, fn=fn, R=list(R), W=list(W), B=list(B), pre=sorted(pre), span=span, ph=cnt["ph"]))
 
     def op(e, tag, fn, R=(), W=(), B=(), c=64, k="n"):
         node(e, tag, (k, c), fn, R, W, B)
 
     def dma(e, out, in_, nb, R=(), W=()):
-        node(e, "dma", ("dma", nb), lambda: Q[e].dma_start(out, in_), R, W, ())
+        node(e, "dma_%s" % out.name, ("dma", nb), lambda: Q[e].dma_start(out, in_), R, W, ())
 
     def send(out, in_, sem, nb, R, lands):
         wr[lands] = (sem, sem, n_in, {})
         node("g", "send " + sem[:1], ("send", nb), lambda: g.remote_dma(out, in_, T.sem[sem], T.sem.sent, pid, rid, mask), R, [lands], ())
-
-    def send2(pairs, sem, nb, R, lands):
-        es = topo.engines(core, nxt)
-        half = [es[:len(es) // 2], es[len(es) // 2:]]
-        for x in lands:
-            wr[x] = (sem, sem, n_in, {})
-        trs = [RemoteDMATransfer(dst_ids=[DstId(rid=rid, pnc=pid)], dma_engine_mask=sum(1 << e for e in h), remote_sem=T.sem[sem], src=p[1], dst=p[0])
-               for p, h in zip(pairs, half)]
-        node("g", "send " + sem[:1], ("send", nb), lambda: g.remote_dma_fused(trs, local_sem=T.sem.sent), R, lands, ())
 
     def need(e, ev):
         sem, val, ck = ev[1], ev[2], ev[3]
@@ -252,7 +252,7 @@ def rank_program(g, core, T, topo):
         else:
             waits(e, e, x["R"], x["W"], x["B"])
             cnt[e] += 1
-            x["fn"]().then_inc(T.sem[e], 1)
+            (x["fn"](e, *x["span"]) if x["span"] else x["fn"]()).then_inc(T.sem[e], 1)
             note((e, e, cnt[e], dict(clock[e])), x["R"], x["W"], x["B"])
 
     def copy(tag, out, in_, R, W, B=(), c=64, k="n", e="v"):
@@ -267,6 +267,9 @@ def rank_program(g, core, T, topo):
         else:
             op("v", tag, lambda: v.tensor_scalar(out, in0, s1, s2, o0, o1), R, W, B, c, k)
 
+    def plus(tag, out, in0, x, R, W, B=(), c=64):
+        ts(tag, out, in0, x, None, A.add, None, R, W, B, c)
+
     def tt(tag, out, in0, in1, o, R, W, B=(), c=64, k="n"):
         op("v", tag, lambda: v.tensor_tensor(out, in0, in1, o), R, W, B, c, k)
 
@@ -276,8 +279,11 @@ def rank_program(g, core, T, topo):
     def act(tag, out, in_, f, R, W, B=(), c=256, **kw):
         op("a", tag, lambda: a.activation(out, in_, f, **kw), R, W, B, c)
 
-    def fill(out, val, W, c=64):
-        op("v", "fill", lambda: v.memset(out, val), (), W, (), c)
+    def affine(tag, out, in_, scale, bias, R, W, B=(), c=256):
+        if CFG["eng"].get(tag, "a") == "a":
+            act(tag, out, in_, F.Identity, R, W, B, c, scale=scale, bias=bias)
+        else:
+            ts(tag, out, in_, scale, bias, A.mult, A.add, R, W, B, c)
 
     def iota(out, pat, base, W, c, cm=0, **kw):
         op("g", "iota", lambda: g.iota(out, pat, base, cm, **kw), (), W, (), 156 + 2 * c)
@@ -285,315 +291,384 @@ def rank_program(g, core, T, topo):
     def mm(tag, out, res, bk, l, r, R, start, stop, c):
         op("t", tag, lambda: t.matmul(out, l, r, start, stop), R, [res], [bk], c, "pe")
 
-    def mm16(tag, out, res, bk, E, rhs, R, start, stop, c=1024):
-        def fn():
-            for r in range(16):
-                last = t.matmul(out, E[:, 15 - r:143 - r], rhs(r), start and r == 0, stop and r == 15)
-            return last
-        op("t", tag, fn, R, [res], [bk], c, "pe")
-
     def blocks(name, b0, b1):
         return [(name, b) for b in range(b0, b1)]
 
     def col(i):
         return T.col[:, i:i + 1]
 
-    Xw, Pw, K = T.X[:, 0:XW], T.PW[:, 0:PWW], T.b0[:, 0:256]
-    C_P, C_R, C_G, C_LT2, C_DX, C_DP, C_PI, C_E, C_R7 = range(9)
-    L_IN, L_OUT, L_B32, L_B8 = T.lst[:, 0:16], T.lst[:, 16:32], T.lst[:, 32:48], T.lst[:, 56:60]
+    IS = {"I": 1.0, "nI": -1.0, "n13": -8192.0, "p13": 8192.0, "p7": 128.0, "p6": 64.0, "p12": 4096.0, "n12": -4096.0, "i1": 0.5}
+    for s in range(S):
+        IS["c%d" % s] = (s - 97.0) / 2
+
+    def Id(name):
+        j = 128 * list(IS).index(name)
+        return T.Is[:, j:j + 128]
+
+    def add(tag, out, res, bk, name, rhs, R, start=False, stop=True, c=256):
+        mm(tag, out, res, bk, Id(name), rhs, R + [name], start, stop, c)
+
+    def chunks(name):
+        return list(enumerate(zip(CFG[name], CFG[name][1:])))
+
+    def chunk_of(name, b):
+        return [k for k, (c0, c1) in chunks(name) if c0 <= 8 * b < c1][0]
+
+    Xw, Pw, K1, K2 = T.X[:, 0:XW], T.PW[:, 0:PWW], T.b0[:, 0:256], T.b1[:, 256:512]
+    pq, pa, pb = T.b6[:, 0:256], T.b7[:, 0:256], T.b7[:, 256:512]
+    C_P, C_R, C_G, C_LT2, C_DX, C_DP, C_E, C_R8, C_T = range(9)
     XR, PR = ["Xa", "Xb", "Xc"], ["PW", "PWa", "PWb"]
-    HF = [("hf", k) for k in range(4)] + ["hf1"]
+    HF = [("hf", k) for k, c in chunks("y1")] + ["hf1"]
+    LAST = ("Ho", len(HF) - 2)
     CM0 = -37888.0 - 80.0 * 131072
 
-    def OF(k, w=264):
-        return T.OO[:, k * OW:k * OW + w]
+    def OF(k, c0=0, c1=256):
+        return T.OO[:, k * OW + c0:k * OW + c1]
 
-    def OC(k, a0=0, a1=256):
-        return T.OO[:, k * OW + 264 + a0:k * OW + 264 + a1]
+    def Nof(buf, k, c0=0, c1=256):
+        return buf[:, k * 256 + c0:k * 256 + c1]
 
-    def Nof(buf, k):
-        return buf[:, k * NS:k * NS + 256]
-
-    def Tof(buf, k):
-        return buf[:, k * ZT + 128:k * ZT + 384]
-
-    def OOR(k):
-        return [("OO", k)]
-
-    def O16R(k):
-        return [("O16p", j) for j in range(4)] if k == 0 else [("O16", k)]
+    def Tof(buf, k, c0=0, c1=256):
+        return buf[:, k * ZT + 128 + c0:k * ZT + 128 + c1]
 
     dma("s", T.pxi[:], T.px[:], 131072, W=["pxi"])
     dma("a", T.oli[:], T.ol[:], 131072, W=["oli"])
     dma("s", T.tli[:], T.tl[:], 131072, W=["tli"])
     dma("a", T.nli[:], T.nl[:], 131072, W=["nli"])
     dma("s", T.ZTo[:, 0:128], T.z[:], 32768, W=[("z", 0)])
+    dma("a", T.thi[0:8, :], T.th[:], 128, W=["thi"])
     xs = CFG["xs"]
     dma("s", T.X[:, 0:xs], T.x[:, 0:xs], 256 * xs, W=["Xa"])
+    op("v", "PW", lambda: v.memset(T.PW[:], 0.0), (), ["PW"], (), 2072)
+    plus("px", T.phi[:], T.pxi[:], -H, ["pxi"], ["phi"], c=256)
+    plus("px", T.pxf[:], T.pxi[:], -H, ["pxi"], ["pxf"], c=256)
+    tt("px", T.plo[:], T.pxf[:], T.phi[:], A.subtract, ["pxf", "phi"], ["plo"], c=512)
+    dma("s", T.PW[0:128:16, PO:PO + 4096], T.phi[:], 65536, ["phi", "PW"], ["PWa"])
+    dma("s", T.PW[1:128:16, PO:PO + 4096], T.plo[:], 65536, ["plo", "PW"], ["PWb"])
+    dma("s", T.X[:, xs:4096], T.x[:, xs:4096], 256 * (4096 - xs), ["plo", "PW"], ["Xb"])
+    plus("in", T.O16[:, 0:256], T.oli[:], float(PO), ["oli"], [("O16", 0)], c=256)
+    plus("in", OF(0), T.oli[:], float(PO), ["oli"], [("OO", 0)], c=256)
+    copy("in", Tof(T.ZTo, 0), T.tli[:], ["tli"], [("T", 0)], c=256)
+    plus("in", Nof(T.No, 0), T.nli[:], -H, ["nli"], [("N", 0)], c=256)
+
     fl = dict(allow_small_or_imprecise_dtypes=True)
     iota(T.ip[:], [[0, 8]], 0, ["ip"], 8, 1)
-    iota(T.io4[:, 0:16], [[1, 8], [-128, 2]], 248, ["io4a"], 16, **fl)
     iota(T.io1[:], [[1, 144]], -15, ["io1"], 144, **fl)
-    iota(T.io4[:, 56:60], [[2, 4]], 0, ["io4e"], 4, **fl)
     iota(T.io2[:], [[16, 8], [0, 16]], 0, ["io2"], 128, **fl)
     iota(T.io3[:], [[0, 8], [1, 16]], 0, ["io3"], 128, **fl)
+    iota(T.c62[:], [[2, 8]], 496, ["c62"], 8, **fl)
+    iota(T.duP[:], [[0, 16], [1, 8]], 0, ["duP"], 128, -1, **fl)
+    iota(T.duX[:], [[1, 8], [0, 16]], 0, ["duX"], 128, -1, **fl)
     iota(T.colc[:], [[1, 256]], 0, ["colc"], 256, **fl)
-    iota(T.io4[:, 16:32], [[-2, 16]], 31, ["io4b"], 16, **fl)
-    iota(T.io4[:, 32:48], [[32, 8], [0, 2]], 31, ["io4c"], 16, **fl)
-    iota(T.c62[:], [[64, 8]], 62, ["c62"], 8, **fl)
-
-    fill(T.PW[:], 0.0, ["PW"], 2072)
-    fill(T.thi[:], 0, ["thi"])
-    dma("a", T.thi[0:128:16, :], T.th[:], 128, W=["thi"])
-    copy("px", T.phi[:], T.pxi[:], ["pxi"], ["phi"], c=256)
-    tt("px", T.plo[:], T.pxi[:], T.phi[:], A.subtract, ["pxi", "phi"], ["plo"], c=512)
-    dma("s", T.PW[0:128:16, PO:PO + 4096], T.phi[:], 65536, ["phi", "PW"], ["PWa"])
-    dma("a", T.PW[1:128:16, PO:PO + 4096], T.plo[:], 65536, ["plo", "PW"], ["PWb"])
-    dma("s", T.X[:, xs:4096], T.x[:, xs:4096], 256 * (4096 - xs), ["plo"], ["Xb"])
+    iota(T.e1[:], [[1, 8], [8, 32]], 0, ["e1"], 256, **fl)
+    for k in range(4):
+        iota(OF(k, 256, OW), [[0, 8]], 6000, [("OF1", k)], 8, **fl)
+    iota(T.X[:, 4096:XW], [[0, 16]], 0, ["Xc"], 16, **fl)
+    iota(T.d0x[:], [[0, 256]], -(1 << 23), ["d0x"], 256, **fl)
+    iota(T.d0n[:], [[0, 256]], 16, ["d0n"], 256, **fl)
+    iota(T.hf[:, 256:264], [[0, 8]], 0, ["hf1"], 8, **fl)
+    iota(T.ones[:], [[0, 256]], 1, ["ones"], 256, **fl)
+    iota(T.thf[:], [[0, 4]], 0, ["thf"], 4, **fl)
+    iota(T.acol[:, 4:5], [[0, 1]], int(CM0), ["ac1"], 1, **fl)
     p0 = T.ip[:, 0:1]
     ts("c", T.ib[:, 0:1], p0, 15, None, A.bitwise_and, None, ["ip"], ["ib0"])
     ts("c", T.ib[:, 1:2], p0, 7, None, A.bitwise_and, None, ["ip"], ["ib1"])
-    ts("c", T.ib[:, 2:3], p0, 3, 1, A.arith_shift_right, A.bitwise_and, ["ip"], ["ib2"])
+    ts("c", T.ib[:, 2:3], p0, 3, None, A.arith_shift_right, None, ["ip"], ["ib2"])
     copy("c", col(C_P), p0, ["ip"], ["cP"])
     copy("c", col(C_R), T.ib[:, 0:1], ["ib0"], ["cR"])
     copy("c", col(C_E), T.ib[:, 2:3], ["ib2"], ["cE"])
-    ts("c", col(C_PI), T.ib[:, 0:1], -8.0, None, A.mult, None, ["ib0"], ["cPI"])
-    ts("c", L_IN, T.io4[:, 0:16], col(C_PI), None, A.add, None, ["io4a", "cPI"], ["L_IN"])
+    copy("c", col(C_R8), T.ib[:, 1:2], ["ib1"], ["cR8"])
     tt("c", col(C_G), p0, T.ib[:, 0:1], A.subtract, ["ip", "ib0"], ["cG"])
-    ts("in", T.OO[:, 0:256], T.oli[:, 0:256].indirect(L_IN), float(PO), None, A.add, None, ["oli", "L_IN"], [("OO", 0)], c=256, k="g")
-    for k in range(4):
-        copy("in", T.O16[:, 64 * k:64 * k + 64], T.OO[:, k:256:4], [("OO", 0)], [("O16p", k)])
-        iota(T.OO[:, k * OW + 256:k * OW + 264], [[0, 8]], 6000, [("OF1", k)], 8, **fl)
-    copy("in", Tof(T.ZTo, 0), T.tli[:, 0:256].indirect(L_IN), ["tli", "L_IN"], [("T", 0)], c=256, k="g")
-    copy("in", Nof(T.NSo, 0), T.nli[:, 0:256].indirect(L_IN), ["nli", "L_IN"], [("N", 0)], c=256, k="g")
-    iota(T.X[:, 4096:XW], [[0, 16]], 0, ["Xc"], 16, **fl)
-    m128 = T.io1[:, 15:143]
     ts("c", col(C_LT2), T.ib[:, 0:1], 2.0, None, A.is_lt, None, ["ib0"], ["cLT2"])
-    ts("c", T.Ey[:], T.io1[:], col(C_G), -512.0, A.is_equal, A.mult, ["io1", "cG"], ["Ey"], c=144)
-    ts("c", T.Ep[:], T.io1[:], col(C_G), col(C_LT2), A.is_equal, A.mult, ["io1", "cG", "cLT2"], ["Ep"], c=144)
-    ts("c", T.Ib[:], m128, col(C_P), None, A.is_equal, None, ["io1", "cP"], ["Ib"], c=128)
-    ts("c", L_B8, T.io4[:, 56:60], col(C_E), None, A.add, None, ["io4e", "cE"], ["L_B8"])
+    ts("c", T.LB[:], T.io1[:, 0:16], 0.0, col(C_R8), A.mult, A.add, ["io1", "cR8"], ["LB"])
+    ts("c", T.E1f[:], T.io1[:], col(C_G), None, A.is_equal, None, ["io1", "cG"], ["E1f"], c=144)
+    ts("c", T.If[:], T.io1[:, 15:143], col(C_P), None, A.is_equal, None, ["io1", "cP"], ["If"], c=128)
     ts("c", T.BD[:], T.io2[:], col(C_G), None, A.is_equal, None, ["io2", "cG"], ["BD"], c=128)
-    copy("c", T.thf[:], T.thi[:], ["thi"], ["thf"])
-    mm("c", T.b7[:, 0:4], "pth", "b7", T.BD[:], T.thf[:], ["BD", "thf"], True, True, 256)
-    act("c", T.If[:], T.Ib[:], F.Copy, ["Ib"], ["If"], c=128)
-    act("c", T.nI8[:], T.Ib[:], F.Identity, ["Ib"], ["nI8"], c=128, scale=-8192.0)
-    act("c", T.E2[:], T.Ey[:], F.Identity, ["Ey"], ["E2"], c=144, scale=-2.0)
-    act("c2", T.nIf[:], T.Ib[:], F.Identity, ["Ib"], ["nIf"], c=128, scale=-1.0)
-    act("c2", T.I99[:], T.Ib[:], F.Identity, ["Ib"], ["I99"], c=128, scale=99.0)
-    act("c2", T.E1f[:], T.Ey[:], F.Identity, ["Ey"], ["E1f"], c=144, scale=-1.0 / 512)
+    ts("c", T.DM[:], T.io3[:], col(C_R), None, A.is_equal, None, ["io3", "cR"], ["DM"], c=128)
+    ts("c", T.LM[:], T.io3[:], col(C_R), 8192.0, A.is_ge, A.mult, ["io3", "cR"], ["LM"], c=128)
+    tt("c", T.A01[:], T.E1f[:, 15:143], T.E1f[:, 14:142], A.subtract, ["E1f"], ["A01"], c=256)
+    copy("c", T.I16[:, 0:128], T.If[:], ["If"], ["I16"], c=128)
+    ts("c", T.I16[:, 128:256], T.If[:], -512.0, None, A.mult, None, ["If"], ["J16"], c=128)
+    ts("c", T.Rep[0:8, :], T.duP[0:8, :], 0.0, None, A.is_equal, None, ["duP"], ["Rep"], c=128)
+    plus("c", T.thf[0:8, :], T.thi[0:8, :], -H, ["thi"], ["thf"])
     for s in range(S):
-        act("c2", T.sI[:, 128 * s:128 * s + 128], T.Ib[:], F.Identity, ["Ib"], [("sI", s)], c=128, scale=float(s + 2))
-    act("c2", T.thS[:], T.b7[:, 0:4], F.Identity, ["pth"], ["thS"], ["b7"], c=64, scale=512.0, bias=256.0 - 2048 * 512)
-    act("c2", T.thA[:], T.b7[:, 0:4], F.Identity, ["pth"], ["thA"], ["b7"], c=64, scale=256.0, bias=256.0 * (1 - 2048) + (1 << 20))
-    act("c2", T.thB[:], T.b7[:, 0:4], F.Identity, ["pth"], ["thB"], ["b7"], c=64, scale=256.0, bias=256.0 * (1 - 2048) - (1 << 20))
-    act("c2", col(C_DX), col(C_R), F.Identity, ["cR"], ["cDX"], c=64, bias=4096.0)
-    act("c2", col(C_DP), col(C_R), F.Identity, ["cR"], ["cDP"], c=64, bias=4096.0 + PO)
-    act("c2", T.sg1[:], T.io3[:], F.Sign, ["io3"], ["sg1"], c=128, scale=-1.0, bias=15.0)
-    act("c2", T.sg2[:], T.io3[:], F.Sign, ["io3"], ["sg2"], c=128)
-    act("c2", T.sg2[:, 15:128:16], T.c62[:], F.Identity, ["c62"], ["sg2"], c=64, scale=0.0, bias=8192.0)
-    iota(T.d0x[:], [[0, 256]], 1 << 23, ["d0x"], 256, **fl)
-    iota(T.d0n[:], [[0, 256]], 2, ["d0n"], 256, **fl)
-    act("c2", T.d0n[:, 0:256:32], T.c62[:], F.Identity, ["c62"], ["d0n"], c=64, scale=0.0, bias=BIG)
-    iota(T.hf[:, 256:264], [[0, 8]], 0, ["hf1"], 8, **fl)
-    ts("c2", T.DM[:], T.io3[:], col(C_R), None, A.is_equal, None, ["io3", "cR"], ["DM"], c=128)
-    ts("c2", T.LM[:], T.io3[:], col(C_R), 8192.0, A.is_ge, A.mult, ["io3", "cR"], ["LM"], c=128)
-    tt("c2", T.A01[:], T.E1f[:, 15:143], T.E1f[:, 14:142], A.subtract, ["E1f"], ["A01"], c=256)
-    ts("c2", col(C_R7), T.ib[:, 1:2], 32.0, col(C_E), A.mult, A.subtract, ["ib1", "cE"], ["cR7"])
-    copy("c2", L_B32, T.io4[:, 32:48], ["io4c"], ["L_B"])
-    ts("c2", L_OUT, T.io4[:, 16:32], col(C_R7), None, A.add, None, ["io4b", "cR7"], ["L_OUT"])
+        ts("c", T.KL[0:32, 128 * s:128 * s + 128], T.duX[0:32, :], 0.0, T.thf[0:32, s:s + 1], A.is_equal, A.mult, ["duX", "thf"], [("KL", s)], c=128)
+    for h in range(2):
+        copy("c", T.KL[32:33, 256 * h:256 * h + 256], T.ones[32:33, :], ["ones"], [("KL1", h)], c=128)
+    ts("c", T.KR[0:32, :], T.ones[0:32, :], 512.0, None, A.mult, None, ["ones"], ["KR"], c=128)
+    copy("c", T.KR[32:33, :], T.e1[32:33, :], ["e1"], ["KR1"], c=256)
+    act("c", col(C_T), col(C_R8), F.Identity, ["cR8", "cE"], ["cT"], c=64, scale=32.0, bias=col(C_E))
+    for k, (c0, c1) in chunks("y3"):
+        ts("c", T.Pm[:, 256 * k:256 * k + 256], T.colc[:], -float(c0 // 8), col(C_T), A.add, A.is_equal, ["colc", "cT"], [("Pm0", k)], c=128)
+        ts("c", T.Pm[:, 256 * k:256 * k + 256], T.Pm[:, 256 * k:256 * k + 256], -512.0, None, A.mult, None, [("Pm0", k)], [("Pm", k)], c=128)
+    for j, x in enumerate((1.0, -1.0, 2.0, col(C_LT2))):
+        act("c", T.Eg[:, 8 * j:8 * j + 8], T.BD[:, 0:128:16], F.Identity, ["BD", "cLT2"], ["Eg"], c=64, scale=x)
+        if j:
+            act("c", T.Es[:, 144 * j:144 * j + 144], T.E1f[:], F.Identity, ["E1f", "cLT2"], ["Es"], c=144, scale=x)
+    for name in IS:
+        act("c", Id(name), T.If[:], F.Identity, ["If"], [name], c=128, scale=IS[name])
+    act("c", col(C_DX), col(C_R), F.Identity, ["cR"], ["cDX"], c=64, bias=4096.0)
+    act("c", col(C_DP), col(C_R), F.Identity, ["cR"], ["cDP"], c=64, bias=4096.0 + PO)
+    act("c", T.sg1[:], T.io3[:], F.Sign, ["io3"], ["sg1"], c=128, scale=-1.0, bias=15.0)
+    act("c", T.sg2[:], T.io3[:], F.Sign, ["io3"], ["sg2"], c=128)
+    act("c", T.sg2[:, 15:128:16], T.c62[:], F.Identity, ["c62"], ["sg2"], c=64, scale=0.0, bias=8192.0)
+    act("c", T.d0x[:, 0:256:32], T.c62[:], F.Identity, ["c62"], ["d0x"], c=64, scale=0.0, bias=-256.0)
+    act("c", T.d0n[:, 0:256:32], T.c62[:], F.Identity, ["c62"], ["d0n"], c=64, scale=0.0, bias=-BIG)
 
-    def gather(e, tag, dst, name, win, R, lists, b0, b1):
-        copy("%s%d" % (tag, b0 // 8), dst[:, 128 * b0:128 * b1], win.indirect(lists(8 * b0, 8 * b1)), R, blocks(name, b0, b1), c=128 * (b1 - b0), k="g", e=e)
+    def gather(name, win, R, lists, l0, c0=0, c1=256):
+        def fn(e, b0, b1):
+            out, in_ = T[name][:, 128 * b0:128 * b1], win.indirect(lists[:, l0 + 8 * b0:l0 + 8 * b1])
+            return v.tensor_copy(out, in_) if e == "v" else a.activation(out, in_, F.Copy)
+        for b in range(c0 // 8, c1 // 8):
+            node("x", "%s_%d" % (name, chunk_of(name, b)), ("g", 128), fn, R(b), [(name, b)], (), (b, b + 1))
 
-    def vmax(tag, m, mn, y, yn, b0, b1):
-        c0 = b0 % 8
-        bk = sorted(set(["pt%d" % (c // 4) for c in range(c0, c0 + b1 - b0)]))
-        tt("%s%d" % (tag, b0 // 8), m[:, 128 * b0:128 * b1], y[:, 128 * b0:128 * b1], T.pt[:, c0:c0 + b1 - b0], A.max,
-           blocks(yn, b0, b1) + bk, blocks(mn, b0, b1), bk, c=128 * (b1 - b0))
+    def vmax(m, y, bk, c0=0, c1=256):
+        def fn(e, b0, b1):
+            return v.tensor_tensor(T[m][:, 128 * b0:128 * b1], T[y][:, 128 * b0:128 * b1], T[bk][:, 0:128 * (b1 - b0)], A.max)
+        for b in range(c0 // 8, c1 // 8):
+            node("v", "%s_%d" % (m, chunk_of(y, b)), ("n", 128), fn, [(y, b), bk], [(m, b)], [bk], (b, b + 1))
 
-    def tile(buf, z0, zR):
-        def half(h):
-            def fn():
-                for k in range(8):
-                    last = t.matmul(T.pt[:, 4 * h:4 * h + 4, k, :], T.Ib[:], buf[:, z0 + 64 * h:z0 + 64 * h + 64], True, True)
-                return last
-            op("t", "tile" if buf is T.ZTo else "tile3", fn, ["Ib"] + zR, ["pt%d" % h], ["pt%d" % h], 512, "pe")
-        half(0), half(1)
+    def tile(tag, bk, z, zR):
+        def fn():
+            for j in range(4):
+                last = t.matmul(T[bk][:, 128 * j:128 * j + 128], Id("I"), z, True, True)
+            return last
+        op("t", tag, fn, ["I"] + zR, [bk], [bk], 512, "pe")
 
-    def fold(tag, out, res, bk, En, name, k, start, stop):
-        mm16("%s%d" % (tag, k), out, res, bk, T[En], lambda r: T[name][:, 1024 * k + r:1024 * (k + 1):16], [En] + blocks(name, 8 * k, 8 * k + 8), start, stop)
+    def lane_sums(tag, buf, z0, zR, b, c0, res, j):
+        def fn():
+            for r in range(16):
+                last = t.matmul(T[b][0:8, c0 + r:c0 + 128:16], buf[:, z0 + r:z0 + 128:16], T.Eg[:, 0:8], True, True)
+            return last
+        op("t", tag, fn, ["Eg"] + zR, [res], [b], 256, "pe")
+        ts(tag, T.Sz[0:8, 128 * j:128 * j + 128], T[b][0:8, c0:c0 + 128], -1.0, H, A.mult, A.add, [res], [("Sz", j)], [b], c=128)
 
-    def lane_sums(o):
-        mm16("sz", T.b7[:, 8:16], "psz", "b7", T.Ey, lambda r: T.ZTo[:, o * ZT + r:o * ZT + 128:16], ["Ey", ("z", o)], True, True)
-        ts("sz", T.sz8[:], T.b7[:, 8:16], -float(1 << 20), None, A.add, None, ["psz"], ["sz8"], ["b7"])
-        copy("sz", T.NSo[:, o * NS + 256:o * NS + 320], T.sz8[:, 0:8].indirect(L_B8), ["sz8", "L_B8"], [("Sz", o)], c=64, k="g")
+    def flat(M):
+        return M in CFG["flat"]
 
-    def chooser(Nap, NR, names):
-        pq = T.b6[:, 256:512]
-        mm("q", pq, "pQ", "b6", T.If[:], Nap, ["If"] + NR, True, False, 1024)
-        for i, nm in enumerate(names):
-            mm("q", pq, "pQ", "b6", T.nI8[:], T[nm][:], ["nI8", nm], False, i == len(names) - 1, 256)
-        ts("sel", T.sel[:], pq, 0.0, None, A.is_ge, None, ["pQ"], ["sel"], ["b6"], c=256)
-        copy("Qs", T.Qs[:], pq, ["pQ"], ["Qs"], ["b6"], c=256, e=CFG["eng"]["Qs"])
+    def form(buf, k, M):
+        return buf[:, 128 * k:128 * k + M] if flat(M) else buf[0:M, 128 * k:128 * k + 128]
+
+    def put(tag, out, res, bk, M, x, ident, R, start, stop):
+        if flat(M):
+            mm(tag, out, res, bk, ident, x, R, start, stop, max(64, M))
+        else:
+            mm(tag, out, res, bk, x, ident, R, start, stop, 128)
+
+    def fold(tag, bk, j, name, c0, c1, is_flat, stop):
+        def fn():
+            for r in range(16):
+                x = T[name][:, 16 * c0 + r:16 * c1:16]
+                if is_flat:
+                    last = t.matmul(T[bk][:, 0:c1 - c0], T.Es[:, 144 * j + 15 - r:144 * j + 143 - r], x, False, stop and r == 15)
+                else:
+                    last = t.matmul(T[bk][0:c1 - c0, r:128:16], x, T.Eg[:, 8 * j:8 * j + 8], False, stop and r == 15)
+            return last
+        op("t", tag, fn, ["Eg", "Es"] + blocks(name, c0 // 8, c1 // 8), [("F", bk)], [bk], 16 * (max(64, c1 - c0) if is_flat else min(64, c1 - c0)), "pe")
+
+    def distances(tags, k, c0, c1, y, m, j, out):
+        bk, M = "b%d" % (2 + cnt["F"] % 2), c1 - c0
+        cnt["F"] += 1
+        mm(tags[0], T[bk][0:M, 0:128], ("F", bk), bk, T.Rep[0:8, 0:M], T.Sz[0:8, 128 * j:128 * j + 128], ["Rep", ("Sz", j)], True, False, 128)
+        fold(tags[1] + str(k), bk, 1, y, c0, c1, False, False)
+        fold(tags[2] + str(k), bk, 2, m, c0, c1, False, True)
+        plus(tags[3] + str(k), T[out][0:M, 128 * k:128 * k + 128], T[bk][0:M, 0:128], -2 * H, [("F", bk)], [(out, k)], [bk], c=128)
+
+    def turn(tag, out, res, bk, src, k, M, rhs, R, start, stop, c):
+        mm(tag, out, res, bk, T[src][0:M, 128 * k:128 * k + 128], rhs, [(src, k)] + R, start, stop, max(64, c))
+
+    def chooser(o, buf, NR):
+        c = 8192 * (o + 0.5)
+        if o == 0:
+            act("s3", T.s3[:], Tof(T.ZTo, 0), F.Relu, [("T", 0)], ["s3"], scale=-8192.0, bias=c)
+        else:
+            act("s3", T.s3[:], pq, F.Relu, ["pQ"], ["s3"], ["b6"], scale=-8192.0, bias=c - 8192.0 * 64)
+        for k, (c0, c1) in chunks("gp"):
+            M = c1 - c0
+            out, res = form(T.b7, k, M), "pa" if k < 2 else "pb"
+            put("qn", out, res, "b7", M, Nof(buf, max(o - 1, 0), c0, c1), T.I16[:, 0:128], NR + ["I16"], True, False)
+            if o == 0:
+                put("q2", out, res, "b7", M, Tof(T.ZTo, 0, c0, c1), Id("n13"), [("T", 0), "n13"], False, False)
+            else:
+                put("q2", out, res, "b7", M, T.Tr[:, c0:c1], Id("p13"), ["Tr", "p13"], False, False)
+            put("q2", out, res, "b7", M, T.s3[:, c0:c1], Id("nI"), ["s3", "nI"], False, True)
+            affine("Qs", form(T.Qs, k, M), out, 1.0, c - (8192.0 * 99 if o else 0.0), [res], [("Qs", k)], ["b7"], c=M if flat(M) else 128)
 
     def part1(o):
-        for k in range(4):
-            act("OC", OC(o, 64 * k, 64 * k + 64), T.OO[:, o * OW + k:o * OW + 256:4], F.Identity, OOR(o), [("OC", o, k)], c=64, scale=1.0 / 512)
-        act("cm", T.b6[:, 256:512], OC(o), F.Identity, [("OC", o, k) for k in range(4)] + ["ac1"], ["pQ"], ["b6"], bias=T.acol[:, 4:5], scale=3232.0 * 512)
-        for e, b0, b1 in CFG["gp0" if o == 0 else "gp"]:
-            gather(e, "GP", T.gp, "gp", Pw, PR + O16R(o), lambda x0, x1: T.O16[:, 256 * o + x0:256 * o + x1], b0, b1)
-        for k in range(4):
-            bk, c0, c1 = "b2" if k % 2 == 0 else "b3", 64 * k, 64 * k + 64
-            mm("po", T[bk][:, 0:64], ("po", k % 2), bk, T.nI8[:], T.sel[:, k:256:4], ["nI8", "sel"], True, False, 64)
-            fold("po", T[bk][:, 0:64], ("po", k % 2), bk, "Ep", "gp", k, False, True)
-            tt("R%d" % k, T.Rf[:, c0:c1], T[bk][:, 0:64], T.Qs[:, k:256:4], A.max, [("po", k % 2), "Qs"], [("Rf", k)], [bk])
-            copy("R%d" % k, T.R16[:, c0:c1], T.Rf[:, c0:c1], [("Rf", k)], [("R16", k)])
-        for e, b0, b1 in CFG["y10" if o == 0 else "y1"]:
-            gather(e, "y1_", T.y1, "y1", Xw, XR + [("R16", b0 // 8)], lambda x0, x1: T.R16[:, x0:x1], b0, b1)
-        for b0, b1 in CFG["m1"]:
-            vmax("m1_", T.m1, "m1", T.y1, "y1", b0, b1)
-        for k in range(4):
-            bk, c0, c1 = "b0" if k % 2 == 0 else "b1", 64 * k, 64 * k + 64
-            pu, res = T[bk][:, 256:320], ("u", k % 2)
-            fold("uy", pu, res, bk, "Ey", "y1", k, True, False)
-            mm("us", pu, res, bk, T.If[:], T.NSo[:, o * NS + 256:o * NS + 320], ["If", ("Sz", o)], False, False, 256)
-            fold("um", pu, res, bk, "E2", "m1", k, False, True)
-            tt("h%d" % k, T.tf[:, c0:c1], pu, OC(o, c0, c1), A.mult, [res, ("OC", o, k)], [("tf", k)], [bk])
-            tt("h%d" % k, T.vi[:, c0:c1], T.tf[:, c0:c1], T.b6[:, 256 + c0:256 + c1], A.add, [("tf", k), "pQ"], [("vi", k)], ["b6"])
-            ts("h%d" % k, T.hi[:, c0:c1], T.vi[:, c0:c1], 5, 4095, A.arith_shift_right, A.bitwise_and, [("vi", k)], [("hi", k)])
-            copy("h%d" % k, T.Ho[:, 256 * o + c0:256 * o + c1], T.hi[:, c0:c1], [("hi", k)], [("Ho", o, k)])
-            send(T.Hi[:, 256 * o + c0:256 * o + c1], T.Ho[:, 256 * o + c0:256 * o + c1], "h%d" % (4 * o + k), 16384, [("Ho", o, k)], ("Hi", o, k))
+        act("cm", T.b6[:, 256:512], OF(o), F.Identity, [("OO", o), "ac1"], ["cm"], ["b6"], bias=T.acol[:, 4:5], scale=3232.0)
+        for x in CFG["seq"].split():
+            (roads if x[0] == "p" else hashes)(o, int(x[1]))
+
+    def roads(o, k):
+        c0, c1 = CFG["gp"][k:k + 2]
+        gather("gp", Pw, lambda b: PR + [("O16", o)], T.O16, 256 * o, c0, c1)
+        bk, M = "b%d" % (2 + cnt["F"] % 2), c1 - c0
+        cnt["F"] += 1
+        put("po", form(T[bk], 0, M), ("F", bk), bk, M, T.s3[:, c0:c1], Id("nI"), ["s3", "nI"], True, False)
+        fold("po%d" % k, bk, 3, "gp", c0, c1, flat(M), True)
+        if flat(M):
+            tt("R%d" % k, T.tf[:, c0:c1], T[bk][:, 0:M], form(T.Qs, k, M), A.max, [("F", bk), ("Qs", k)], blocks("tf", c0 // 8, c1 // 8), [bk], c=M)
+            plus("R%d" % k, T.R16[:, c0:c1], T.tf[:, c0:c1], H, blocks("tf", c0 // 8, c1 // 8), [("R16", k)], c=M)
+        else:
+            tt("R%d" % k, T.Rf[0:M, 128 * k:128 * k + 128], T[bk][0:M, 0:128], T.Qs[0:M, 128 * k:128 * k + 128], A.max, [("F", bk), ("Qs", k)], [("Rf", k)], [bk], c=128)
+            turn("R%d" % k, T.b1[:, c0:c1], ("pR", k), "b1", "Rf", k, M, T.I16[0:M, 0:M], ["I16"], True, True, M)
+            plus("R%d" % k, T.R16[:, c0:c1], T.b1[:, c0:c1], H, [("pR", k)], [("R16", k)], ["b1"], c=M)
+
+    def hashes(o, k):
+        c0, c1 = CFG["y1"][k:k + 2]
+        gather("y1", Xw, lambda b: XR + [("R16", chunk_of("gp", b))], T.R16, 0, c0, c1)
+        vmax("m1", "y1", "pt", c0, c1)
+        M, tf = c1 - c0, blocks("tf", c0 // 8, c1 // 8)
+        if flat(M):
+            bk = "b%d" % (2 + cnt["F"] % 2)
+            cnt["F"] += 1
+            pu, res = T[bk][:, 0:M], ("F", bk)
+            mm("us", pu, res, bk, T.Sz[0:8, 0:128], T.Rep[0:8, 0:M], ["Rep", ("Sz", 0)], True, False, 64)
+            add("us", pu, res, bk, "n12", T.ones[:, 0:M], ["ones"], False, False, 64)
+            fold("uy%d" % k, bk, 1, "y1", c0, c1, True, False)
+            fold("um%d" % k, bk, 2, "m1", c0, c1, True, True)
+        else:
+            bk, pu, res = "b0", T.b0[:, 256 + c0:256 + c1], ("pu", k)
+            distances(("us", "uy", "um", "h"), k, c0, c1, "y1", "m1", 0, "uf")
+            turn("h%d" % k, pu, res, bk, "uf", k, M, T.I16[0:M, 0:M], ["I16"], True, True, M)
+        tt("h%d" % k, T.tf[:, c0:c1], pu, OF(o, c0, c1), A.mult, [res, ("OO", o)], tf, [bk], c=M)
+        tt("h%d" % k, T.vi[:, c0:c1], T.tf[:, c0:c1], T.b6[:, 256 + c0:256 + c1], A.add, tf + ["cm"], [("vi", k)], ["b6"], c=M)
+        ts("h%d" % k, T.hi[:, c0:c1], T.vi[:, c0:c1], 5, 4095, A.arith_shift_right, A.bitwise_and, [("vi", k)], [("hi", k)], c=M)
+        copy("h%d" % k, Nof(T.Ho, o, c0, c1), T.hi[:, c0:c1], [("hi", k)], [("Ho", k)], c=M)
+        send(Nof(T.Hi, o, c0, c1), Nof(T.Ho, o, c0, c1), "h%d" % (4 * o + k), 256 * M, [("Ho", k)], ("Hi", o, k))
 
     def send_state(o):
-        z0, s0 = o * ZT, o * NS + 256
-        send2([(T.ZTi[:, z0:z0 + 128], T.ZTo[:, z0:z0 + 128]), (T.NSi[:, s0:s0 + 64], T.NSo[:, s0:s0 + 64])], "z%d" % o, 65536,
-              [("z", o), ("Sz", o)], [("Zi", o), ("Si", o)])
+        z0 = o * ZT
+        send(T.ZTi[:, z0:z0 + 128], T.ZTo[:, z0:z0 + 128], "z%d" % o, 32768, [("z", o)], ("Zi", o))
         if o < S - 1:
-            send(OF(o + 1, 256), OF(o, 256), "o%d" % o, 131072, OOR(o) + [("Hi", o - 1, 3)], ("OO", o + 1))
+            after = [("Hi", o - 1, LAST[1]) if o else LAST]
+            send(OF(o + 1), OF(o), "o%d" % o, 131072, [("OO", o)] + after, ("OO", o + 1))
+            send(Nof(T.O16, o + 1), Nof(T.O16, o), "l%d" % o, 65536, [("O16", o)] + after, ("O16", o + 1))
 
     def send_rest(o):
-        after = [("Ho", o, 3)] if o else []
-        if o < S - 1:
-            send2([(Tof(T.ZTi, o), Tof(T.ZTo, o)), (T.O16[:, (o + 1) * 256:(o + 2) * 256], T.O16[:, o * 256:(o + 1) * 256])], "t%d" % o, 131072,
-                  [("T", o)] + O16R(o) + after, [("Ti", o), ("O16", o + 1)])
-        else:
-            send(Tof(T.ZTi, o), Tof(T.ZTo, o), "t%d" % o, 65536, [("T", o)] + after, ("Ti", o))
-        send(Nof(T.NSi, o), Nof(T.NSo, o), "n%d" % o, 131072, [("N", o)] + after, ("Ni", o))
+        after = {x: [LAST] if CFG["after"][x] >= 0 else [] if o else ["Xb"] for x in "tn"}
+        send(Tof(T.ZTi, o), Tof(T.ZTo, o), "t%d" % o, 65536, [("T", o)] + after["t"], ("Ti", o))
+        send(Nof(T.Ni, o), Nof(T.No, o), "n%d" % o, 65536, [("N", o)] + after["n"], ("Ni", o))
 
     def part3(s):
-        tile(T.ZTi, s * ZT, [("Zi", s)])
-        for e, b0, b1 in CFG["y3"]:
-            gather(e, "y3_", T.y3, "y3", Xw, XR + [("Hi", s, b0 // 8)], lambda x0, x1: T.Hi[:, 256 * s + x0:256 * s + x1], b0, b1)
-        for b0, b1 in CFG["m3"]:
-            vmax("m3_", T.m3, "m3", T.y3, "y3", b0, b1)
-        for k in range(4):
-            out = T.b0[:, k:256:4]
-            mm("kc", out, "K", "b0", T.Ib[:], T.colc[:, k:256:4], ["Ib", "colc"], True, False, 64)
-            mm("ks", out, "K", "b0", T.If[:], T.NSi[:, s * NS + 256:s * NS + 320], ["If", ("Si", s)], False, False, 256)
-            fold("ky", out, "K", "b0", "Ey", "y3", k, False, False)
-            fold("km", out, "K", "b0", "E2", "m3", k, False, True)
-            copy("hf", T.hf[:, k:256:4], T.Hi[:, 256 * s + 64 * k:256 * s + 64 * k + 64], [("Hi", s, k)], [("hf", k)])
-        Tin = Tof(T.ZTi, s)
-        act("thE", T.d0x[:, 0:256:32], T.c62[:], F.Identity, ["c62", "thS"], ["d0x"], c=64, bias=T.thS[:, s:s + 1], scale=0.0)
-        act("thE", T.ta[:], Tin, F.Abs, [("Ti", s)], ["ta"], bias=-(s + 99) / 2.0)
-        act("thE", T.tb[:], T.ta[:], F.Sign, ["ta"], ["tb"], bias=-(98 - s) / 2.0)
-        act("thE", T.thE[:], T.tb[:], F.Identity, ["tb", "thA", "thB"], ["thE"], bias=T.thB[:, s:s + 1], scale=T.thA[:, s:s + 1])
-        if s < S - 1:
-            act("tgt", T.tgt[:], Tin, F.Relu, [("Ti", s)], ["tgt"], bias=-float(s + 1))
-
-    def first_of_block(x, ps, res, Mk, key, eq, du, t8, off, dummy, dR):
-        mm("lm" + x, ps, res, "b1", T.Ib[:], T.LM[:], ["Ib", "LM"], True, False, 128)
-        mm("row" + x, ps, res, "b1", T.BD[:], T[Mk][:], ["BD", Mk], False, True, 512)
-        scan("key" + x, T[key][:, ::-1], T.sg1[:, ::-1], T[Mk][:, ::-1], 0.0, A.mult, A.add, ["sg1", Mk], [key])
-        tt("eq" + x, T[eq][:], ps, T[key][:], A.is_equal, [res, key], [eq], ["b1"], c=128)
-        scan("du" + x, T[du][:], T.sg2[:], T[eq][:], 0.0, A.mult, A.add, ["sg2", eq], [du])
-        tt("off" + x, T[t8][:], T[du][:, 15:128:16], T[key][:, 0:128:16], A.add, [du, key], [t8])
-        ts("off" + x, T[off][:, 0:16:2], T[t8][:], dummy, None, A.min, None, [t8, dR], [off])
-
-    def refuse(s):
-        o = (s + 1) % S
-        scan("scM", T.scM[:], T.d0x[:], K, T.thS[:, s:s + 1], A.min, A.max, ["d0x", "K", "thS"], ["scM"], ["b0"], c=256)
-        act("Ksb", T.Ksb[:], K, F.Copy, ["K"], ["Ksb"], ["b0"])
+        z0 = s * ZT
+        tile("zt3", "pu", T.ZTi[:, z0:z0 + 128], [("Zi", s)])
+        lane_sums("szk", T.ZTi, z0, [("Zi", s)], "b6", 0, "pQ", 1)
+        gather("y3", Xw, lambda b: XR + [("Hi", s, chunk_of("y1", b))], T.Hi, 256 * s)
+        vmax("m3", "y3", "pu")
+        KL = [("KL", s), ("KL1", s // 2), "KR", "KR1"]
+        mm("ks", K1, "K1", "b0", T.KL[0:33, 128 * s:128 * s + 128], T.KR[0:33, :], KL, True, False, 256)
+        mm("ks", K2, "K2", "b1", T.KL[0:8, 128 * s:128 * s + 128], T.KR[0:8, :], KL, True, False, 256)
+        for k, (c0, c1) in chunks("y1"):
+            plus("hf", T.hf[:, c0:c1], Nof(T.Hi, s, c0, c1), -H, [("Hi", s, k)], [("hf", k)], c=c1 - c0)
+        act("e", T.e1[:], Tof(T.ZTi, s), F.Abs, [("Ti", s)], ["e1"], bias=-(s + 99) / 2.0)
+        act("e", T.e2[:], T.e1[:], F.Relu, ["e1"], ["e2"], scale=-float(1 << 22), bias=(98 - s) * float(1 << 21))
+        add("ke", K2, "K2", "b1", "nI", T.e2[:], ["e2"], False, False)
+        add("q", pq, "pQ", "b6", "I", Tof(T.ZTi, s), [("Ti", s)], True, False)
+        for k, (c0, c1) in chunks("y3"):
+            M = c1 - c0
+            distances(("ks", "ky", "km", "K"), k, c0, c1, "y3", "m3", 1, "Kf")
+            turn("K%d" % k, K1, "K1", "b0", "Kf", k, M, T.Pm[0:M, 256 * k:256 * k + 256], [("Pm", k)], False, c1 == 256, 256)
+            turn("k2", T.b1[:, 256 + c0:256 + c1], "K2", "b1", "Kf", k, M, T.I16[0:M, 128:128 + M], ["J16"], False, c1 == 256, M)
+        cnt["ph"] += 1
+        scan("scM", T.scM[:], T.d0x[:], K1, -256.0, A.max, A.min, ["d0x", "K1"], ["scM"], ["b0"], c=256)
+        scan("scN", T.scN[:], T.d0n[:], K1, 0.0, A.add, A.max, ["d0n", "K1"], ["scN"], ["b0"], c=256)
         copy("p", T.pi1[:], T.scM[:, 31:256:32], ["scM"], ["pi1"])
         ts("p", T.pi2[:], T.pi1[:], 511, None, A.bitwise_and, None, ["pi1"], ["pi2"])
-        copy("p", T.cj[:], T.pi2[:], ["pi2"], ["cj"])
-        tt("MkO", T.MkO[:], OF(o).indirect(T.cj[:, 0:8]), T.DM[:], A.mult, OOR(o) + [("OF1", o), "cj", "DM"], ["MkO"], c=128, k="g")
+        copy("p", T.cj[:, 0:8], T.pi2[:], ["pi2"], ["cj"])
+        tt("x", T.xi1[:], T.c62[:], T.scN[:, 31:256:32], A.subtract, ["c62", "scN"], ["xi1"])
+        ts("x", T.xi2[:], T.xi1[:], 511, None, A.bitwise_and, None, ["xi1"], ["xi2"])
+        copy("x", T.cj[:, 8:16], T.xi2[:], ["xi2"], ["cb"])
         tt("Mkh", T.Mkh[:], T.hf[:, 0:264].indirect(T.cj[:, 0:8]), T.DM[:], A.mult, HF + ["cj", "DM"], ["Mkh"], c=128, k="g")
-        act("Mkhb", T.Mkhb[:], T.Mkh[:], F.Copy, ["Mkh"], ["Mkhb"], c=128)
-        mm("val", T.b2[:, 64:192], "pv", "b2", T.E1f[:, 14:142], T.Mkh[:], ["E1f", "Mkh"], True, False, 512)
-        mm("val", T.b2[:, 64:192], "pv", "b2", T.A01[:], T.Mkhb[:], ["A01", "Mkhb"], False, True, 128)
-        act("val", T.val[:], T.b2[:, 64:192], F.Copy, ["pv"], ["val"], ["b2"], c=128)
-        first_of_block("P", T.b1[:, 0:128], "rowO", "MkO", "kO", "eqO", "duO", "pt8", "offP", col(C_DP), "cDP")
+        tt("MkX", T.MkX[:], T.hf[:, 0:264].indirect(T.cj[:, 8:16]), T.DM[:], A.mult, HF + ["cb", "DM"], ["MkX"], c=128, k="g")
+
+    def first_of_block(x, bk, shift, dummy, dR):
+        Mk, key, eq, du, t8 = [T[y + x] for y in ("Mk", "key", "eq", "du", "t8")]
+        ps, res = T[bk][:, 128:256], "row" + x
+        add("lm" + x, ps, res, bk, "I", T.LM[:], ["LM"], True, False, 128)
+        mm("row" + x, ps, res, bk, T.BD[:], Mk[:], ["BD", "Mk" + x], False, True, 512)
+        scan("key" + x, key[:, ::-1], T.sg1[:, ::-1], Mk[:, ::-1], 0.0, A.mult, A.add, ["sg1", "Mk" + x], ["key" + x])
+        tt("eq" + x, eq[:], ps, key[:], A.is_equal, [res, "key" + x], ["eq" + x], [bk], c=128)
+        scan("du" + x, du[:], T.sg2[:], eq[:], 0.0, A.mult, A.add, ["sg2", "eq" + x], ["du" + x])
+        tt("off" + x, t8[:], du[:, 15:128:16], key[:, 0:128:16], A.add, ["du" + x, "key" + x], ["t8" + x])
+        ts("off" + x, T["off" + x][:, 0:16:2], t8[:], shift, dummy, A.add, A.min, ["t8" + x, dR], ["off" + x])
+
+    def refuse(s):
+        o, pv = (s + 1) % S, T.b2[:, 256:384]
+        tt("MkP", T.MkP[:], OF(o, 0, OW).indirect(T.cj[:, 0:8]), T.DM[:], A.mult, [("OO", o), ("OF1", o), "cj", "DM"], ["MkP"], c=128, k="g")
+        first_of_block("P", "b2", 0.0, col(C_DP), "cDP")
+        act("val", T.Mkhb[:], T.Mkh[:], F.Copy, ["Mkh"], ["Mkhb"], c=128)
+        mm("val", pv, "pv", "b2", T.E1f[:, 14:142], T.Mkh[:], ["E1f", "Mkh"], True, False, 512)
+        mm("val", pv, "pv", "b2", T.A01[:], T.Mkhb[:], ["A01", "Mkhb"], False, True, 128)
+        act("val", T.val[:], pv, F.Copy, ["pv"], ["val"], ["b2"], c=128)
         for c in range(7, -1, -1):
             copy("scatP", Pw.indirect(T.offP[:, 2 * c:2 * c + 1]), T.val[:, 16 * c:16 * c + 16], ["offP", "val"], PR, c=16, k="s")
 
     def learn(s):
         z1 = (s + 1) * ZT
-        scan("scN", T.scN[:], T.d0n[:], K, 0.0, A.add, A.min, ["d0n", "K"], ["scN"], ["b0"], c=256)
-        tt("x", T.xi1[:], T.c62[:], T.scN[:, 31:256:32], A.subtract, ["c62", "scN"], ["xi1"])
-        ts("x", T.xi2[:], T.xi1[:], 511, None, A.bitwise_and, None, ["xi1"], ["xi2"])
-        copy("x", T.cb[:], T.xi2[:], ["xi2"], ["cb"])
-        tt("Mkb", T.Mkb[:], T.hf[:, 0:264].indirect(T.cb[:, 0:8]), T.DM[:], A.mult, HF + ["cb", "DM"], ["Mkb"], c=128, k="g")
-        first_of_block("X", T.b1[:, 128:256], "rowX", "Mkb", "kb", "eqb", "dub", "xt8", "offX", col(C_DX), "cDX")
-        copy("hb", T.hb[:], T.kb[:, 0:128:16], ["kb"], ["hb"])
-        tt("zs", T.zs[:], Xw.indirect(T.hb[:, 0:8]), T.ZTi[:, s * ZT:s * ZT + 128], A.add, XR + ["hb", ("Zi", s)], ["zs"], c=128, k="g")
-        ts("zi", T.zi[:], T.zs[:], 0.5, -0.25, A.mult, A.add, ["zs"], ["zi"], c=128)
-        copy("zn", T.ZTo[:, z1:z1 + 128], T.zi[:], ["zi"], [("z", s + 1)], c=128)
+        first_of_block("X", "b3", H, col(C_DX), "cDX")
+        plus("hb", T.hb[:], T.keyX[:, 0:128:16], H, ["keyX"], ["hb"])
+        zi = T.ZTi[:, s * ZT:s * ZT + 128]
+        if CFG["eng"]["z%d" % (s == S - 1)] == "v":
+            tt("zs", T.zs[:], Xw.indirect(T.hb[:, 0:8]), zi, A.add, XR + ["hb", ("Zi", s)], ["zs"], c=128, k="g")
+            ts("zi", T.zi[:], T.zs[:], 0.5, -0.25, A.mult, A.add, ["zs"], ["zi"], c=128)
+            copy("zn", T.ZTo[:, z1:z1 + 128], T.zi[:], ["zi"], [("z", s + 1)], c=128)
+        else:
+            ps = T.b3[:, 256:384]
+            add("zp", ps, "pzs", "b3", "I", zi, [("Zi", s)], True, False, 128)
+            copy("zs", T.gb[:], Xw.indirect(T.hb[:, 0:8]), XR + ["hb"], ["gb"], c=128, k="g", e="a")
+            add("zp", ps, "pzs", "b3", "I", T.gb[:], ["gb"], c=128)
+            act("zi", T.zs[:], ps, F.Identity, ["pzs"], ["zs"], ["b3"], c=128, scale=0.49999, bias=1.5 * BIG)
+            act("zn", T.ZTo[:, z1:z1 + 128], T.zs[:], F.Identity, ["zs"], [("z", s + 1)], c=128, bias=-1.5 * BIG)
         for c in range(7, -1, -1):
             copy("scatX", Xw.indirect(T.offX[:, 2 * c:2 * c + 1]), T.ZTo[:, z1 + 16 * c:z1 + 16 * c + 16], ["offX", ("z", s + 1)], XR, c=16, k="s")
 
     def marks(s):
-        mm("hn", T.b6[:, 0:256], "pHN", "b6", T.nIf[:], Nof(T.NSi, s), ["nIf", ("Ni", s)], True, False, 1024)
-        mm("hn", T.b6[:, 0:256], "pHN", "b6", T.If[:], T.hf[:, 0:256], ["If"] + HF, False, True, 1024)
-        tt("red", T.red[:], K, T.thE[:], A.is_lt, ["K", "thE"], ["red"], ["b0"], c=256)
-        tt("ref", T.ref[:], T.scM[:, 0:256].indirect(L_B32), T.Ksb[:], A.is_equal, ["scM", "L_B", "Ksb"], ["ref"], c=256, k="g")
+        act("sg", T.sg[:], K2, F.Sign, ["K2"], ["sg", "ac0"], ["b1"], c=280, bias=0.5, accum_out=T.acol[:, 0:1])
+        tt("ref", T.ref[:], T.pi2[:, 0:8].indirect(T.LB[:, 0:16]), T.colc[:], A.is_equal, ["pi2", "LB", "colc"], ["ref"], c=256, k="g")
+        add("q", pq, "pQ", "b6", "p6", T.sg[:], ["sg"], False, False)
+        add("q", pq, "pQ", "b6", "p7", T.ref[:], ["ref"])
+        act("Tr", T.Tr[:], pq, F.Relu, ["pQ"], ["Tr"], ["b6"], scale=-1.0, bias=35.0)
 
     def count():
-        if CFG["eng"]["A"] == "a":
-            act("A", T.junk[:], T.red[:], F.Copy, ["red"], ["junk", "ac0"], accum_out=T.acol[:, 0:1])
-        mm("A", T.b7[:, 0:1], "pA", "b7", T.BD[:], T.acol[:, 0:1], ["BD", "ac0"], True, True, 256)
-        ts("A", T.acol[:, 4:5], T.b7[:, 0:1], 32.0, CM0, A.mult, A.add, ["pA"], ["ac1"], ["b7"])
+        mm("A", T.b3[:, 384:385], "pA", "b3", T.BD[:], T.acol[:, 0:1], ["BD", "ac0"], True, True, 256)
+        act("A", T.acol[:, 4:5], T.b3[:, 384:385], F.Identity, ["pA"], ["ac1"], ["b3"], c=64, scale=16.0, bias=65536.0 + CM0)
 
-    def new_state(s):
-        p7, p3 = T.b7[:, 256:512], T.b3[:, 256:512]
-        mm("T", p7, "pT", "b7", T.Ib[:], Tof(T.ZTi, s), ["Ib", ("Ti", s)], True, False, 256)
-        mm("T", p7, "pT", "b7", T.nI8[:], T.red[:], ["nI8", "red"], False, False, 256)
-        mm("T", p7, "pT", "b7", T.nI8[:], T.ref[:], ["nI8", "ref"], False, True, 256)
-        mm("T", p3, "pM", "b3", T.sI[:, 128 * s:128 * s + 128], T.red[:], [("sI", s), "red"], True, False, 256)
-        mm("T", p3, "pM", "b3", T.I99[:], T.ref[:], ["I99", "ref"], False, True, 256)
-        if CFG["eng"]["Tr"] == "a":
-            act("Tr", T.Tr[:], p7, F.Relu, ["pT"], ["Tr"], ["b7"])
-        else:
-            ts("Tr", T.Tr[:], p7, 0.0, None, A.max, None, ["pT"], ["Tr"], ["b7"], c=256)
-        tt("Tn", Tof(T.ZTo, s + 1), p3, T.Tr[:], A.add, ["pM", "Tr"], [("T", s + 1)], ["b3"], c=256)
-        tt("dN", T.dN[:], T.b6[:, 0:256], T.red[:], A.mult, ["pHN", "red"], ["dN"], ["b6"], c=256)
-        mm("N", p7, "pT", "b7", T.If[:], Nof(T.NSi, s), ["If", ("Ni", s)], True, False, 1024)
-        mm("N", p7, "pT", "b7", T.If[:], T.dN[:], ["If", "dN"], False, True, 1024)
-        copy("Nn", Nof(T.NSo, s + 1), p7, ["pT"], [("N", s + 1)], ["b7"], c=256, e=CFG["eng"]["Nn"])
+    def new_dates(s, out, res):
+        add("T", pa, "pa", "b7", "nI", T.Tr[:], ["Tr"], True, False)
+        add("T", pa, "pa", "b7", "c%d" % s, T.sg[:], ["sg"])
+        affine("Tn", out, pa, 1.0, 99 - (97 - s) / 2.0, ["pa"], [res], ["b7"])
 
-    act("tgt", T.tgt[:], Tof(T.ZTo, 0), F.Relu, [("T", 0)], ["tgt"])
-    tile(T.ZTo, 0, [("z", 0)])
-    lane_sums(0)
-    chooser(Nof(T.NSo, 0), [("N", 0)], ["tgt"])
-    iota(T.acol[:, 4:5], [[0, 1]], int(CM0), ["ac1"], 1, **fl)
-    send_state(0)
+    def new_names(s, out, res):
+        add("N", pb, "pb", "b7", "p12", T.sg[:], ["sg"], True)
+        tt("t1", T.t1[:], pb, T.hf[:, 0:256], A.min, ["pb"] + HF, ["t1"], ["b7"], c=256)
+        mm("N", pb, "pb", "b7", T.I16[:, 0:128], Nof(T.Ni, s), [("Ni", s), "I16"], True, False, 256)
+        add("N", pb, "pb", "b7", "n12", T.ones[:], ["ones"], False, False)
+        add("N", pb, "pb", "b7", "n12", T.sg[:], ["sg"])
+        tt("Nn", out, pb, T.t1[:], A.max, ["pb", "t1"], [res], ["b7"], c=256)
+
+    def new_z(o):
+        tile("zt", "pt", T.ZTo[:, o * ZT:o * ZT + 128], [("z", o)])
+        lane_sums("szu", T.ZTo, o * ZT, [("z", o)], "b2", 384, "psu", 0)
+
+    new_z(0)
+    chooser(0, T.No, [("N", 0)])
     part1(0)
+    send_state(0)
     send_rest(0)
     for s in range(S):
         part3(s)
-        cnt["ph"] += 1
         if s < S - 1:
             refuse(s)
-            marks(s)
             learn(s)
-            chooser(Nof(T.NSi, s), [("Ni", s)], ["tgt", "red", "ref"])
+            marks(s)
             count()
-            tile(T.ZTo, (s + 1) * ZT, [("z", s + 1)])
-            lane_sums(s + 1)
-            new_state(s)
-            send_state(s + 1)
+            new_names(s, Nof(T.No, s + 1), ("N", s + 1))
+            chooser(s + 1, T.Ni, [("Ni", s)])
+            new_z(s + 1)
+            new_dates(s, Tof(T.ZTo, s + 1), ("T", s + 1))
             part1(s + 1)
+            send_state(s + 1)
             send_rest(s + 1)
         else:
             learn(s)
@@ -601,18 +676,24 @@ def rank_program(g, core, T, topo):
             dma("s", T.yz[:], T.ZTo[:, S * ZT:S * ZT + 128], 32768, [("z", S)], ["yz"])
             refuse(s)
             marks(s)
-            new_state(s)
-            mm16("oP", T.b2[:, 256:512], "poP", "b2", T.Ep, lambda r: T.PW[:, PO + 256 * r:PO + 256 * r + 256], ["Ep"] + PR, True, True, 4096)
-            act("oP", T.oP[:], T.b2[:, 256:512], F.Copy, ["poP"], ["oP"], ["b2"])
-            dma("a", T.yp[:], T.oP[:], 131072, ["oP"], ["yp"])
-            copy("oT", T.oT[:], Tof(T.ZTo, S).indirect(L_OUT), [("T", S), "L_OUT"], ["oT"], c=256, k="g")
+            new_dates(s, T.oT[:], "oT")
             dma("s", T.yt[:], T.oT[:], 131072, ["oT"], ["yt"])
-            copy("oN", T.oN[:], Nof(T.NSo, S).indirect(L_OUT), [("N", S), "L_OUT"], ["oN"], c=256, k="g", e="a")
+            new_names(s, T.e1[:], "e1")
+            act("oN", T.oN[:], T.e1[:], F.Identity, ["e1"], ["oN"], bias=H)
             dma("a", T.yn[:], T.oN[:], 131072, ["oN"], ["yn"])
 
-    NODES[:] = nodes
-    for i in run_plan(nodes, EST, None, CFG)[0]:
-        emit(nodes[i])
+            def unfold():
+                for r in range(16):
+                    last = t.matmul(T.b0[:, 256:512], T.Es[:, 432 + 15 - r:432 + 143 - r], T.PW[:, PO + 256 * r:PO + 256 * r + 256], r == 0, r == 15)
+                return last
+            op("t", "oP", unfold, ["Es"] + PR, ["poP"] + [("pu", k) for k, c in chunks("y1")], ["b0"], 4096, "pe")
+            act("oP", T.oP[:], T.b0[:, 256:512], F.Identity, ["poP"], ["oP"], ["b0"], bias=H)
+            dma("a", T.yp[:], T.oP[:], 131072, ["oP"], ["yp"])
+
+    if not PLAN:
+        PLAN.extend(run_plan(nodes, EST, CFG))
+    for i, x in PLAN:
+        emit(dict(nodes[i], **x))
     TAG[0] = "end"
     for e in "vatg":
         g.sync.wait_ge(T.sem[e], cnt[e])

@@ -1,4 +1,3 @@
-from concourse.bass import DstId, RemoteDMATransfer
 from concourse.mybir import AluOpType as A, ActivationFunctionType as F
 
 S = 4
@@ -21,14 +20,14 @@ SCRATCH = {
     "pxi": _sb(256, i32), "oli": _sb(256, i32), "nli": _sb(256, i32), "tli": _sb(256, i32), "thi": _sb(4, i32),
     "pxf": _sb(256, f32), "phi": _sb(256, bf), "plo": _sb(256, bf),
     "ip": _sb(8, i32), "ib": _sb(8, i32), "col": _sb(16, f32), "io1": _sb(144, f32), "io2": _sb(128, f32), "io3": _sb(128, f32),
-    "Es": _sb(4 * 144, bf), "E1f": _sb(144, f32), "A01": _sb(128, bf), "Eg": _sb(32, bf), "If": _sb(128, f32), "Is": _sb(13 * 128, bf),
-    "I16": _sb(256, f16), "Pm": _sb(4 * 256, f16), "Rep": _sb(128, f16), "KL": _sb(512, f16), "KR": _sb(256, f16), "colc": _sb(256, bf),
+    "Es": _sb(4 * 144, bf), "E1f": _sb(144, f32), "A01": _sb(128, bf), "Eg": _sb(32, bf), "If": _sb(128, f32), "Is": _sb(12 * 128, bf),
+    "I16": _sb(256, f16), "Pm": _sb(4 * 256, f16), "Rep": _sb(128, f16), "Repb": _sb(256, bf), "KL": _sb(512, f16), "KR": _sb(256, f16), "colc": _sb(256, bf),
     "BD": _sb(128, f32), "DM": _sb(128, f32), "LM": _sb(128, bf), "ones": _sb(256, bf), "c62": _sb(8, f32),
     "sg1": _sb(128, f32), "sg2": _sb(128, f32), "d0x": _sb(256, f32), "d0n": _sb(256, f32),
-    "LB": _sb(16, u16), "thf": _sb(4, f32), "Sz": _sb(256, f16),
-    "hf": _sb(264, f32), "scM": _sb(256, f32), "scN": _sb(256, f32), "e1": _sb(256, f32), "e2": _sb(256, bf),
-    "pi1": _sb(8, i32), "pi2": _sb(8, i32), "xi1": _sb(8, i32), "xi2": _sb(8, i32), "cj": _sb(16, u16),
-    "MkP": _sb(128, f32), "MkX": _sb(128, f32), "Mkh": _sb(128, f32), "Mkhb": _sb(128, bf), "gb": _sb(128, bf),
+    "LB": _sb(16, u16), "thf": _sb(4, f32), "So": _sb(512, f16), "Si": _sb(512, f16),
+    "hf": _sb(264, f32), "scM": _sb(256, i32), "scN": _sb(256, f32), "e1": _sb(256, f32), "e2": _sb(256, bf),
+    "pi2": _sb(8, i32), "xi1": _sb(8, i32), "xi2": _sb(8, i32), "cj": _sb(16, u16), "cjb": _sb(8, bf), "cjT": _sb(128, bf),
+    "MkP": _sb(128, f32), "MkX": _sb(128, f16), "BD16": _sb(128, f16), "Mkh": _sb(128, f32), "Mkhb": _sb(128, bf), "Gh": _sb(256, f32), "gb": _sb(128, bf),
     "keyP": _sb(128, f32), "keyX": _sb(128, f32), "eqP": _sb(128, f32), "eqX": _sb(128, f32), "duP": _sb(128, f32), "duX": _sb(128, f32),
     "t8P": _sb(8, f32), "t8X": _sb(8, f32), "offP": _sb(16, u16), "offX": _sb(16, u16), "val": _sb(128, bf), "hb": _sb(8, u16),
     "zs": _sb(128, f32), "zi": _sb(128, i32),
@@ -39,27 +38,27 @@ SCRATCH = {
 }
 for _b in ("b0", "b1", "b2", "b3", "pt", "pu", "b6", "b7"):
     SCRATCH[_b] = ("psum", [128, 512], f32)
-SEMAPHORES = (["v", "a", "t", "g", "sent"] + ["d%d" % i for i in range(20)] + ["h%d" % i for i in range(16)]
-              + ["z%d" % i for i in range(4)] + ["t%d" % i for i in range(4)] + ["n%d" % i for i in range(4)] + ["o%d" % i for i in range(3)] + ["l%d" % i for i in range(3)])
+SEMAPHORES = (["v", "a", "t", "g", "sent"] + ["d%d" % i for i in range(20)] + ["h%d" % i for i in range(20)]
+              + [x + str(i) for x in "zstnol" for i in range(4)])
 TAG = [""]
 PLAN = []
 
 CFG = {
-    "gp": [0, 128, 256], "y1": [0, 128, 224, 256], "y3": [0, 128, 224, 256],
-    "run": {"a": 4, "v": 2, "m": 4},
-    "eng": {"Qs": "a", "Tn": "a", "z0": "a", "z1": "v"},
-    "xs": 256, "share": 0.1, "ahead": 50.0, "hold": {},
-    "after": {"t": -1, "n": 9},
-    "turn": "scM scN p MkP x lmP rowP Mkh keyP eqP k2 sg val duP offP scatP MkX lmX rowX keyX hb zs zp A cm ref eqX q duX s3 zi zn offX send_z Tr qn q2 Qs "
-            "zt szu scatX T Tn send_t send_h gp_0 po0 R0 gp_1 po1 R1 gp_2 po2 R2 us y1_0 uy0 m1_0 um0 h0 zt3 szk y1_1 uy1 m1_1 um1 h1 y1_2 uy2 m1_2 um2 h2 "
-            "y1_3 uy3 m1_3 um3 h3 N t1 Nn send_n ks hf y3_0 ky0 m3_0 km0 K0 y3_1 ky1 m3_1 km1 K1 y3_2 ky2 m3_2 km2 K2 y3_3 ky3 m3_3 km3 K3 e send_o send_l",
-    "first": "PW dma_pxi dma_oli dma_thi dma_tli dma_ZTo dma_nli px dma_PW dma_X send_z",
-    "last": "scN x scM p MkX lmX rowX keyX hb eqX zs duX zi offX zn scatX dma_yx",
+    "gp": [0, 64, 192, 256], "y1": [0, 64, 128, 192, 256], "y3": [0, 128, 224, 256], "flat": (64,),
+    "seq": "p0 u0 p1 p2 u1 u2 u3",
+    "run": {"a": 4, "v": 2, "m": 8, "y3_1v": 1, "y3_0a": 3, "gp_2a": 8, "gp_1a": 8, "gp_0a": 5},
+    "eng": {"Qs": "a", "Tn": "a", "z0": "a", "z1": "v", "ref": "v", "Mkh": "a", "MkX": "a"},
+    "xs": 256, "yield": 2000, "rounds": 1, "tile": 2, "haste": 60,
+    "hold": {"p": 150, "MkP": 60, "eqP": 60, "scatP": 60, "R0": 60, "R1": 150, "R2": 1, "h0": 80, "h1": 60, "h2": 60, "h3": 60, "K0": 1, "po0": 60, "y1_2": 40, "uy0": 1},
+    "turn": "rowX Mkh keyP scM scN p MkP x lmP rowP eqP zi k2 sg N t1 val duX duP offP scatP MkX lmX keyX hb zs zp eqX q po1 s3 Qs zn A offX send_z Nn Tr qn q2 "
+            "ref scatX send_h po po0 cm R0 R1 po2 R2 h0 h1 h2 h3 szu K0 K1 K2 zt uy0 um0 m1_0 gp_0 y1_0 gp_1 gp_2 T y1_1 Tn send_t uy1 um1 us m1_1 zt3 szk "
+            "uy2 um2 m1_2 y1_2 uy3 um3 m1_3 y1_3 ks ky0 km0 send_o m3_0 y3_0 m3_1 send_n hf e ke ky1 km1 y3_1 ky2 km2 m3_2 y3_2 send_l",
+    "first": "PW dma_pxi dma_oli dma_thi po dma_tli dma_nli px dma_PW dma_X send_z",
+    "last": "scN x scM p MkX lmX rowX hb eqX zs zi offX zn scatX dma_yx",
 }
-CFG.update(gp=[0, 96, 224, 256], y1=[0, 96, 192, 256], y3=[0, 128, 224, 256], seq="p0 p1 p2 u0 u1 u2", flat=(64,))
-CFG.update({'turn': 'hb p keyP scM scN MkP x lmP rowP Mkh eqP k2 po2 offP sg val duP scatP MkX lmX rowX keyX zs zp R1 A ref eqX q duX s3 zi zn offX R2 send_z Tr qn q2 Qs scatX send_h R0 po po0 po1 h0 h2 K0 K1 K2 gp_0 zt gp_1 cm T N send_t us uy0 Tn szu ks um0 m1_0 y1_0 uy1 h1 um1 m1_1 y1_1 zt3 uy2 um2 m1_2 y1_2 gp_2 ky0 km0 m3_0 m3_1 szk t1 Nn hf e ke ky1 km1 y3_0 y3_1 ky2 km2 m3_2 y3_2 send_l send_o send_n', 'first': 'PW R2 dma_pxi dma_oli dma_thi um0 dma_tli dma_ZTo dma_nli zt3 px dma_PW dma_X send_z', 'last': 'scN x lmP scM p MkX lmX rowX Mkh keyX eqX zs duX zi offX zn scatX dma_yx', 'hold': {'R0': 70, 'R1': 70, 'R2': 70, 'h0': 70, 'h1': 70, 'h2': 70, 'K0': 70, 'K1': 70, 'K2': 70, 'Qs': 300, 'p': 70, 'MkP': 70, 'zi': 150, 's3': 300}, 'run': {'a': 3, 'v': 2, 'm': 2, 'y3_2v': 6, 'y1_2v': 0, 'gp_0a': 5, 'y3_0a': 8, 'y1_2a': 1, 'y3_1a': 8, 'gp_1v': 3, 'y1_0v': 6, 'gp_1a': 8, 'y3_0v': 8, 'm3_0m': 3, 'y3_1v': 3, 'gp_2a': 6, 'y3_2a': 5}, 'ahead': 50.0, 'share': 0})
-CFG.update(dict(gp=[0,64,192,256],y1=[0,64,128,192,256],y3=[0,128,224,256],after={"t":-1,"n":-1},seq="p0 u0 p1 p2 u1 u2 u3", **{'turn': 'rowX Mkh keyP scM scN p MkP x lmP rowP eqP zi k2 sg N t1 val duX duP offP scatP MkX lmX keyX hb zs zp eqX q po1 s3 Qs zn A offX send_z Nn Tr qn q2 ref scatX send_h po po0 cm R0 R1 po2 R2 h0 h1 h2 h3 szu K0 K1 K2 K3 zt uy0 um0 m1_0 gp_0 y1_0 gp_1 gp_2 T y1_1 Tn send_t uy1 um1 us m1_1 zt3 szk uy2 um2 m1_2 y1_2 uy3 um3 m1_3 y1_3 ks ky0 km0 send_o m3_0 y3_0 m3_1 send_n hf e ke ky1 km1 y3_1 ky2 km2 m3_2 y3_2 ky3 km3 m3_3 y3_3 send_l', 'first': 'PW dma_pxi dma_oli dma_thi po dma_tli dma_nli px dma_PW dma_X send_z', 'last': 'scN x scM p MkX lmX rowX hb eqX zs zi offX zn scatX dma_yx', 'hold': {'p': 150, 'MkP': 60, 'rowP': 60, 'eqP': 60, 'duP': 60, 'scatP': 60, 'R0': 60, 'R1': 150, 'R2': 1, 'h0': 80, 'h1': 60, 'h2': 60, 'h3': 60, 'K0': 1, 'K1': 60, 'K2': 60, 'po0': 60, 'um0': 60, 'um1': 60, 'um2': 60, 'um3': 1, 'km2': 60, 'scM': 60, 'val': 60, 'po1': 1, 'scatX': 250, 'y1_2': 40, 'uy0': 1, 'po': 40, 'km0': 40}, 'run': {'a': 4, 'v': 2, 'm': 8, 'y3_1v': 1, 'm3_1m': 6, 'y1_2v': 2, 'm1_2m': 8, 'm3_2m': 5, 'y1_3v': 6, 'm3_0m': 4, 'm1_0m': 5, 'y3_0a': 3, 'gp_2a': 8, 'gp_1a': 8, 'gp_0a': 5}, 'ahead': 0, 'share': 0}))
-EST = dict(cyc=0.87, g=1.56, sc=3.8, ind=55.0, pe=0.6, wake=185.0, dlat=800.0, drow=160.0, dbw=380.0, issue=400.0, rlat=700.0, rrow=320.0, rbw=128.0)
+CFG.update({'turn': 'MkP duX gMkh Tr lmP scM keyP Nn rowX val scN p x eqP zi k2 sg t1 qn offP MkX szu lmX hf ky0 eqX keyX cm zs po1 Mkh N hb s3 Qs zn A rowP send_z offX scatP ref scatX send_h y1_1 po0 po2 R0 R1 h0 h3 K0 K2 zt uy0 h2 gp_0 h1 m1_0 po duP ks y1_0 gp_1 gp_2 T send_t uy1 q um1 m1_1 um3 um0 R2 zt3 uy2 e um2 us m1_2 q2 y1_2 uy3 m3_0 m1_3 y1_3 km0 send_o y3_0 m3_1 send_s send_n ke ky1 K1 km1 y3_1 ky2 km2 m3_2 y3_2 send_l Tn', 'first': 'PW uy0 dma_pxi dma_oli um3 dma_thi q km0 dma_tli uy1 dma_nli K2 dma_PW po um2 dma_X send_h send_z px', 'last': 'p offP MkX lmX sg hb oP eqX ref zs x T zi MkP offX rowX scatX dma_yx', 'hold': {'eqP': 60, 'R0': 60, 'h0': 80, 'h1': 40, 'h3': 60, 'K0': 1, 'uy0': 1, 'm1_0': 80, 'm3_0': 80, 'm1_2': 1, 'y1_0': 80, 'm3_1': 40, 'h2': 80, 'm1_1': 40}, 'run': {'a': 4, 'v': 4, 'm': 3, 'gp_1a': 8, 'gp_0a': 2, 'y3_1a': 5, 'y1_0v': 1, 'y1_2a': 3, 'gp_0v': 8, 'gp_2a': 6}, 'yield': 10, 'haste': 300, 'y3': [0, 96, 224, 256],
+            'eng': {"Qs": "a", "Tn": "a", "z0": "v", "z1": "v", "ref": "v", "Mkh": "a", "MkX": "v"}})
+EST = dict(cyc=0.85, g=1.56, sc=3.8, ind=55.0, pe=0.5, wake=185.0, dlat=800.0, drow=160.0, dbw=380.0, issue=400.0, rlat=700.0, rrow=320.0, rbw=128.0)
 
 
 def run_plan(nodes, P, cfg):
@@ -120,14 +119,15 @@ def run_plan(nodes, P, cfg):
         for b in x["B"]:
             bfree.setdefault(b, {})[e] = done[i]
 
+    hold = [cfg["hold"].get(x["tag"]) if x["ph"] < S else cfg["haste"] * (x["tag"] in cfg["last"].split()) for x in nodes]
     left = [len(x["pre"]) for x in nodes]
     ready, order = [i for i in range(n) if left[i] == 0], []
     while ready:
         es = [(est(i, e), e, i) for i in ready for e in (nodes[i]["e"] if nodes[i]["e"] != "x" else "av" if cfg["run"].get(nodes[i]["tag"] + "v", 1) else "a")]
         t0, e0 = min(es)[:2]
-        mine = [(prio[i] - (1e9 if e == "v" and nodes[i]["e"] == "x" else 0.0), -i, t, i) for t, e, i in es if e == e0]
+        mine = [(prio[i] - (1e4 * cfg["yield"] if e == "v" and nodes[i]["e"] == "x" else 0.0), -i, t, i) for t, e, i in es if e == e0]
         now = sorted([m for m in mine if m[2] <= t0], reverse=True)
-        soon = [(m[2] + cfg["hold"][nodes[m[3]]["tag"]], m) for m in mine if m > now[0] and nodes[m[3]]["tag"] in cfg["hold"]]
+        soon = [(m[2] + hold[m[3]], m) for m in mine if m > now[0] and hold[m[3]]]
         room, first = min(soon) if soon else (1e18, None)
         t1, i1 = ([m for m in now if t0 + busy[m[3]] + (P["ind"] if nodes[m[3]]["e"] == "x" else 0.0) <= room] + [first])[0][2:]
         x, run = nodes[i1], [i1]
@@ -138,7 +138,7 @@ def run_plan(nodes, P, cfg):
             if kind == "v":
                 near = near[::-1]
             run = near[:1]
-            for i in near[1:min(most, 4) if kind == "m" else most]:
+            for i in near[1:min(most, cfg["tile"]) if kind == "m" else most]:
                 if abs(i - run[-1]) != 1:
                     break
                 run.append(i)
@@ -156,6 +156,59 @@ def run_plan(nodes, P, cfg):
                 left[j] -= 1
                 if left[j] == 0:
                     ready.append(j)
+
+    head = {}
+    for i in order:
+        for j in range(nodes[i]["span"][1] - nodes[i]["span"][0] if nodes[i]["span"] else 1):
+            head[i + j] = i
+    pre, suc = {i: set() for i in order}, {i: set() for i in order}
+    for j, x in enumerate(nodes):
+        for p in x["pre"]:
+            pre[head[j]].add(head[p])
+            suc[head[p]].add(head[j])
+    full = {i: busy[i] + lat[i] for i in order}
+
+    def gap(taken, a, d):
+        for s, f in taken:
+            if f > a + 1e-6:
+                if s >= a + d - 1e-6:
+                    break
+                a = f
+        return a
+
+    def sweep(order, before, back):
+        taken, banks, st = {}, {}, {}
+        for i in order:
+            x = nodes[i]
+            e, k = x["e"], x["c"][0]
+            t = max([st[p] + full[p] + (0.0 if e == "t" and nodes[p]["e"] == "t" else P["wake"]) for p in before[i]] + [0.0])
+            uses = [(e, lat[i] if back else 0.0, busy[i])]
+            if k in ("dma", "send"):
+                ahead, behind = (P["dlat"], 0.0) if k == "dma" else (0.0, P["rlat"])
+                uses.append(("pipe", behind if back else busy[i] + ahead, lat[i] - ahead - behind))
+            t1 = -1.0
+            while t > t1 + 1e-6:
+                t1 = t
+                for r, off, d in uses:
+                    t = gap(taken.setdefault(r, []), t + off, d) - off
+                for b in x["B"]:
+                    for s, f, e2 in banks.setdefault(b, []):
+                        if e2 != e and t < f + P["wake"] and s < t + busy[i] + P["wake"]:
+                            t = f + P["wake"]
+            st[i] = t
+            for r, off, d in uses:
+                taken[r].append((t + off, t + off + d))
+                taken[r].sort()
+            for b in x["B"]:
+                banks[b].append((t, t + busy[i], e))
+        return st
+
+    for back in (False, True) * cfg["rounds"]:
+        st = sweep(order, suc if back else pre, back)
+        order = sorted(order, key=lambda i: (-st[i] - full[i], i if back else -i))
+    if cfg["rounds"]:
+        st = sweep(order, pre, False)
+        order = sorted(order, key=lambda i: (st[i], i))
     return [(i, {k: nodes[i][k] for k in ("e", "span", "R", "W")}) for i in order]
 
 
@@ -297,7 +350,7 @@ def rank_program(g, core, T, topo):
     def col(i):
         return T.col[:, i:i + 1]
 
-    IS = {"I": 1.0, "nI": -1.0, "n13": -8192.0, "p13": 8192.0, "p7": 128.0, "p6": 64.0, "p12": 4096.0, "n12": -4096.0, "i1": 0.5}
+    IS = {"I": 1.0, "nI": -1.0, "n13": -8192.0, "p13": 8192.0, "p7": 128.0, "p6": 64.0, "p12": 4096.0, "n12": -4096.0}
     for s in range(S):
         IS["c%d" % s] = (s - 97.0) / 2
 
@@ -390,6 +443,12 @@ def rank_program(g, core, T, topo):
     copy("c", T.I16[:, 0:128], T.If[:], ["If"], ["I16"], c=128)
     ts("c", T.I16[:, 128:256], T.If[:], -512.0, None, A.mult, None, ["If"], ["J16"], c=128)
     ts("c", T.Rep[0:8, :], T.duP[0:8, :], 0.0, None, A.is_equal, None, ["duP"], ["Rep"], c=128)
+    if CFG["eng"]["ref"] == "a":
+        for h in range(2):
+            copy("c", T.Repb[0:8, 128 * h:128 * h + 128], T.Rep[0:8, :], ["Rep"], [("Repb", h)])
+    for h in range(2):
+        copy("c", T.So[:, 256 * h:256 * h + 256], T.ones[:], ["ones"], ["So"], c=128)
+    act("c", T.pu[:, 384:512], T.DM[:], F.Copy, ["DM"], ["DMp"], ["pu"], c=128)
     plus("c", T.thf[0:8, :], T.thi[0:8, :], -H, ["thi"], ["thf"])
     for s in range(S):
         ts("c", T.KL[0:32, 128 * s:128 * s + 128], T.duX[0:32, :], 0.0, T.thf[0:32, s:s + 1], A.is_equal, A.mult, ["duX", "thf"], [("KL", s)], c=128)
@@ -399,12 +458,13 @@ def rank_program(g, core, T, topo):
     copy("c", T.KR[32:33, :], T.e1[32:33, :], ["e1"], ["KR1"], c=256)
     act("c", col(C_T), col(C_R8), F.Identity, ["cR8", "cE"], ["cT"], c=64, scale=32.0, bias=col(C_E))
     for k, (c0, c1) in chunks("y3"):
-        ts("c", T.Pm[:, 256 * k:256 * k + 256], T.colc[:], -float(c0 // 8), col(C_T), A.add, A.is_equal, ["colc", "cT"], [("Pm0", k)], c=128)
-        ts("c", T.Pm[:, 256 * k:256 * k + 256], T.Pm[:, 256 * k:256 * k + 256], -512.0, None, A.mult, None, [("Pm0", k)], [("Pm", k)], c=128)
+        act("c", col(C_T + 1 + k), col(C_T), F.Identity, ["cT"], [("cT", k)], c=64, bias=float(c0 // 8))
+        ts("c", T.Pm[:, 256 * k:256 * k + 256], T.colc[:], col(C_T + 1 + k), -512.0, A.is_equal, A.mult, ["colc", ("cT", k)], [("Pm", k)], c=128)
+    copy("c", T.BD16[:], T.BD[:], ["BD"], ["BD16"], c=128)
     for j, x in enumerate((1.0, -1.0, 2.0, col(C_LT2))):
-        act("c", T.Eg[:, 8 * j:8 * j + 8], T.BD[:, 0:128:16], F.Identity, ["BD", "cLT2"], ["Eg"], c=64, scale=x)
+        act("c", T.Eg[:, 8 * j:8 * j + 8], T.BD[:, 0:128:16], F.Identity, ["BD", "cLT2"], [("Eg", j)], c=64, scale=x)
         if j:
-            act("c", T.Es[:, 144 * j:144 * j + 144], T.E1f[:], F.Identity, ["E1f", "cLT2"], ["Es"], c=144, scale=x)
+            act("c", T.Es[:, 144 * j:144 * j + 144], T.E1f[:], F.Identity, ["E1f", "cLT2"], [("Es", j)], c=144, scale=x)
     for name in IS:
         act("c", Id(name), T.If[:], F.Identity, ["If"], [name], c=128, scale=IS[name])
     act("c", col(C_DX), col(C_R), F.Identity, ["cR"], ["cDX"], c=64, bias=4096.0)
@@ -430,18 +490,18 @@ def rank_program(g, core, T, topo):
 
     def tile(tag, bk, z, zR):
         def fn():
-            for j in range(4):
+            for j in range(CFG["tile"]):
                 last = t.matmul(T[bk][:, 128 * j:128 * j + 128], Id("I"), z, True, True)
             return last
-        op("t", tag, fn, ["I"] + zR, [bk], [bk], 512, "pe")
+        op("t", tag, fn, ["I"] + zR, [bk], [bk], 128 * CFG["tile"], "pe")
 
-    def lane_sums(tag, buf, z0, zR, b, c0, res, j):
+    def lane_sums(o):
         def fn():
             for r in range(16):
-                last = t.matmul(T[b][0:8, c0 + r:c0 + 128:16], buf[:, z0 + r:z0 + 128:16], T.Eg[:, 0:8], True, True)
+                last = t.matmul(T.b2[0:8, 384 + r:512:16], T.ZTo[:, o * ZT + r:o * ZT + 128:16], T.Eg[:, 0:8], True, True)
             return last
-        op("t", tag, fn, ["Eg"] + zR, [res], [b], 256, "pe")
-        ts(tag, T.Sz[0:8, 128 * j:128 * j + 128], T[b][0:8, c0:c0 + 128], -1.0, H, A.mult, A.add, [res], [("Sz", j)], [b], c=128)
+        op("t", "szu", fn, [("Eg", 0), ("z", o)], ["psu"], ["b2"], 256, "pe")
+        ts("szu", T.So[0:8, 128 * o:128 * o + 128], T.b2[0:8, 384:512], -1.0, H, A.mult, A.add, ["psu", "So"], [("So", o)], ["b2"], c=128)
 
     def flat(M):
         return M in CFG["flat"]
@@ -464,12 +524,12 @@ def rank_program(g, core, T, topo):
                 else:
                     last = t.matmul(T[bk][0:c1 - c0, r:128:16], x, T.Eg[:, 8 * j:8 * j + 8], False, stop and r == 15)
             return last
-        op("t", tag, fn, ["Eg", "Es"] + blocks(name, c0 // 8, c1 // 8), [("F", bk)], [bk], 16 * (max(64, c1 - c0) if is_flat else min(64, c1 - c0)), "pe")
+        op("t", tag, fn, [("Es" if is_flat else "Eg", j)] + blocks(name, c0 // 8, c1 // 8), [("F", bk)], [bk], 16 * (max(64, c1 - c0) if is_flat else min(64, c1 - c0)), "pe")
 
-    def distances(tags, k, c0, c1, y, m, j, out):
+    def distances(tags, k, c0, c1, y, m, sums, o, out):
         bk, M = "b%d" % (2 + cnt["F"] % 2), c1 - c0
         cnt["F"] += 1
-        mm(tags[0], T[bk][0:M, 0:128], ("F", bk), bk, T.Rep[0:8, 0:M], T.Sz[0:8, 128 * j:128 * j + 128], ["Rep", ("Sz", j)], True, False, 128)
+        mm(tags[0], T[bk][0:M, 0:128], ("F", bk), bk, T.Rep[0:8, 0:M], T[sums][0:8, 128 * o:128 * o + 128], ["Rep", (sums, o)], True, False, 128)
         fold(tags[1] + str(k), bk, 1, y, c0, c1, False, False)
         fold(tags[2] + str(k), bk, 2, m, c0, c1, False, True)
         plus(tags[3] + str(k), T[out][0:M, 128 * k:128 * k + 128], T[bk][0:M, 0:128], -2 * H, [("F", bk)], [(out, k)], [bk], c=128)
@@ -523,37 +583,34 @@ def rank_program(g, core, T, topo):
             bk = "b%d" % (2 + cnt["F"] % 2)
             cnt["F"] += 1
             pu, res = T[bk][:, 0:M], ("F", bk)
-            mm("us", pu, res, bk, T.Sz[0:8, 0:128], T.Rep[0:8, 0:M], ["Rep", ("Sz", 0)], True, False, 64)
+            mm("us", pu, res, bk, T.So[0:8, 128 * o:128 * o + 128], T.Rep[0:8, 0:M], ["Rep", ("So", o)], True, False, 64)
             add("us", pu, res, bk, "n12", T.ones[:, 0:M], ["ones"], False, False, 64)
             fold("uy%d" % k, bk, 1, "y1", c0, c1, True, False)
             fold("um%d" % k, bk, 2, "m1", c0, c1, True, True)
         else:
             bk, pu, res = "b0", T.b0[:, 256 + c0:256 + c1], ("pu", k)
-            distances(("us", "uy", "um", "h"), k, c0, c1, "y1", "m1", 0, "uf")
+            distances(("us", "uy", "um", "h"), k, c0, c1, "y1", "m1", "So", o, "uf")
             turn("h%d" % k, pu, res, bk, "uf", k, M, T.I16[0:M, 0:M], ["I16"], True, True, M)
         tt("h%d" % k, T.tf[:, c0:c1], pu, OF(o, c0, c1), A.mult, [res, ("OO", o)], tf, [bk], c=M)
         tt("h%d" % k, T.vi[:, c0:c1], T.tf[:, c0:c1], T.b6[:, 256 + c0:256 + c1], A.add, tf + ["cm"], [("vi", k)], ["b6"], c=M)
         ts("h%d" % k, T.hi[:, c0:c1], T.vi[:, c0:c1], 5, 4095, A.arith_shift_right, A.bitwise_and, [("vi", k)], [("hi", k)], c=M)
         copy("h%d" % k, Nof(T.Ho, o, c0, c1), T.hi[:, c0:c1], [("hi", k)], [("Ho", k)], c=M)
-        send(Nof(T.Hi, o, c0, c1), Nof(T.Ho, o, c0, c1), "h%d" % (4 * o + k), 256 * M, [("Ho", k)], ("Hi", o, k))
+        send(Nof(T.Hi, o, c0, c1), Nof(T.Ho, o, c0, c1), "h%d" % (5 * o + k), 256 * M, [("Ho", k)], ("Hi", o, k))
 
     def send_state(o):
-        z0 = o * ZT
+        z0, first = o * ZT, [] if o else ["Xb"]
         send(T.ZTi[:, z0:z0 + 128], T.ZTo[:, z0:z0 + 128], "z%d" % o, 32768, [("z", o)], ("Zi", o))
+        send(T.Si[:, 128 * o:128 * o + 128], T.So[:, 128 * o:128 * o + 128], "s%d" % o, 32768, [("So", o), "So"] + first, ("Si", o))
         if o < S - 1:
             after = [("Hi", o - 1, LAST[1]) if o else LAST]
             send(OF(o + 1), OF(o), "o%d" % o, 131072, [("OO", o)] + after, ("OO", o + 1))
             send(Nof(T.O16, o + 1), Nof(T.O16, o), "l%d" % o, 65536, [("O16", o)] + after, ("O16", o + 1))
-
-    def send_rest(o):
-        after = {x: [LAST] if CFG["after"][x] >= 0 else [] if o else ["Xb"] for x in "tn"}
-        send(Tof(T.ZTi, o), Tof(T.ZTo, o), "t%d" % o, 65536, [("T", o)] + after["t"], ("Ti", o))
-        send(Nof(T.Ni, o), Nof(T.No, o), "n%d" % o, 65536, [("N", o)] + after["n"], ("Ni", o))
+        send(Tof(T.ZTi, o), Tof(T.ZTo, o), "t%d" % o, 65536, [("T", o)] + first, ("Ti", o))
+        send(Nof(T.Ni, o), Nof(T.No, o), "n%d" % o, 65536, [("N", o)] + first, ("Ni", o))
 
     def part3(s):
         z0 = s * ZT
         tile("zt3", "pu", T.ZTi[:, z0:z0 + 128], [("Zi", s)])
-        lane_sums("szk", T.ZTi, z0, [("Zi", s)], "b6", 0, "pQ", 1)
         gather("y3", Xw, lambda b: XR + [("Hi", s, chunk_of("y1", b))], T.Hi, 256 * s)
         vmax("m3", "y3", "pu")
         KL = [("KL", s), ("KL1", s // 2), "KR", "KR1"]
@@ -563,30 +620,35 @@ def rank_program(g, core, T, topo):
             plus("hf", T.hf[:, c0:c1], Nof(T.Hi, s, c0, c1), -H, [("Hi", s, k)], [("hf", k)], c=c1 - c0)
         act("e", T.e1[:], Tof(T.ZTi, s), F.Abs, [("Ti", s)], ["e1"], bias=-(s + 99) / 2.0)
         act("e", T.e2[:], T.e1[:], F.Relu, ["e1"], ["e2"], scale=-float(1 << 22), bias=(98 - s) * float(1 << 21))
-        add("ke", K2, "K2", "b1", "nI", T.e2[:], ["e2"], False, False)
         add("q", pq, "pQ", "b6", "I", Tof(T.ZTi, s), [("Ti", s)], True, False)
         for k, (c0, c1) in chunks("y3"):
             M = c1 - c0
-            distances(("ks", "ky", "km", "K"), k, c0, c1, "y3", "m3", 1, "Kf")
+            distances(("ks", "ky", "km", "K"), k, c0, c1, "y3", "m3", "Si", s, "Kf")
             turn("K%d" % k, K1, "K1", "b0", "Kf", k, M, T.Pm[0:M, 256 * k:256 * k + 256], [("Pm", k)], False, c1 == 256, 256)
-            turn("k2", T.b1[:, 256 + c0:256 + c1], "K2", "b1", "Kf", k, M, T.I16[0:M, 128:128 + M], ["J16"], False, c1 == 256, M)
+            turn("k2", T.b1[:, 256 + c0:256 + c1], "K2", "b1", "Kf", k, M, T.I16[0:M, 128:128 + M], ["J16"], False, False, M)
+        add("ke", K2, "K2", "b1", "nI", T.e2[:], ["e2"])
         cnt["ph"] += 1
         scan("scM", T.scM[:], T.d0x[:], K1, -256.0, A.max, A.min, ["d0x", "K1"], ["scM"], ["b0"], c=256)
         scan("scN", T.scN[:], T.d0n[:], K1, 0.0, A.add, A.max, ["d0n", "K1"], ["scN"], ["b0"], c=256)
-        copy("p", T.pi1[:], T.scM[:, 31:256:32], ["scM"], ["pi1"])
-        ts("p", T.pi2[:], T.pi1[:], 511, None, A.bitwise_and, None, ["pi1"], ["pi2"])
+        ts("p", T.pi2[:], T.scM[:, 31:256:32], 511, None, A.bitwise_and, None, ["scM"], ["pi2"])
         copy("p", T.cj[:, 0:8], T.pi2[:], ["pi2"], ["cj"])
         tt("x", T.xi1[:], T.c62[:], T.scN[:, 31:256:32], A.subtract, ["c62", "scN"], ["xi1"])
         ts("x", T.xi2[:], T.xi1[:], 511, None, A.bitwise_and, None, ["xi1"], ["xi2"])
         copy("x", T.cj[:, 8:16], T.xi2[:], ["xi2"], ["cb"])
-        tt("Mkh", T.Mkh[:], T.hf[:, 0:264].indirect(T.cj[:, 0:8]), T.DM[:], A.mult, HF + ["cj", "DM"], ["Mkh"], c=128, k="g")
-        tt("MkX", T.MkX[:], T.hf[:, 0:264].indirect(T.cj[:, 8:16]), T.DM[:], A.mult, HF + ["cb", "DM"], ["MkX"], c=128, k="g")
+        for x, j, lst in (("Mkh", 0, "cj"), ("MkX", 1, "cb")):
+            src = T.hf[:, 0:264].indirect(T.cj[:, 8 * j:8 * j + 8])
+            if CFG["eng"][x] == "v" or s == S - 1:
+                tt(x, T[x][:], src, T.DM[:], A.mult, HF + [lst, "DM"], [x], c=128, k="g")
+            else:
+                copy("g" + x, T.Gh[:, 128 * j:128 * j + 128], src, HF + [lst], [("Gh", j)], c=128, k="g", e="a")
+                tt(x, T[x][:], T.Gh[:, 128 * j:128 * j + 128], T.pu[:, 384:512], A.mult, [("Gh", j), "DMp"], [x], ["pu"], c=128)
 
     def first_of_block(x, bk, shift, dummy, dR):
         Mk, key, eq, du, t8 = [T[y + x] for y in ("Mk", "key", "eq", "du", "t8")]
         ps, res = T[bk][:, 128:256], "row" + x
         add("lm" + x, ps, res, bk, "I", T.LM[:], ["LM"], True, False, 128)
-        mm("row" + x, ps, res, bk, T.BD[:], Mk[:], ["BD", "Mk" + x], False, True, 512)
+        BD = "BD" if x == "P" else "BD16"
+        mm("row" + x, ps, res, bk, T[BD][:], Mk[:], [BD, "Mk" + x], False, True, 512 if x == "P" else 128)
         scan("key" + x, key[:, ::-1], T.sg1[:, ::-1], Mk[:, ::-1], 0.0, A.mult, A.add, ["sg1", "Mk" + x], ["key" + x])
         tt("eq" + x, eq[:], ps, key[:], A.is_equal, [res, "key" + x], ["eq" + x], [bk], c=128)
         scan("du" + x, du[:], T.sg2[:], eq[:], 0.0, A.mult, A.add, ["sg2", "eq" + x], ["du" + x])
@@ -625,7 +687,17 @@ def rank_program(g, core, T, topo):
 
     def marks(s):
         act("sg", T.sg[:], K2, F.Sign, ["K2"], ["sg", "ac0"], ["b1"], c=280, bias=0.5, accum_out=T.acol[:, 0:1])
-        tt("ref", T.ref[:], T.pi2[:, 0:8].indirect(T.LB[:, 0:16]), T.colc[:], A.is_equal, ["pi2", "LB", "colc"], ["ref"], c=256, k="g")
+        if CFG["eng"]["ref"] == "v":
+            tt("ref", T.ref[:], T.pi2[:, 0:8].indirect(T.LB[:, 0:16]), T.colc[:], A.is_equal, ["pi2", "LB", "colc"], ["ref"], c=256, k="g")
+        else:
+            pd = T.b0[:, 256:512]
+            copy("rf", T.cjb[:], T.pi2[:], ["pi2"], ["cjb"])
+            mm("rf", T.b1[0:8, 0:128], ("pR", 0), "b1", T.cjb[:], Id("I"), ["cjb", "I", ("pR", 1)], True, True, 128)
+            act("rf", T.cjT[0:8, :], T.b1[0:8, 0:128], F.Copy, [("pR", 0)], ["cjT", ("pR", 1)], ["b1"], c=128)
+            add("rf", pd, "pd", "b0", "nI", T.colc[:], ["colc"], True, False)
+            mm("rf", pd, "pd", "b0", T.cjT[0:8, :], T.Repb[0:8, :], ["cjT", ("Repb", 0), ("Repb", 1)], False, True, 256)
+            act("ref", T.e2[:], pd, F.Abs, ["pd"], ["e2"], ["b0"])
+            act("ref", T.ref[:], T.e2[:], F.Relu, ["e2"], ["ref"], scale=-1.0, bias=1.0)
         add("q", pq, "pQ", "b6", "p6", T.sg[:], ["sg"], False, False)
         add("q", pq, "pQ", "b6", "p7", T.ref[:], ["ref"])
         act("Tr", T.Tr[:], pq, F.Relu, ["pQ"], ["Tr"], ["b6"], scale=-1.0, bias=35.0)
@@ -649,13 +721,12 @@ def rank_program(g, core, T, topo):
 
     def new_z(o):
         tile("zt", "pt", T.ZTo[:, o * ZT:o * ZT + 128], [("z", o)])
-        lane_sums("szu", T.ZTo, o * ZT, [("z", o)], "b2", 384, "psu", 0)
+        lane_sums(o)
 
     new_z(0)
     chooser(0, T.No, [("N", 0)])
     part1(0)
     send_state(0)
-    send_rest(0)
     for s in range(S):
         part3(s)
         if s < S - 1:
@@ -669,7 +740,6 @@ def rank_program(g, core, T, topo):
             new_dates(s, Tof(T.ZTo, s + 1), ("T", s + 1))
             part1(s + 1)
             send_state(s + 1)
-            send_rest(s + 1)
         else:
             learn(s)
             dma("s", T.yx[:], T.X[:, 0:4096], 1048576, XR, ["yx"])
@@ -681,14 +751,17 @@ def rank_program(g, core, T, topo):
             new_names(s, T.e1[:], "e1")
             act("oN", T.oN[:], T.e1[:], F.Identity, ["e1"], ["oN"], bias=H)
             dma("a", T.yn[:], T.oN[:], 131072, ["oN"], ["yn"])
-
-            def unfold():
-                for r in range(16):
-                    last = t.matmul(T.b0[:, 256:512], T.Es[:, 432 + 15 - r:432 + 143 - r], T.PW[:, PO + 256 * r:PO + 256 * r + 256], r == 0, r == 15)
-                return last
-            op("t", "oP", unfold, ["Es"] + PR, ["poP"] + [("pu", k) for k, c in chunks("y1")], ["b0"], 4096, "pe")
-            act("oP", T.oP[:], T.b0[:, 256:512], F.Identity, ["poP"], ["oP"], ["b0"], bias=H)
-            dma("a", T.yp[:], T.oP[:], 131072, ["oP"], ["yp"])
+            for h, bk in enumerate(("pt", "pu")):
+                def unfold(h=h, bk=bk):
+                    for r in range(16):
+                        c0 = PO + 2048 * h + 128 * r
+                        last = t.matmul(T[bk][:, r:128:16], T.PW[:, c0:c0 + 128], T.Eg[:, 24:32], True, True)
+                    return last
+                op("t", "oP", unfold, [("Eg", 3)] + PR, [bk], [bk], 1024, "pe")
+                copy("oP", T.Kf[:, 128 * h:128 * h + 128], T[bk][:, 0:128], [bk], [("Kf", h)], [bk], c=128)
+                turn("oP", T[bk][:, 128:256], ("oq", h), bk, "Kf", h, 128, T.I16[:, 0:128], ["I16", bk], True, True, 128)
+                act("oP", T.oP[:, 128 * h:128 * h + 128], T[bk][:, 128:256], F.Identity, [("oq", h)], [("oP", h)], [bk], c=128, bias=H)
+                dma("as"[h], T.yp[:, 2048 * h:2048 * h + 2048], T.oP[:, 128 * h:128 * h + 128], 65536, [("oP", h)], [("yp", h)])
 
     if not PLAN:
         PLAN.extend(run_plan(nodes, EST, CFG))

from concourse.mybir import AluOpType as A, ActivationFunctionType as F

S = 4
PO = 32
XW, PWW = 4112, 4144
BIG = float(1 << 23)
ZT, OW = 384, 264
H = 2048.0
bf, f16, f32, i32, u16 = "bfloat16", "float16", "float32", "int32", "uint16"


def _sb(w, d):
    return ("sbuf", [128, w], d)


SCRATCH = {
    "X": _sb(XW, bf), "PW": _sb(PWW, bf), "y1": _sb(4096, bf), "m1": _sb(4096, bf), "y3": _sb(4096, bf), "m3": _sb(4096, bf), "gp": _sb(4096, bf),
    "ZTo": _sb(5 * ZT, bf), "No": _sb(4 * 256, f16), "ZTi": _sb(4 * ZT, bf), "Ni": _sb(4 * 256, f16),
    "OO": _sb(4 * OW, f32), "O16": _sb(4 * 256, u16), "Ho": _sb(4 * 256, u16), "Hi": _sb(4 * 256, u16),
    "pxi": _sb(256, i32), "oli": _sb(256, i32), "nli": _sb(256, i32), "tli": _sb(256, i32), "thi": _sb(4, i32),
    "pxf": _sb(256, f32), "phi": _sb(256, bf), "plo": _sb(256, bf),
    "ip": _sb(8, i32), "ib": _sb(8, i32), "col": _sb(16, f32), "io1": _sb(144, f32), "io2": _sb(128, f32), "io3": _sb(128, f32),
    "Es": _sb(4 * 144, bf), "E1f": _sb(144, f32), "A01": _sb(128, bf), "Eg": _sb(32, bf), "If": _sb(128, f32), "Is": _sb(12 * 128, bf),
    "I16": _sb(256, f16), "Pm": _sb(4 * 256, f16), "Rep": _sb(128, f16), "Repb": _sb(256, bf), "KL": _sb(512, f16), "KR": _sb(256, f16), "colc": _sb(256, bf),
    "BD": _sb(128, f32), "DM": _sb(128, f32), "LM": _sb(128, bf), "ones": _sb(256, bf), "c62": _sb(8, f32),
    "sg1": _sb(128, f32), "sg2": _sb(128, f32), "d0x": _sb(256, f32), "d0n": _sb(256, f32),
    "LB": _sb(16, u16), "thf": _sb(4, f32), "So": _sb(512, f16), "Si": _sb(512, f16),
    "hf": _sb(264, f32), "scM": _sb(256, i32), "scN": _sb(256, f32), "e1": _sb(256, f32), "e2": _sb(256, bf),
    "pi2": _sb(8, i32), "xi1": _sb(8, i32), "xi2": _sb(8, i32), "cj": _sb(16, u16), "cjb": _sb(8, bf), "cjT": _sb(128, bf),
    "MkP": _sb(128, f32), "MkX": _sb(128, f16), "BD16": _sb(128, f16), "Mkh": _sb(128, f32), "Mkhb": _sb(128, bf), "Gh": _sb(256, f32), "gb": _sb(128, bf),
    "keyP": _sb(128, f32), "keyX": _sb(128, f32), "eqP": _sb(128, f32), "eqX": _sb(128, f32), "duP": _sb(128, f32), "duX": _sb(128, f32),
    "t8P": _sb(8, f32), "t8X": _sb(8, f32), "offP": _sb(16, u16), "offX": _sb(16, u16), "val": _sb(128, bf), "hb": _sb(8, u16),
    "zs": _sb(128, f32), "zi": _sb(128, i32),
    "sg": _sb(256, bf), "ref": _sb(256, bf), "s3": _sb(256, bf), "Tr": _sb(256, bf), "Qs": _sb(384, f32), "t1": _sb(256, f32),
    "Rf": _sb(512, f16), "uf": _sb(512, f16), "Kf": _sb(512, f16),
    "acol": _sb(8, f32), "R16": _sb(256, u16), "tf": _sb(256, f32), "vi": _sb(256, i32), "hi": _sb(256, i32),
    "oP": _sb(256, f32), "oN": _sb(256, f32), "oT": _sb(256, f32),
}
for _b in ("b0", "b1", "b2", "b3", "pt", "pu", "b6", "b7"):
    SCRATCH[_b] = ("psum", [128, 512], f32)
SEMAPHORES = (["v", "a", "t", "g", "sent"] + ["d%d" % i for i in range(20)] + ["h%d" % i for i in range(20)]
              + [x + str(i) for x in "zstnol" for i in range(4)])
TAG = [""]
PLAN = []

CFG = {
    "gp": [0, 64, 192, 256], "y1": [0, 64, 128, 192, 256], "y3": [0, 128, 224, 256], "flat": (64,),
    "seq": "p0 u0 p1 p2 u1 u2 u3",
    "run": {"a": 4, "v": 2, "m": 8, "y3_1v": 1, "y3_0a": 3, "gp_2a": 8, "gp_1a": 8, "gp_0a": 5},
    "eng": {"Qs": "a", "Tn": "a", "z0": "a", "z1": "v", "ref": "v", "Mkh": "a", "MkX": "a"},
    "xs": 256, "yield": 2000, "rounds": 1, "tile": 2, "haste": 60,
    "hold": {"p": 150, "MkP": 60, "eqP": 60, "scatP": 60, "R0": 60, "R1": 150, "R2": 1, "h0": 80, "h1": 60, "h2": 60, "h3": 60, "K0": 1, "po0": 60, "y1_2": 40, "uy0": 1},
    "turn": "rowX Mkh keyP scM scN p MkP x lmP rowP eqP zi k2 sg N t1 val duX duP offP scatP MkX lmX keyX hb zs zp eqX q po1 s3 Qs zn A offX send_z Nn Tr qn q2 "
            "ref scatX send_h po po0 cm R0 R1 po2 R2 h0 h1 h2 h3 szu K0 K1 K2 zt uy0 um0 m1_0 gp_0 y1_0 gp_1 gp_2 T y1_1 Tn send_t uy1 um1 us m1_1 zt3 szk "
            "uy2 um2 m1_2 y1_2 uy3 um3 m1_3 y1_3 ks ky0 km0 send_o m3_0 y3_0 m3_1 send_n hf e ke ky1 km1 y3_1 ky2 km2 m3_2 y3_2 send_l",
    "first": "PW dma_pxi dma_oli dma_thi po dma_tli dma_nli px dma_PW dma_X send_z",
    "last": "scN x scM p MkX lmX rowX hb eqX zs zi offX zn scatX dma_yx",
}
CFG.update({'turn': 'MkP duX gMkh Tr lmP scM keyP Nn rowX val scN p x eqP zi k2 sg t1 qn offP MkX szu lmX hf ky0 eqX keyX cm zs po1 Mkh N hb s3 Qs zn A rowP send_z offX scatP ref scatX send_h y1_1 po0 po2 R0 R1 h0 h3 K0 K2 zt uy0 h2 gp_0 h1 m1_0 po duP ks y1_0 gp_1 gp_2 T send_t uy1 q um1 m1_1 um3 um0 R2 zt3 uy2 e um2 us m1_2 q2 y1_2 uy3 m3_0 m1_3 y1_3 km0 send_o y3_0 m3_1 send_s send_n ke ky1 K1 km1 y3_1 ky2 km2 m3_2 y3_2 send_l Tn', 'first': 'PW uy0 dma_pxi dma_oli um3 dma_thi q km0 dma_tli uy1 dma_nli K2 dma_PW po um2 dma_X send_h send_z px', 'last': 'p offP MkX lmX sg hb oP eqX ref zs x T zi MkP offX rowX scatX dma_yx', 'hold': {'eqP': 60, 'R0': 60, 'h0': 80, 'h1': 40, 'h3': 60, 'K0': 1, 'uy0': 1, 'm1_0': 80, 'm3_0': 80, 'm1_2': 1, 'y1_0': 80, 'm3_1': 40, 'h2': 80, 'm1_1': 40}, 'run': {'a': 4, 'v': 4, 'm': 3, 'gp_1a': 8, 'gp_0a': 2, 'y3_1a': 5, 'y1_0v': 1, 'y1_2a': 3, 'gp_0v': 8, 'gp_2a': 6}, 'yield': 10, 'haste': 300, 'y3': [0, 96, 224, 256],
            'eng': {"Qs": "a", "Tn": "a", "z0": "v", "z1": "v", "ref": "v", "Mkh": "a", "MkX": "v"}})
EST = dict(cyc=0.85, g=1.56, sc=3.8, ind=55.0, pe=0.5, wake=185.0, dlat=800.0, drow=160.0, dbw=380.0, issue=400.0, rlat=700.0, rrow=320.0, rbw=128.0)


def run_plan(nodes, P, cfg):
    n = len(nodes)
    busy, lat = [0.0] * n, [0.0] * n
    for i, x in enumerate(nodes):
        k, c = x["c"]
        if k == "n":
            busy[i] = max(64, c) * P["cyc"]
        elif k == "g":
            busy[i] = (0.0 if x["e"] == "x" else P["ind"]) + c * P["g"] * P["cyc"]
        elif k == "s":
            busy[i] = P["ind"] + c * P["sc"] * P["cyc"]
        elif k == "pe":
            busy[i] = c * P["pe"]
        elif k == "dma":
            busy[i], lat[i] = 60.0, P["dlat"] + P["drow"] + c / P["dbw"]
        else:
            busy[i], lat[i] = P["issue"], P["rlat"] + P["rrow"] + c / P["rbw"]
    free, pipe, done, bfree = {}, [0.0], [None] * n, {}
    suc = [[] for i in range(n)]
    for i, x in enumerate(nodes):
        for p in x["pre"]:
            suc[p].append(i)
    prio, since = [0.0] * n, {}
    turn = [({0: cfg["first"], S: cfg["last"]}.get(ph, "") + " " + cfg["turn"]).split()[::-1] for ph in range(S + 1)]
    turn = [{x.replace("send_", "send "): j for j, x in enumerate(names)} for names in turn]
    for i in range(n - 1, -1, -1):
        x = nodes[i]
        if x["tag"] in turn[x["ph"]]:
            prio[i] = 1e4 * (turn[x["ph"]][x["tag"]] - 1000 * x["ph"])
        else:
            prio[i] = busy[i] + lat[i] + max([prio[j] for j in suc[i]] + [-1e7 * S])

    def est(i, e):
        x = nodes[i]
        if i not in since:
            since[i] = max([done[p] + (0.0 if e == "t" and nodes[p]["e"] == "t" else P["wake"]) for p in x["pre"]] + [0.0])
        t0 = max(since[i], free.get(e, 0.0))
        for b in x["B"]:
            for e2, t2 in bfree.get(b, {}).items():
                if e2 != e:
                    t0 = max(t0, t2 + P["wake"])
        return t0

    def place(i, e, t0):
        x = nodes[i]
        x["e"] = e
        free[e] = t0 + busy[i]
        k = x["c"][0]
        if k == "dma":
            pipe[0] = done[i] = max(pipe[0], t0 + busy[i] + P["dlat"]) + lat[i] - P["dlat"]
        elif k == "send":
            pipe[0] = max(pipe[0], t0 + busy[i]) + lat[i] - P["rlat"]
            done[i] = pipe[0] + P["rlat"]
        else:
            done[i] = t0 + busy[i]
        for b in x["B"]:
            bfree.setdefault(b, {})[e] = done[i]

    hold = [cfg["hold"].get(x["tag"]) if x["ph"] < S else cfg["haste"] * (x["tag"] in cfg["last"].split()) for x in nodes]
    left = [len(x["pre"]) for x in nodes]
    ready, order = [i for i in range(n) if left[i] == 0], []
    while ready:
        es = [(est(i, e), e, i) for i in ready for e in (nodes[i]["e"] if nodes[i]["e"] != "x" else "av" if cfg["run"].get(nodes[i]["tag"] + "v", 1) else "a")]
        t0, e0 = min(es)[:2]
        mine = [(prio[i] - (1e4 * cfg["yield"] if e == "v" and nodes[i]["e"] == "x" else 0.0), -i, t, i) for t, e, i in es if e == e0]
        now = sorted([m for m in mine if m[2] <= t0], reverse=True)
        soon = [(m[2] + hold[m[3]], m) for m in mine if m > now[0] and hold[m[3]]]
        room, first = min(soon) if soon else (1e18, None)
        t1, i1 = ([m for m in now if t0 + busy[m[3]] + (P["ind"] if nodes[m[3]]["e"] == "x" else 0.0) <= room] + [first])[0][2:]
        x, run = nodes[i1], [i1]
        if x["span"]:
            near = sorted(i for t, e, i in es if e == e0 and t <= t1 and nodes[i]["tag"] == x["tag"] and nodes[i]["ph"] == x["ph"])
            kind = "m" if x["e"] == "v" else e0
            most = max(1, min(cfg["run"].get(x["tag"] + kind, cfg["run"][kind]), int((room - t1 - (P["ind"] if kind != "m" else 0.0)) / busy[i1])))
            if kind == "v":
                near = near[::-1]
            run = near[:1]
            for i in near[1:min(most, cfg["tile"]) if kind == "m" else most]:
                if abs(i - run[-1]) != 1:
                    break
                run.append(i)
            run.sort()
            i1, x = run[0], nodes[run[0]]
            busy[i1] = sum(busy[i] for i in run) + (P["ind"] if kind != "m" else 0.0)
            x["span"] = (x["span"][0], nodes[run[-1]]["span"][1])
            x["R"], x["W"] = sum([nodes[i]["R"] for i in run], []), sum([nodes[i]["W"] for i in run], [])
        place(i1, e0, t1)
        order.append(i1)
        for i in run:
            done[i] = done[i1]
            ready.remove(i)
            for j in suc[i]:
                left[j] -= 1
                if left[j] == 0:
                    ready.append(j)

    head = {}
    for i in order:
        for j in range(nodes[i]["span"][1] - nodes[i]["span"][0] if nodes[i]["span"] else 1):
            head[i + j] = i
    pre, suc = {i: set() for i in order}, {i: set() for i in order}
    for j, x in enumerate(nodes):
        for p in x["pre"]:
            pre[head[j]].add(head[p])
            suc[head[p]].add(head[j])
    full = {i: busy[i] + lat[i] for i in order}

    def gap(taken, a, d):
        for s, f in taken:
            if f > a + 1e-6:
                if s >= a + d - 1e-6:
                    break
                a = f
        return a

    def sweep(order, before, back):
        taken, banks, st = {}, {}, {}
        for i in order:
            x = nodes[i]
            e, k = x["e"], x["c"][0]
            t = max([st[p] + full[p] + (0.0 if e == "t" and nodes[p]["e"] == "t" else P["wake"]) for p in before[i]] + [0.0])
            uses = [(e, lat[i] if back else 0.0, busy[i])]
            if k in ("dma", "send"):
                ahead, behind = (P["dlat"], 0.0) if k == "dma" else (0.0, P["rlat"])
                uses.append(("pipe", behind if back else busy[i] + ahead, lat[i] - ahead - behind))
            t1 = -1.0
            while t > t1 + 1e-6:
                t1 = t
                for r, off, d in uses:
                    t = gap(taken.setdefault(r, []), t + off, d) - off
                for b in x["B"]:
                    for s, f, e2 in banks.setdefault(b, []):
                        if e2 != e and t < f + P["wake"] and s < t + busy[i] + P["wake"]:
                            t = f + P["wake"]
            st[i] = t
            for r, off, d in uses:
                taken[r].append((t + off, t + off + d))
                taken[r].sort()
            for b in x["B"]:
                banks[b].append((t, t + busy[i], e))
        return st

    for back in (False, True) * cfg["rounds"]:
        st = sweep(order, suc if back else pre, back)
        order = sorted(order, key=lambda i: (-st[i] - full[i], i if back else -i))
    if cfg["rounds"]:
        st = sweep(order, pre, False)
        order = sorted(order, key=lambda i: (st[i], i))
    return [(i, {k: nodes[i][k] for k in ("e", "span", "R", "W")}) for i in order]


def rank_program(g, core, T, topo):
    rank = T.rank_of(core)
    if rank is None:
        return
    nxt = T.cores[(rank + 1) % len(T.cores)]
    prv = T.cores[(rank - 1) % len(T.cores)]
    assert topo.may_write(core, nxt)
    rid, pid = topo.addr(nxt)[0], topo.addr(nxt)[1]
    mask = topo.mask(core, nxt)
    n_in = len(topo.engines(prv, core))
    n_out = len(topo.engines(core, nxt))
    v, a, t = g.vector, g.scalar, g.tensor
    Q = {"v": v, "a": a, "t": t, "g": g, "s": g.sync}
    cnt = {"v": 0, "a": 0, "t": 0, "g": 0, "d": 0, "sent": 0, "ph": 0, "F": 0}
    clock = {e: {} for e in Q}
    wr, rd, bank = {}, {}, {}
    nodes, lw, lr, lb = [], {}, {}, {}

    def node(e, tag, c, fn, R, W, B, span=None):
        i = len(nodes)
        pre = set(lw[r] for r in R if r in lw)
        for w in W:
            pre |= set(lr.get(w, []))
            if w in lw:
                pre.add(lw[w])
        if e == "t":
            for b in B:
                if b in lb:
                    pre.add(lb[b])
                lb[b] = i
        for r in R:
            lr.setdefault(r, []).append(i)
        for w in W:
            lw[w] = i
            lr[w] = []
        nodes.append(dict(e=e, tag=tag, c=c, fn=fn, R=list(R), W=list(W), B=list(B), pre=sorted(pre), span=span, ph=cnt["ph"]))

    def op(e, tag, fn, R=(), W=(), B=(), c=64, k="n"):
        node(e, tag, (k, c), fn, R, W, B)

    def dma(e, out, in_, nb, R=(), W=()):
        node(e, "dma_%s" % out.name, ("dma", nb), lambda: Q[e].dma_start(out, in_), R, W, ())

    def send(out, in_, sem, nb, R, lands):
        wr[lands] = (sem, sem, n_in, {})
        node("g", "send " + sem[:1], ("send", nb), lambda: g.remote_dma(out, in_, T.sem[sem], T.sem.sent, pid, rid, mask), R, [lands], ())

    def need(e, ev):
        sem, val, ck = ev[1], ev[2], ev[3]
        if clock[e].get(sem, 0) >= val:
            return
        Q[e].wait_ge(T.sem[sem], val)
        clock[e][sem] = val
        for k in ck:
            if clock[e].get(k, 0) < ck[k]:
                clock[e][k] = ck[k]

    def waits(e, me, R, W, B):
        evs = [wr[r] for r in R if r in wr]
        for w in W:
            evs += rd.get(w, []) + ([wr[w]] if w in wr else [])
        for b in B:
            evs += [x for k, x in bank.get(b, {}).items() if k != me]
        evs.sort(key=lambda x: -x[2])
        for ev in evs:
            if not (me == "t" and ev[0] == "t"):
                need(e, ev)

    def note(ev, R, W, B):
        for r in R:
            rd.setdefault(r, []).append(ev)
        for w in W:
            wr[w] = ev
            rd[w] = []
        for b in B:
            bank.setdefault(b, {})[ev[0]] = ev

    def emit(x):
        e, k = x["e"], x["c"][0]
        TAG[0] = x["tag"]
        if k == "send":
            waits("g", "rem", x["R"], (), ())
            x["fn"]()
            cnt["sent"] += n_out
        elif k == "dma":
            sem = "d%d" % cnt["d"]
            cnt["d"] += 1
            waits(e, sem, x["R"], x["W"], ())
            x["fn"]().then_inc(T.sem[sem], 16)
            note((sem, sem, 16, dict(clock[e])), x["R"], x["W"], ())
        else:
            waits(e, e, x["R"], x["W"], x["B"])
            cnt[e] += 1
            (x["fn"](e, *x["span"]) if x["span"] else x["fn"]()).then_inc(T.sem[e], 1)
            note((e, e, cnt[e], dict(clock[e])), x["R"], x["W"], x["B"])

    def copy(tag, out, in_, R, W, B=(), c=64, k="n", e="v"):
        if e == "v":
            op("v", tag, lambda: v.tensor_copy(out, in_), R, W, B, c, k)
        else:
            op("a", tag, lambda: a.activation(out, in_, F.Copy), R, W, B, c, k)

    def ts(tag, out, in0, s1, s2, o0, o1, R, W, B=(), c=64, k="n"):
        if o1 is None:
            op("v", tag, lambda: v.tensor_scalar(out, in0, s1, None, o0), R, W, B, c, k)
        else:
            op("v", tag, lambda: v.tensor_scalar(out, in0, s1, s2, o0, o1), R, W, B, c, k)

    def plus(tag, out, in0, x, R, W, B=(), c=64):
        ts(tag, out, in0, x, None, A.add, None, R, W, B, c)

    def tt(tag, out, in0, in1, o, R, W, B=(), c=64, k="n"):
        op("v", tag, lambda: v.tensor_tensor(out, in0, in1, o), R, W, B, c, k)

    def scan(tag, out, d0, d1, init, o0, o1, R, W, B=(), c=128):
        op("v", tag, lambda: v.tensor_tensor_scan(out, d0, d1, init, o0, o1), R, W, B, c)

    def act(tag, out, in_, f, R, W, B=(), c=256, **kw):
        op("a", tag, lambda: a.activation(out, in_, f, **kw), R, W, B, c)

    def affine(tag, out, in_, scale, bias, R, W, B=(), c=256):
        if CFG["eng"].get(tag, "a") == "a":
            act(tag, out, in_, F.Identity, R, W, B, c, scale=scale, bias=bias)
        else:
            ts(tag, out, in_, scale, bias, A.mult, A.add, R, W, B, c)

    def iota(out, pat, base, W, c, cm=0, **kw):
        op("g", "iota", lambda: g.iota(out, pat, base, cm, **kw), (), W, (), 156 + 2 * c)

    def mm(tag, out, res, bk, l, r, R, start, stop, c):
        op("t", tag, lambda: t.matmul(out, l, r, start, stop), R, [res], [bk], c, "pe")

    def blocks(name, b0, b1):
        return [(name, b) for b in range(b0, b1)]

    def col(i):
        return T.col[:, i:i + 1]

    IS = {"I": 1.0, "nI": -1.0, "n13": -8192.0, "p13": 8192.0, "p7": 128.0, "p6": 64.0, "p12": 4096.0, "n12": -4096.0}
    for s in range(S):
        IS["c%d" % s] = (s - 97.0) / 2

    def Id(name):
        j = 128 * list(IS).index(name)
        return T.Is[:, j:j + 128]

    def add(tag, out, res, bk, name, rhs, R, start=False, stop=True, c=256):
        mm(tag, out, res, bk, Id(name), rhs, R + [name], start, stop, c)

    def chunks(name):
        return list(enumerate(zip(CFG[name], CFG[name][1:])))

    def chunk_of(name, b):
        return [k for k, (c0, c1) in chunks(name) if c0 <= 8 * b < c1][0]

    Xw, Pw, K1, K2 = T.X[:, 0:XW], T.PW[:, 0:PWW], T.b0[:, 0:256], T.b1[:, 256:512]
    pq, pa, pb = T.b6[:, 0:256], T.b7[:, 0:256], T.b7[:, 256:512]
    C_P, C_R, C_G, C_LT2, C_DX, C_DP, C_E, C_R8, C_T = range(9)
    XR, PR = ["Xa", "Xb", "Xc"], ["PW", "PWa", "PWb"]
    HF = [("hf", k) for k, c in chunks("y1")] + ["hf1"]
    LAST = ("Ho", len(HF) - 2)
    CM0 = -37888.0 - 80.0 * 131072

    def OF(k, c0=0, c1=256):
        return T.OO[:, k * OW + c0:k * OW + c1]

    def Nof(buf, k, c0=0, c1=256):
        return buf[:, k * 256 + c0:k * 256 + c1]

    def Tof(buf, k, c0=0, c1=256):
        return buf[:, k * ZT + 128 + c0:k * ZT + 128 + c1]

    dma("s", T.pxi[:], T.px[:], 131072, W=["pxi"])
    dma("a", T.oli[:], T.ol[:], 131072, W=["oli"])
    dma("s", T.tli[:], T.tl[:], 131072, W=["tli"])
    dma("a", T.nli[:], T.nl[:], 131072, W=["nli"])
    dma("s", T.ZTo[:, 0:128], T.z[:], 32768, W=[("z", 0)])
    dma("a", T.thi[0:8, :], T.th[:], 128, W=["thi"])
    xs = CFG["xs"]
    dma("s", T.X[:, 0:xs], T.x[:, 0:xs], 256 * xs, W=["Xa"])
    op("v", "PW", lambda: v.memset(T.PW[:], 0.0), (), ["PW"], (), 2072)
    plus("px", T.phi[:], T.pxi[:], -H, ["pxi"], ["phi"], c=256)
    plus("px", T.pxf[:], T.pxi[:], -H, ["pxi"], ["pxf"], c=256)
    tt("px", T.plo[:], T.pxf[:], T.phi[:], A.subtract, ["pxf", "phi"], ["plo"], c=512)
    dma("s", T.PW[0:128:16, PO:PO + 4096], T.phi[:], 65536, ["phi", "PW"], ["PWa"])
    dma("s", T.PW[1:128:16, PO:PO + 4096], T.plo[:], 65536, ["plo", "PW"], ["PWb"])
    dma("s", T.X[:, xs:4096], T.x[:, xs:4096], 256 * (4096 - xs), ["plo", "PW"], ["Xb"])
    plus("in", T.O16[:, 0:256], T.oli[:], float(PO), ["oli"], [("O16", 0)], c=256)
    plus("in", OF(0), T.oli[:], float(PO), ["oli"], [("OO", 0)], c=256)
    copy("in", Tof(T.ZTo, 0), T.tli[:], ["tli"], [("T", 0)], c=256)
    plus("in", Nof(T.No, 0), T.nli[:], -H, ["nli"], [("N", 0)], c=256)

    fl = dict(allow_small_or_imprecise_dtypes=True)
    iota(T.ip[:], [[0, 8]], 0, ["ip"], 8, 1)
    iota(T.io1[:], [[1, 144]], -15, ["io1"], 144, **fl)
    iota(T.io2[:], [[16, 8], [0, 16]], 0, ["io2"], 128, **fl)
    iota(T.io3[:], [[0, 8], [1, 16]], 0, ["io3"], 128, **fl)
    iota(T.c62[:], [[2, 8]], 496, ["c62"], 8, **fl)
    iota(T.duP[:], [[0, 16], [1, 8]], 0, ["duP"], 128, -1, **fl)
    iota(T.duX[:], [[1, 8], [0, 16]], 0, ["duX"], 128, -1, **fl)
    iota(T.colc[:], [[1, 256]], 0, ["colc"], 256, **fl)
    iota(T.e1[:], [[1, 8], [8, 32]], 0, ["e1"], 256, **fl)
    for k in range(4):
        iota(OF(k, 256, OW), [[0, 8]], 6000, [("OF1", k)], 8, **fl)
    iota(T.X[:, 4096:XW], [[0, 16]], 0, ["Xc"], 16, **fl)
    iota(T.d0x[:], [[0, 256]], -(1 << 23), ["d0x"], 256, **fl)
    iota(T.d0n[:], [[0, 256]], 16, ["d0n"], 256, **fl)
    iota(T.hf[:, 256:264], [[0, 8]], 0, ["hf1"], 8, **fl)
    iota(T.ones[:], [[0, 256]], 1, ["ones"], 256, **fl)
    iota(T.thf[:], [[0, 4]], 0, ["thf"], 4, **fl)
    iota(T.acol[:, 4:5], [[0, 1]], int(CM0), ["ac1"], 1, **fl)
    p0 = T.ip[:, 0:1]
    ts("c", T.ib[:, 0:1], p0, 15, None, A.bitwise_and, None, ["ip"], ["ib0"])
    ts("c", T.ib[:, 1:2], p0, 7, None, A.bitwise_and, None, ["ip"], ["ib1"])
    ts("c", T.ib[:, 2:3], p0, 3, None, A.arith_shift_right, None, ["ip"], ["ib2"])
    copy("c", col(C_P), p0, ["ip"], ["cP"])
    copy("c", col(C_R), T.ib[:, 0:1], ["ib0"], ["cR"])
    copy("c", col(C_E), T.ib[:, 2:3], ["ib2"], ["cE"])
    copy("c", col(C_R8), T.ib[:, 1:2], ["ib1"], ["cR8"])
    tt("c", col(C_G), p0, T.ib[:, 0:1], A.subtract, ["ip", "ib0"], ["cG"])
    ts("c", col(C_LT2), T.ib[:, 0:1], 2.0, None, A.is_lt, None, ["ib0"], ["cLT2"])
    ts("c", T.LB[:], T.io1[:, 0:16], 0.0, col(C_R8), A.mult, A.add, ["io1", "cR8"], ["LB"])
    ts("c", T.E1f[:], T.io1[:], col(C_G), None, A.is_equal, None, ["io1", "cG"], ["E1f"], c=144)
    ts("c", T.If[:], T.io1[:, 15:143], col(C_P), None, A.is_equal, None, ["io1", "cP"], ["If"], c=128)
    ts("c", T.BD[:], T.io2[:], col(C_G), None, A.is_equal, None, ["io2", "cG"], ["BD"], c=128)
    ts("c", T.DM[:], T.io3[:], col(C_R), None, A.is_equal, None, ["io3", "cR"], ["DM"], c=128)
    ts("c", T.LM[:], T.io3[:], col(C_R), 8192.0, A.is_ge, A.mult, ["io3", "cR"], ["LM"], c=128)
    tt("c", T.A01[:], T.E1f[:, 15:143], T.E1f[:, 14:142], A.subtract, ["E1f"], ["A01"], c=256)
    copy("c", T.I16[:, 0:128], T.If[:], ["If"], ["I16"], c=128)
    ts("c", T.I16[:, 128:256], T.If[:], -512.0, None, A.mult, None, ["If"], ["J16"], c=128)
    ts("c", T.Rep[0:8, :], T.duP[0:8, :], 0.0, None, A.is_equal, None, ["duP"], ["Rep"], c=128)
    if CFG["eng"]["ref"] == "a":
        for h in range(2):
            copy("c", T.Repb[0:8, 128 * h:128 * h + 128], T.Rep[0:8, :], ["Rep"], [("Repb", h)])
    for h in range(2):
        copy("c", T.So[:, 256 * h:256 * h + 256], T.ones[:], ["ones"], ["So"], c=128)
    act("c", T.pu[:, 384:512], T.DM[:], F.Copy, ["DM"], ["DMp"], ["pu"], c=128)
    plus("c", T.thf[0:8, :], T.thi[0:8, :], -H, ["thi"], ["thf"])
    for s in range(S):
        ts("c", T.KL[0:32, 128 * s:128 * s + 128], T.duX[0:32, :], 0.0, T.thf[0:32, s:s + 1], A.is_equal, A.mult, ["duX", "thf"], [("KL", s)], c=128)
    for h in range(2):
        copy("c", T.KL[32:33, 256 * h:256 * h + 256], T.ones[32:33, :], ["ones"], [("KL1", h)], c=128)
    ts("c", T.KR[0:32, :], T.ones[0:32, :], 512.0, None, A.mult, None, ["ones"], ["KR"], c=128)
    copy("c", T.KR[32:33, :], T.e1[32:33, :], ["e1"], ["KR1"], c=256)
    act("c", col(C_T), col(C_R8), F.Identity, ["cR8", "cE"], ["cT"], c=64, scale=32.0, bias=col(C_E))
    for k, (c0, c1) in chunks("y3"):
        act("c", col(C_T + 1 + k), col(C_T), F.Identity, ["cT"], [("cT", k)], c=64, bias=float(c0 // 8))
        ts("c", T.Pm[:, 256 * k:256 * k + 256], T.colc[:], col(C_T + 1 + k), -512.0, A.is_equal, A.mult, ["colc", ("cT", k)], [("Pm", k)], c=128)
    copy("c", T.BD16[:], T.BD[:], ["BD"], ["BD16"], c=128)
    for j, x in enumerate((1.0, -1.0, 2.0, col(C_LT2))):
        act("c", T.Eg[:, 8 * j:8 * j + 8], T.BD[:, 0:128:16], F.Identity, ["BD", "cLT2"], [("Eg", j)], c=64, scale=x)
        if j:
            act("c", T.Es[:, 144 * j:144 * j + 144], T.E1f[:], F.Identity, ["E1f", "cLT2"], [("Es", j)], c=144, scale=x)
    for name in IS:
        act("c", Id(name), T.If[:], F.Identity, ["If"], [name], c=128, scale=IS[name])
    act("c", col(C_DX), col(C_R), F.Identity, ["cR"], ["cDX"], c=64, bias=4096.0)
    act("c", col(C_DP), col(C_R), F.Identity, ["cR"], ["cDP"], c=64, bias=4096.0 + PO)
    act("c", T.sg1[:], T.io3[:], F.Sign, ["io3"], ["sg1"], c=128, scale=-1.0, bias=15.0)
    act("c", T.sg2[:], T.io3[:], F.Sign, ["io3"], ["sg2"], c=128)
    act("c", T.sg2[:, 15:128:16], T.c62[:], F.Identity, ["c62"], ["sg2"], c=64, scale=0.0, bias=8192.0)
    act("c", T.d0x[:, 0:256:32], T.c62[:], F.Identity, ["c62"], ["d0x"], c=64, scale=0.0, bias=-256.0)
    act("c", T.d0n[:, 0:256:32], T.c62[:], F.Identity, ["c62"], ["d0n"], c=64, scale=0.0, bias=-BIG)

    def gather(name, win, R, lists, l0, c0=0, c1=256):
        def fn(e, b0, b1):
            out, in_ = T[name][:, 128 * b0:128 * b1], win.indirect(lists[:, l0 + 8 * b0:l0 + 8 * b1])
            return v.tensor_copy(out, in_) if e == "v" else a.activation(out, in_, F.Copy)
        for b in range(c0 // 8, c1 // 8):
            node("x", "%s_%d" % (name, chunk_of(name, b)), ("g", 128), fn, R(b), [(name, b)], (), (b, b + 1))

    def vmax(m, y, bk, c0=0, c1=256):
        def fn(e, b0, b1):
            return v.tensor_tensor(T[m][:, 128 * b0:128 * b1], T[y][:, 128 * b0:128 * b1], T[bk][:, 0:128 * (b1 - b0)], A.max)
        for b in range(c0 // 8, c1 // 8):
            node("v", "%s_%d" % (m, chunk_of(y, b)), ("n", 128), fn, [(y, b), bk], [(m, b)], [bk], (b, b + 1))

    def tile(tag, bk, z, zR):
        def fn():
            for j in range(CFG["tile"]):
                last = t.matmul(T[bk][:, 128 * j:128 * j + 128], Id("I"), z, True, True)
            return last
        op("t", tag, fn, ["I"] + zR, [bk], [bk], 128 * CFG["tile"], "pe")

    def lane_sums(o):
        def fn():
            for r in range(16):
                last = t.matmul(T.b2[0:8, 384 + r:512:16], T.ZTo[:, o * ZT + r:o * ZT + 128:16], T.Eg[:, 0:8], True, True)
            return last
        op("t", "szu", fn, [("Eg", 0), ("z", o)], ["psu"], ["b2"], 256, "pe")
        ts("szu", T.So[0:8, 128 * o:128 * o + 128], T.b2[0:8, 384:512], -1.0, H, A.mult, A.add, ["psu", "So"], [("So", o)], ["b2"], c=128)

    def flat(M):
        return M in CFG["flat"]

    def form(buf, k, M):
        return buf[:, 128 * k:128 * k + M] if flat(M) else buf[0:M, 128 * k:128 * k + 128]

    def put(tag, out, res, bk, M, x, ident, R, start, stop):
        if flat(M):
            mm(tag, out, res, bk, ident, x, R, start, stop, max(64, M))
        else:
            mm(tag, out, res, bk, x, ident, R, start, stop, 128)

    def fold(tag, bk, j, name, c0, c1, is_flat, stop):
        def fn():
            for r in range(16):
                x = T[name][:, 16 * c0 + r:16 * c1:16]
                if is_flat:
                    last = t.matmul(T[bk][:, 0:c1 - c0], T.Es[:, 144 * j + 15 - r:144 * j + 143 - r], x, False, stop and r == 15)
                else:
                    last = t.matmul(T[bk][0:c1 - c0, r:128:16], x, T.Eg[:, 8 * j:8 * j + 8], False, stop and r == 15)
            return last
        op("t", tag, fn, [("Es" if is_flat else "Eg", j)] + blocks(name, c0 // 8, c1 // 8), [("F", bk)], [bk], 16 * (max(64, c1 - c0) if is_flat else min(64, c1 - c0)), "pe")

    def distances(tags, k, c0, c1, y, m, sums, o, out):
        bk, M = "b%d" % (2 + cnt["F"] % 2), c1 - c0
        cnt["F"] += 1
        mm(tags[0], T[bk][0:M, 0:128], ("F", bk), bk, T.Rep[0:8, 0:M], T[sums][0:8, 128 * o:128 * o + 128], ["Rep", (sums, o)], True, False, 128)
        fold(tags[1] + str(k), bk, 1, y, c0, c1, False, False)
        fold(tags[2] + str(k), bk, 2, m, c0, c1, False, True)
        plus(tags[3] + str(k), T[out][0:M, 128 * k:128 * k + 128], T[bk][0:M, 0:128], -2 * H, [("F", bk)], [(out, k)], [bk], c=128)

    def turn(tag, out, res, bk, src, k, M, rhs, R, start, stop, c):
        mm(tag, out, res, bk, T[src][0:M, 128 * k:128 * k + 128], rhs, [(src, k)] + R, start, stop, max(64, c))

    def chooser(o, buf, NR):
        c = 8192 * (o + 0.5)
        if o == 0:
            act("s3", T.s3[:], Tof(T.ZTo, 0), F.Relu, [("T", 0)], ["s3"], scale=-8192.0, bias=c)
        else:
            act("s3", T.s3[:], pq, F.Relu, ["pQ"], ["s3"], ["b6"], scale=-8192.0, bias=c - 8192.0 * 64)
        for k, (c0, c1) in chunks("gp"):
            M = c1 - c0
            out, res = form(T.b7, k, M), "pa" if k < 2 else "pb"
            put("qn", out, res, "b7", M, Nof(buf, max(o - 1, 0), c0, c1), T.I16[:, 0:128], NR + ["I16"], True, False)
            if o == 0:
                put("q2", out, res, "b7", M, Tof(T.ZTo, 0, c0, c1), Id("n13"), [("T", 0), "n13"], False, False)
            else:
                put("q2", out, res, "b7", M, T.Tr[:, c0:c1], Id("p13"), ["Tr", "p13"], False, False)
            put("q2", out, res, "b7", M, T.s3[:, c0:c1], Id("nI"), ["s3", "nI"], False, True)
            affine("Qs", form(T.Qs, k, M), out, 1.0, c - (8192.0 * 99 if o else 0.0), [res], [("Qs", k)], ["b7"], c=M if flat(M) else 128)

    def part1(o):
        act("cm", T.b6[:, 256:512], OF(o), F.Identity, [("OO", o), "ac1"], ["cm"], ["b6"], bias=T.acol[:, 4:5], scale=3232.0)
        for x in CFG["seq"].split():
            (roads if x[0] == "p" else hashes)(o, int(x[1]))

    def roads(o, k):
        c0, c1 = CFG["gp"][k:k + 2]
        gather("gp", Pw, lambda b: PR + [("O16", o)], T.O16, 256 * o, c0, c1)
        bk, M = "b%d" % (2 + cnt["F"] % 2), c1 - c0
        cnt["F"] += 1
        put("po", form(T[bk], 0, M), ("F", bk), bk, M, T.s3[:, c0:c1], Id("nI"), ["s3", "nI"], True, False)
        fold("po%d" % k, bk, 3, "gp", c0, c1, flat(M), True)
        if flat(M):
            tt("R%d" % k, T.tf[:, c0:c1], T[bk][:, 0:M], form(T.Qs, k, M), A.max, [("F", bk), ("Qs", k)], blocks("tf", c0 // 8, c1 // 8), [bk], c=M)
            plus("R%d" % k, T.R16[:, c0:c1], T.tf[:, c0:c1], H, blocks("tf", c0 // 8, c1 // 8), [("R16", k)], c=M)
        else:
            tt("R%d" % k, T.Rf[0:M, 128 * k:128 * k + 128], T[bk][0:M, 0:128], T.Qs[0:M, 128 * k:128 * k + 128], A.max, [("F", bk), ("Qs", k)], [("Rf", k)], [bk], c=128)
            turn("R%d" % k, T.b1[:, c0:c1], ("pR", k), "b1", "Rf", k, M, T.I16[0:M, 0:M], ["I16"], True, True, M)
            plus("R%d" % k, T.R16[:, c0:c1], T.b1[:, c0:c1], H, [("pR", k)], [("R16", k)], ["b1"], c=M)

    def hashes(o, k):
        c0, c1 = CFG["y1"][k:k + 2]
        gather("y1", Xw, lambda b: XR + [("R16", chunk_of("gp", b))], T.R16, 0, c0, c1)
        vmax("m1", "y1", "pt", c0, c1)
        M, tf = c1 - c0, blocks("tf", c0 // 8, c1 // 8)
        if flat(M):
            bk = "b%d" % (2 + cnt["F"] % 2)
            cnt["F"] += 1
            pu, res = T[bk][:, 0:M], ("F", bk)
            mm("us", pu, res, bk, T.So[0:8, 128 * o:128 * o + 128], T.Rep[0:8, 0:M], ["Rep", ("So", o)], True, False, 64)
            add("us", pu, res, bk, "n12", T.ones[:, 0:M], ["ones"], False, False, 64)
            fold("uy%d" % k, bk, 1, "y1", c0, c1, True, False)
            fold("um%d" % k, bk, 2, "m1", c0, c1, True, True)
        else:
            bk, pu, res = "b0", T.b0[:, 256 + c0:256 + c1], ("pu", k)
            distances(("us", "uy", "um", "h"), k, c0, c1, "y1", "m1", "So", o, "uf")
            turn("h%d" % k, pu, res, bk, "uf", k, M, T.I16[0:M, 0:M], ["I16"], True, True, M)
        tt("h%d" % k, T.tf[:, c0:c1], pu, OF(o, c0, c1), A.mult, [res, ("OO", o)], tf, [bk], c=M)
        tt("h%d" % k, T.vi[:, c0:c1], T.tf[:, c0:c1], T.b6[:, 256 + c0:256 + c1], A.add, tf + ["cm"], [("vi", k)], ["b6"], c=M)
        ts("h%d" % k, T.hi[:, c0:c1], T.vi[:, c0:c1], 5, 4095, A.arith_shift_right, A.bitwise_and, [("vi", k)], [("hi", k)], c=M)
        copy("h%d" % k, Nof(T.Ho, o, c0, c1), T.hi[:, c0:c1], [("hi", k)], [("Ho", k)], c=M)
        send(Nof(T.Hi, o, c0, c1), Nof(T.Ho, o, c0, c1), "h%d" % (5 * o + k), 256 * M, [("Ho", k)], ("Hi", o, k))

    def send_state(o):
        z0, first = o * ZT, [] if o else ["Xb"]
        send(T.ZTi[:, z0:z0 + 128], T.ZTo[:, z0:z0 + 128], "z%d" % o, 32768, [("z", o)], ("Zi", o))
        send(T.Si[:, 128 * o:128 * o + 128], T.So[:, 128 * o:128 * o + 128], "s%d" % o, 32768, [("So", o), "So"] + first, ("Si", o))
        if o < S - 1:
            after = [("Hi", o - 1, LAST[1]) if o else LAST]
            send(OF(o + 1), OF(o), "o%d" % o, 131072, [("OO", o)] + after, ("OO", o + 1))
            send(Nof(T.O16, o + 1), Nof(T.O16, o), "l%d" % o, 65536, [("O16", o)] + after, ("O16", o + 1))
        send(Tof(T.ZTi, o), Tof(T.ZTo, o), "t%d" % o, 65536, [("T", o)] + first, ("Ti", o))
        send(Nof(T.Ni, o), Nof(T.No, o), "n%d" % o, 65536, [("N", o)] + first, ("Ni", o))

    def part3(s):
        z0 = s * ZT
        tile("zt3", "pu", T.ZTi[:, z0:z0 + 128], [("Zi", s)])
        gather("y3", Xw, lambda b: XR + [("Hi", s, chunk_of("y1", b))], T.Hi, 256 * s)
        vmax("m3", "y3", "pu")
        KL = [("KL", s), ("KL1", s // 2), "KR", "KR1"]
        mm("ks", K1, "K1", "b0", T.KL[0:33, 128 * s:128 * s + 128], T.KR[0:33, :], KL, True, False, 256)
        mm("ks", K2, "K2", "b1", T.KL[0:8, 128 * s:128 * s + 128], T.KR[0:8, :], KL, True, False, 256)
        for k, (c0, c1) in chunks("y1"):
            plus("hf", T.hf[:, c0:c1], Nof(T.Hi, s, c0, c1), -H, [("Hi", s, k)], [("hf", k)], c=c1 - c0)
        act("e", T.e1[:], Tof(T.ZTi, s), F.Abs, [("Ti", s)], ["e1"], bias=-(s + 99) / 2.0)
        act("e", T.e2[:], T.e1[:], F.Relu, ["e1"], ["e2"], scale=-float(1 << 22), bias=(98 - s) * float(1 << 21))
        add("q", pq, "pQ", "b6", "I", Tof(T.ZTi, s), [("Ti", s)], True, False)
        for k, (c0, c1) in chunks("y3"):
            M = c1 - c0
            distances(("ks", "ky", "km", "K"), k, c0, c1, "y3", "m3", "Si", s, "Kf")
            turn("K%d" % k, K1, "K1", "b0", "Kf", k, M, T.Pm[0:M, 256 * k:256 * k + 256], [("Pm", k)], False, c1 == 256, 256)
            turn("k2", T.b1[:, 256 + c0:256 + c1], "K2", "b1", "Kf", k, M, T.I16[0:M, 128:128 + M], ["J16"], False, False, M)
        add("ke", K2, "K2", "b1", "nI", T.e2[:], ["e2"])
        cnt["ph"] += 1
        scan("scM", T.scM[:], T.d0x[:], K1, -256.0, A.max, A.min, ["d0x", "K1"], ["scM"], ["b0"], c=256)
        scan("scN", T.scN[:], T.d0n[:], K1, 0.0, A.add, A.max, ["d0n", "K1"], ["scN"], ["b0"], c=256)
        ts("p", T.pi2[:], T.scM[:, 31:256:32], 511, None, A.bitwise_and, None, ["scM"], ["pi2"])
        copy("p", T.cj[:, 0:8], T.pi2[:], ["pi2"], ["cj"])
        tt("x", T.xi1[:], T.c62[:], T.scN[:, 31:256:32], A.subtract, ["c62", "scN"], ["xi1"])
        ts("x", T.xi2[:], T.xi1[:], 511, None, A.bitwise_and, None, ["xi1"], ["xi2"])
        copy("x", T.cj[:, 8:16], T.xi2[:], ["xi2"], ["cb"])
        for x, j, lst in (("Mkh", 0, "cj"), ("MkX", 1, "cb")):
            src = T.hf[:, 0:264].indirect(T.cj[:, 8 * j:8 * j + 8])
            if CFG["eng"][x] == "v" or s == S - 1:
                tt(x, T[x][:], src, T.DM[:], A.mult, HF + [lst, "DM"], [x], c=128, k="g")
            else:
                copy("g" + x, T.Gh[:, 128 * j:128 * j + 128], src, HF + [lst], [("Gh", j)], c=128, k="g", e="a")
                tt(x, T[x][:], T.Gh[:, 128 * j:128 * j + 128], T.pu[:, 384:512], A.mult, [("Gh", j), "DMp"], [x], ["pu"], c=128)

    def first_of_block(x, bk, shift, dummy, dR):
        Mk, key, eq, du, t8 = [T[y + x] for y in ("Mk", "key", "eq", "du", "t8")]
        ps, res = T[bk][:, 128:256], "row" + x
        add("lm" + x, ps, res, bk, "I", T.LM[:], ["LM"], True, False, 128)
        BD = "BD" if x == "P" else "BD16"
        mm("row" + x, ps, res, bk, T[BD][:], Mk[:], [BD, "Mk" + x], False, True, 512 if x == "P" else 128)
        scan("key" + x, key[:, ::-1], T.sg1[:, ::-1], Mk[:, ::-1], 0.0, A.mult, A.add, ["sg1", "Mk" + x], ["key" + x])
        tt("eq" + x, eq[:], ps, key[:], A.is_equal, [res, "key" + x], ["eq" + x], [bk], c=128)
        scan("du" + x, du[:], T.sg2[:], eq[:], 0.0, A.mult, A.add, ["sg2", "eq" + x], ["du" + x])
        tt("off" + x, t8[:], du[:, 15:128:16], key[:, 0:128:16], A.add, ["du" + x, "key" + x], ["t8" + x])
        ts("off" + x, T["off" + x][:, 0:16:2], t8[:], shift, dummy, A.add, A.min, ["t8" + x, dR], ["off" + x])

    def refuse(s):
        o, pv = (s + 1) % S, T.b2[:, 256:384]
        tt("MkP", T.MkP[:], OF(o, 0, OW).indirect(T.cj[:, 0:8]), T.DM[:], A.mult, [("OO", o), ("OF1", o), "cj", "DM"], ["MkP"], c=128, k="g")
        first_of_block("P", "b2", 0.0, col(C_DP), "cDP")
        act("val", T.Mkhb[:], T.Mkh[:], F.Copy, ["Mkh"], ["Mkhb"], c=128)
        mm("val", pv, "pv", "b2", T.E1f[:, 14:142], T.Mkh[:], ["E1f", "Mkh"], True, False, 512)
        mm("val", pv, "pv", "b2", T.A01[:], T.Mkhb[:], ["A01", "Mkhb"], False, True, 128)
        act("val", T.val[:], pv, F.Copy, ["pv"], ["val"], ["b2"], c=128)
        for c in range(7, -1, -1):
            copy("scatP", Pw.indirect(T.offP[:, 2 * c:2 * c + 1]), T.val[:, 16 * c:16 * c + 16], ["offP", "val"], PR, c=16, k="s")

    def learn(s):
        z1 = (s + 1) * ZT
        first_of_block("X", "b3", H, col(C_DX), "cDX")
        plus("hb", T.hb[:], T.keyX[:, 0:128:16], H, ["keyX"], ["hb"])
        zi = T.ZTi[:, s * ZT:s * ZT + 128]
        if CFG["eng"]["z%d" % (s == S - 1)] == "v":
            tt("zs", T.zs[:], Xw.indirect(T.hb[:, 0:8]), zi, A.add, XR + ["hb", ("Zi", s)], ["zs"], c=128, k="g")
            ts("zi", T.zi[:], T.zs[:], 0.5, -0.25, A.mult, A.add, ["zs"], ["zi"], c=128)
            copy("zn", T.ZTo[:, z1:z1 + 128], T.zi[:], ["zi"], [("z", s + 1)], c=128)
        else:
            ps = T.b3[:, 256:384]
            add("zp", ps, "pzs", "b3", "I", zi, [("Zi", s)], True, False, 128)
            copy("zs", T.gb[:], Xw.indirect(T.hb[:, 0:8]), XR + ["hb"], ["gb"], c=128, k="g", e="a")
            add("zp", ps, "pzs", "b3", "I", T.gb[:], ["gb"], c=128)
            act("zi", T.zs[:], ps, F.Identity, ["pzs"], ["zs"], ["b3"], c=128, scale=0.49999, bias=1.5 * BIG)
            act("zn", T.ZTo[:, z1:z1 + 128], T.zs[:], F.Identity, ["zs"], [("z", s + 1)], c=128, bias=-1.5 * BIG)
        for c in range(7, -1, -1):
            copy("scatX", Xw.indirect(T.offX[:, 2 * c:2 * c + 1]), T.ZTo[:, z1 + 16 * c:z1 + 16 * c + 16], ["offX", ("z", s + 1)], XR, c=16, k="s")

    def marks(s):
        act("sg", T.sg[:], K2, F.Sign, ["K2"], ["sg", "ac0"], ["b1"], c=280, bias=0.5, accum_out=T.acol[:, 0:1])
        if CFG["eng"]["ref"] == "v":
            tt("ref", T.ref[:], T.pi2[:, 0:8].indirect(T.LB[:, 0:16]), T.colc[:], A.is_equal, ["pi2", "LB", "colc"], ["ref"], c=256, k="g")
        else:
            pd = T.b0[:, 256:512]
            copy("rf", T.cjb[:], T.pi2[:], ["pi2"], ["cjb"])
            mm("rf", T.b1[0:8, 0:128], ("pR", 0), "b1", T.cjb[:], Id("I"), ["cjb", "I", ("pR", 1)], True, True, 128)
            act("rf", T.cjT[0:8, :], T.b1[0:8, 0:128], F.Copy, [("pR", 0)], ["cjT", ("pR", 1)], ["b1"], c=128)
            add("rf", pd, "pd", "b0", "nI", T.colc[:], ["colc"], True, False)
            mm("rf", pd, "pd", "b0", T.cjT[0:8, :], T.Repb[0:8, :], ["cjT", ("Repb", 0), ("Repb", 1)], False, True, 256)
            act("ref", T.e2[:], pd, F.Abs, ["pd"], ["e2"], ["b0"])
            act("ref", T.ref[:], T.e2[:], F.Relu, ["e2"], ["ref"], scale=-1.0, bias=1.0)
        add("q", pq, "pQ", "b6", "p6", T.sg[:], ["sg"], False, False)
        add("q", pq, "pQ", "b6", "p7", T.ref[:], ["ref"])
        act("Tr", T.Tr[:], pq, F.Relu, ["pQ"], ["Tr"], ["b6"], scale=-1.0, bias=35.0)

    def count():
        mm("A", T.b3[:, 384:385], "pA", "b3", T.BD[:], T.acol[:, 0:1], ["BD", "ac0"], True, True, 256)
        act("A", T.acol[:, 4:5], T.b3[:, 384:385], F.Identity, ["pA"], ["ac1"], ["b3"], c=64, scale=16.0, bias=65536.0 + CM0)

    def new_dates(s, out, res):
        add("T", pa, "pa", "b7", "nI", T.Tr[:], ["Tr"], True, False)
        add("T", pa, "pa", "b7", "c%d" % s, T.sg[:], ["sg"])
        affine("Tn", out, pa, 1.0, 99 - (97 - s) / 2.0, ["pa"], [res], ["b7"])

    def new_names(s, out, res):
        add("N", pb, "pb", "b7", "p12", T.sg[:], ["sg"], True)
        tt("t1", T.t1[:], pb, T.hf[:, 0:256], A.min, ["pb"] + HF, ["t1"], ["b7"], c=256)
        mm("N", pb, "pb", "b7", T.I16[:, 0:128], Nof(T.Ni, s), [("Ni", s), "I16"], True, False, 256)
        add("N", pb, "pb", "b7", "n12", T.ones[:], ["ones"], False, False)
        add("N", pb, "pb", "b7", "n12", T.sg[:], ["sg"])
        tt("Nn", out, pb, T.t1[:], A.max, ["pb", "t1"], [res], ["b7"], c=256)

    def new_z(o):
        tile("zt", "pt", T.ZTo[:, o * ZT:o * ZT + 128], [("z", o)])
        lane_sums(o)

    new_z(0)
    chooser(0, T.No, [("N", 0)])
    part1(0)
    send_state(0)
    for s in range(S):
        part3(s)
        if s < S - 1:
            refuse(s)
            learn(s)
            marks(s)
            count()
            new_names(s, Nof(T.No, s + 1), ("N", s + 1))
            chooser(s + 1, T.Ni, [("Ni", s)])
            new_z(s + 1)
            new_dates(s, Tof(T.ZTo, s + 1), ("T", s + 1))
            part1(s + 1)
            send_state(s + 1)
        else:
            learn(s)
            dma("s", T.yx[:], T.X[:, 0:4096], 1048576, XR, ["yx"])
            dma("s", T.yz[:], T.ZTo[:, S * ZT:S * ZT + 128], 32768, [("z", S)], ["yz"])
            refuse(s)
            marks(s)
            new_dates(s, T.oT[:], "oT")
            dma("s", T.yt[:], T.oT[:], 131072, ["oT"], ["yt"])
            new_names(s, T.e1[:], "e1")
            act("oN", T.oN[:], T.e1[:], F.Identity, ["e1"], ["oN"], bias=H)
            dma("a", T.yn[:], T.oN[:], 131072, ["oN"], ["yn"])
            for h, bk in enumerate(("pt", "pu")):
                def unfold(h=h, bk=bk):
                    for r in range(16):
                        c0 = PO + 2048 * h + 128 * r
                        last = t.matmul(T[bk][:, r:128:16], T.PW[:, c0:c0 + 128], T.Eg[:, 24:32], True, True)
                    return last
                op("t", "oP", unfold, [("Eg", 3)] + PR, [bk], [bk], 1024, "pe")
                copy("oP", T.Kf[:, 128 * h:128 * h + 128], T[bk][:, 0:128], [bk], [("Kf", h)], [bk], c=128)
                turn("oP", T[bk][:, 128:256], ("oq", h), bk, "Kf", h, 128, T.I16[:, 0:128], ["I16", bk], True, True, 128)
                act("oP", T.oP[:, 128 * h:128 * h + 128], T[bk][:, 128:256], F.Identity, [("oq", h)], [("oP", h)], [bk], c=128, bias=H)
                dma("as"[h], T.yp[:, 2048 * h:2048 * h + 2048], T.oP[:, 128 * h:128 * h + 128], 65536, [("oP", h)], [("yp", h)])

    if not PLAN:
        PLAN.extend(run_plan(nodes, EST, CFG))
    for i, x in PLAN:
        emit(dict(nodes[i], **x))
    TAG[0] = "end"
    for e in "vatg":
        g.sync.wait_ge(T.sem[e], cnt[e])
    for k in range(cnt["d"]):
        g.sync.wait_ge(T.sem["d%d" % k], 16)
    g.wait_ge(T.sem.sent, cnt["sent"])
